import numpy as np
import ml_dtypes


def mxq(x, axis, fmt="e4m3"):
    dtype, down = {"e4m3": (ml_dtypes.float8_e4m3fn, 7), "e5m2": (ml_dtypes.float8_e5m2, 14)}[fmt]
    v = np.moveaxis(np.asarray(x, np.float32).astype(ml_dtypes.bfloat16).astype(np.float64), axis, -1)
    blocks = v.reshape(v.shape[:-1] + (-1, 32))
    amax = np.abs(blocks).max(-1, keepdims=True)
    byte = np.maximum(np.where(amax > 0, np.frexp(amax)[1] - 1 + 127, 0) - down, 1)
    scale = np.exp2(byte - 127.0)
    codes = (blocks / scale).astype(np.float32).astype(dtype).astype(np.float64)
    return np.moveaxis((codes * scale).reshape(v.shape), -1, axis)


WIDE = False


def mx_kscale(k):
    if not WIDE:
        return np.ones(k)
    levels = np.array([10, -10, 5, -5, 0])
    if k % 512:
        return np.exp2(np.random.permutation(np.resize(levels, k // 32))).repeat(32)
    a = np.empty((k // 512, 16))
    for p in range(k // 512):
        a[p, :8] = np.random.permutation(np.resize(levels, 8))
        for g in range(8):
            far = levels[np.abs(levels - a[p, g]) >= 10]
            a[p, g + 8] = far[np.random.randint(len(far))]
    return np.exp2(a.ravel()).repeat(32)


def f64(x):
    return np.asarray(x).astype(np.float64)


def striped(idx):
    return np.tile(idx.reshape(-1, 16).T, (8, 1)).astype(np.uint16)


def unstriped(offs):
    return offs[:16].T.reshape(-1).astype(np.int64)


E2M1 = np.array([0.0, 0.5, 1.0, 1.5, 2.0, 3.0, 4.0, 6.0, -0.0, -0.5, -1.0, -1.5, -2.0, -3.0, -4.0, -6.0])


def pack_weight(w, fmt):
    k, n = w.shape
    w = f64(np.asarray(w, np.float32).astype(ml_dtypes.bfloat16)).reshape(k // 32, 32, n)
    amax = np.abs(w).max(1)
    if fmt == "e4m3":
        byte = np.frexp(amax)[1] - 1 + 127 - 7
    else:
        mant, ex = np.frexp(amax / 6.0)
        byte = np.where(mant > 0.5, ex, ex - 1) + 127
    byte = np.clip(np.where(amax > 0, byte, 1), 1, 254)
    scaled = (w * np.exp2(127.0 - byte)[:, None, :]).reshape(k, n).astype(np.float32)
    by_word = np.ascontiguousarray(scaled.reshape(k // 512, 128, 4, n).transpose(0, 1, 3, 2))
    if fmt == "e4m3":
        words = by_word.astype(ml_dtypes.float8_e4m3fn).view(np.uint8)
    else:
        c = by_word.astype(ml_dtypes.float4_e2m1fn).view(np.uint8) & 0xF
        words = (c[..., 0::2] | (c[..., 1::2] << 4)).reshape(k // 512, 128, 2 * n)
    return np.ascontiguousarray(words), np.ascontiguousarray(byte.astype(np.uint8).reshape(k // 512, 16, n))


def unpack_weight(words, scales, fmt):
    g, _, n = scales.shape
    words = np.ascontiguousarray(words).reshape(g, 128, n, -1)
    if fmt == "e4m3":
        vals = words.view(ml_dtypes.float8_e4m3fn).astype(np.float64)
    else:
        nib = np.empty((g, 128, n, 4), np.uint8)
        nib[..., 0::2] = words & 0xF
        nib[..., 1::2] = words >> 4
        vals = E2M1[nib]
    vals = vals * np.repeat(np.exp2(scales.astype(np.float64) - 127.0), 8, axis=1)[..., None]
    return vals.transpose(0, 1, 3, 2).reshape(g * 512, n)


def gelu(v):
    return 0.5 * v * (1.0 + np.tanh(np.sqrt(2.0 / np.pi) * (v + 0.044715 * v**3)))


K, T, S, T2, S2, N = 1024, 2048, 1024, 4096, 1024, 512

def setup_inputs():
    n = np.random.standard_normal
    s = mx_kscale(K)[:, None]
    u = mx_kscale(S)[:, None]
    tab_words, tab_scales = pack_weight(n((K, T)) * s, "e4m3")
    tab2_words, tab2_scales = pack_weight(n((K, T2)) / s / np.sqrt(K), "e4m3")
    wact_words, wact_scales = pack_weight(1.5 * n((S, N)) / np.sqrt(S) / u, "e2m1")
    return {
        "tab_words": tab_words, "tab_scales": tab_scales,
        "offs": striped(np.random.permutation(T)[:S]),
        "tab2_words": tab2_words, "tab2_scales": tab2_scales,
        "offs2": striped(np.random.permutation(T2)[:S2]),
        "sharp": np.exp(0.3 * n(S)).astype(np.float32),
        "trust": (np.exp(0.3 * n(S)) * u[:, 0]).astype(np.float32),
        "wact_words": wact_words, "wact_scales": wact_scales,
        "wgate": (1.5 * n((S, N)) / np.sqrt(S) / u).astype(np.float32),
    }

def reference(tab_words, tab_scales, offs, tab2_words, tab2_scales, offs2,
              sharp, trust, wact_words, wact_scales, wgate):
    v = unpack_weight(tab_words, tab_scales, "e4m3")[:, unstriped(offs)]
    v2 = unpack_weight(tab2_words, tab2_scales, "e4m3")[:, unstriped(offs2)]
    a = v.T @ v2
    h = np.tanh(f64(sharp)[:, None] * a) * f64(trust)[:, None]
    hq = mxq(h, 0, "e4m3")
    wact = unpack_weight(wact_words, wact_scales, "e2m1")
    y = wact.T @ hq
    c = mxq(f64(wgate), 0, "e4m3").T @ hq
    return y * (1.0 / (1.0 + np.exp(-c)))

@@ -1,0 +1,228 @@
+from contextlib import ExitStack
+
+import concourse.mybir as mybir
+
+K, T, S, T2, S2, N = 1024, 2048, 1024, 4096, 1024, 512
+FLOPS = 2 * K * S * S2 + 2 * 2 * S * N * S2
+
+F32 = mybir.dt.float32
+BF16 = mybir.dt.bfloat16
+I32 = mybir.dt.int32
+U32 = mybir.dt.uint32
+U16 = mybir.dt.uint16
+U8 = mybir.dt.uint8
+FP8X4 = mybir.dt.float8_e4m3fn_x4
+FP4X4 = mybir.dt.float4_e2m1fn_x4
+ACT = mybir.ActivationFunctionType
+ALU = mybir.AluOpType
+
+P = 128
+PACK = 4
+KP = P * PACK
+JW = 512
+HALF = JW // 2
+V_PLANE = (12, 8)
+V2_PLANE = (0, 4)
+
+
+def tile_list_hopfield_episode_actions_kernel(
+    tc, tab_words, tab_scales, offs, tab2_words, tab2_scales, offs2,
+    sharp, trust, wact_words, wact_scales, wgate, out,
+):
+    nc = tc.nc
+    with ExitStack() as ctx:
+        keep = ctx.enter_context(tc.tile_pool(name="keep", bufs=1))
+        work = ctx.enter_context(tc.tile_pool(name="work", bufs=2))
+        psum = ctx.enter_context(tc.psum_pool(name="psum", bufs=8))
+
+        idx = keep.tile([P, S // 16], U16, name="idx")
+        idx2 = keep.tile([P, S2 // 16], U16, name="idx2")
+        tab_w = [keep.tile([P, T], I32, name=f"tab_w{a}", align_bytes=64) for a in range(2)]
+        tab2_w = [keep.tile([P, T2], I32, name=f"tab2_w{a}", align_bytes=64) for a in range(2)]
+        tab_s = keep.tile([P, T // 4], I32, name="tab_s", align_bytes=64)
+        tab2_s = keep.tile([P, T2 // 4], I32, name="tab2_s", align_bytes=64)
+        wact_w = keep.tile([P, 2, 2 * N // 4], I32, name="wact_w", align_bytes=64)
+        wact_s = keep.tile([P, 2, N // 4], I32, name="wact_s", align_bytes=64)
+        sharp_sb = keep.tile([P, 2, PACK], F32, name="sharp_sb")
+        trust_sb = keep.tile([P, 2, PACK], F32, name="trust_sb")
+        wg_raw = [keep.tile([P, PACK, N], F32, name=f"wg_raw{g}") for g in range(2)]
+        warm = keep.tile([P, 8], F32, name="warm")
+        warm_out = keep.tile([P, 8], F32, name="warm_out")
+
+        nc.vector.memset(tab_s[:], 0)
+        nc.gpsimd.memset(tab2_s[:], 0)
+        nc.vector.memset(warm[:], 0.0)
+        nc.vector.memset(wact_s[:], 0)
+        nc.scalar.activation(warm_out[:], warm[:], ACT.Sigmoid)
+
+        def load_words(dst, words, a):
+            nc.sync.dma_start(dst[:], words[a].rearrange("p t i -> p (t i)").bitcast(I32))
+
+        def load_scale_rows(dst, scales, planes, a, r):
+            src = scales[a].bitcast(I32).rearrange("(q r) t -> r q t", r=4)[r]
+            nc.sync.dma_start(dst[planes[a] + r : P : 32, :], src)
+
+        rows = [(a, r) for a in range(2) for r in range(4)]
+        nc.sync.dma_start(idx[:], offs)
+        load_words(tab_w[0], tab_words, 0)
+        nc.sync.dma_start(idx2[:], offs2)
+        nc.sync.dma_start(sharp_sb[:], sharp.rearrange("(g p t) -> p g t", g=2, t=PACK))
+        for a, r in rows[:4]:
+            load_scale_rows(tab_s, tab_scales, V_PLANE, a, r)
+        load_words(tab_w[1], tab_words, 1)
+        for a, r in rows[4:]:
+            load_scale_rows(tab_s, tab_scales, V_PLANE, a, r)
+        for a, r in rows[:2]:
+            load_scale_rows(tab2_s, tab2_scales, V2_PLANE, a, r)
+        load_words(tab2_w[0], tab2_words, 0)
+        for a, r in rows[2:]:
+            load_scale_rows(tab2_s, tab2_scales, V2_PLANE, a, r)
+        load_words(tab2_w[1], tab2_words, 1)
+        nc.sync.dma_start(wg_raw[0][:], wgate[0:KP, :].rearrange("(p t) n -> p t n", t=PACK))
+        nc.sync.dma_start(trust_sb[:], trust.rearrange("(g p t) -> p g t", g=2, t=PACK))
+        nc.sync.dma_start(wact_w[:], wact_words.bitcast(I32).rearrange("g p e -> p g e"))
+        for r in range(4):
+            src = wact_scales.bitcast(I32).rearrange("g (q r) e -> r q g e", r=4)[r]
+            nc.sync.dma_start(wact_s[r:P:32, :, :], src)
+        nc.sync.dma_start(wg_raw[1][:], wgate[KP : 2 * KP, :].rearrange("(p t) n -> p t n", t=PACK))
+
+        v_w = [keep.tile([P, S], U32, name=f"v_w{a}", align_bytes=64) for a in range(2)]
+        v_s_list = keep.tile([P, S], U8, name="v_s_list", align_bytes=64)
+        v_s = keep.tile([P, S], U8, name="v_s", align_bytes=64)
+        v2_w = [[keep.tile([P, JW], U32, name=f"v2_w{a}{jh}", align_bytes=64) for jh in range(2)] for a in range(2)]
+        v2_s = [keep.tile([P, JW], U8, name=f"v2_s{jh}", align_bytes=64) for jh in range(2)]
+
+        for a in range(2):
+            nc.vector.tensor_copy(
+                v_w[a][:].rearrange("p (g t m) -> p g m t", g=2, t=PACK),
+                tab_w[a][:].bitcast(U32).indirect(idx[:]),
+            )
+        nc.vector.tensor_copy(v_s_list[:], tab_s[:].bitcast(U8).indirect(idx[:]))
+
+        def probe_list(jh):
+            return idx2[:, jh * JW // 16 : (jh + 1) * JW // 16]
+
+        def gather_probe_words(a, jh):
+            nc.vector.tensor_copy(v2_w[a][jh][:], tab2_w[a][:].bitcast(U32).indirect(probe_list(jh)))
+
+        def gather_probe_scales(jh):
+            nc.vector.tensor_copy(v2_s[jh][:], tab2_s[:].bitcast(U8).indirect(probe_list(jh)))
+
+        gather_probe_words(0, 0)
+        nc.vector.tensor_copy(
+            v_s[:].rearrange("p (g t m) -> p g t m", g=2, t=PACK),
+            v_s_list[:].rearrange("p (g m t) -> p g t m", g=2, t=PACK),
+        )
+        gather_probe_scales(0)
+        gather_probe_words(0, 1)
+        gather_probe_scales(1)
+
+        def sim_pass(acc, a, g, t, jh):
+            cols = slice(g * KP + t * P, g * KP + (t + 1) * P)
+            nc.tensor.matmul_mx(
+                out=acc[:],
+                lhsT=v_w[a][:, cols].bitcast(FP8X4),
+                lhsT_scale=v_s[V_PLANE[a] :, cols],
+                rhs=v2_w[a][jh][:].bitcast(FP8X4),
+                rhs_scale=v2_s[jh][V2_PLANE[a] :, :],
+                start=(a == 0),
+                stop=(a == 1),
+            )
+
+        h_w = [[keep.tile([P, JW], U32, name=f"h_w{g}{jh}", align_bytes=64) for jh in range(2)] for g in range(2)]
+        h_s = [[keep.tile([P, JW], U8, name=f"h_s{g}{jh}", align_bytes=64) for jh in range(2)] for g in range(2)]
+        wg_bf = [keep.tile([P, N * PACK], BF16, name=f"wg_bf{g}", align_bytes=64) for g in range(2)]
+        wg_w = [keep.tile([P, N], U32, name=f"wg_w{g}", align_bytes=64) for g in range(2)]
+        wg_s = [keep.tile([P, N], U8, name=f"wg_s{g}", align_bytes=64) for g in range(2)]
+
+        def pairs_out(ap):
+            return ap.rearrange("p (c i t) -> p c t i", i=2, t=PACK)
+
+        def pairs_in(ap):
+            return ap.rearrange("p t (c i) -> p c t i", i=2)
+
+        def separate(accs, g):
+            th = work.tile([P, PACK, JW], F32, name="th", bufs=3)
+            for t in range(PACK):
+                nc.scalar.activation(th[:, t, :], accs[t][:], ACT.Tanh, scale=sharp_sb[:, g, t : t + 1])
+            return th
+
+        def weigh_and_quantize(th, g, jh):
+            hb = work.tile([P, JW * PACK], BF16, name="hb", align_bytes=64)
+            factor = trust_sb[:, g, :].unsqueeze(1).unsqueeze(3).to_broadcast([P, HALF // 2, PACK, 2])
+            for u in range(2):
+                nc.vector.tensor_tensor(
+                    pairs_out(hb[:, u * HALF * PACK : (u + 1) * HALF * PACK]),
+                    pairs_in(th[:, :, u * HALF : (u + 1) * HALF]),
+                    factor,
+                    ALU.mult,
+                )
+            for u in range(2):
+                cols = slice(u * HALF, (u + 1) * HALF)
+                nc.vector.quantize_mx(
+                    out=h_w[g][jh][:, cols].bitcast(FP8X4),
+                    scales=h_s[g][jh][:, cols],
+                    in_=hb[:, u * HALF * PACK : (u + 1) * HALF * PACK],
+                )
+
+        def quantize_gate(g):
+            nc.vector.quantize_mx(out=wg_w[g][:].bitcast(FP8X4), scales=wg_s[g][:], in_=wg_bf[g][:])
+
+        def similarity(g, jh):
+            accs = [psum.tile([P, JW], F32, name="bank") for t in range(PACK)]
+            for t in range(PACK):
+                sim_pass(accs[t], 0, g, t, jh)
+                sim_pass(accs[t], 1, g, t, jh)
+            return accs
+
+        def project(nb, jh):
+            cols = slice(nb * P, (nb + 1) * P)
+            c = psum.tile([P, JW], F32, name="bank")
+            y = psum.tile([P, JW], F32, name="bank")
+            for g in range(2):
+                nc.tensor.matmul_mx(
+                    out=c[:], lhsT=wg_w[g][:, cols].bitcast(FP8X4), lhsT_scale=wg_s[g][:, cols],
+                    rhs=h_w[g][jh][:].bitcast(FP8X4), rhs_scale=h_s[g][jh][:],
+                    start=(g == 0), stop=(g == 1),
+                )
+            for g in range(2):
+                nc.tensor.matmul_mx(
+                    out=y[:],
+                    lhsT=wact_w[:, g, :].bitcast(U8)[:, 2 * nb * P : 2 * (nb + 1) * P].bitcast(FP4X4),
+                    lhsT_scale=wact_s[:, g, :].bitcast(U8)[:, cols],
+                    rhs=h_w[g][jh][:].bitcast(FP8X4), rhs_scale=h_s[g][jh][:],
+                    start=(g == 0), stop=(g == 1),
+                )
+            gate = work.tile([P, JW], F32, name="gate", bufs=3)
+            nc.scalar.activation(gate[:], c[:], ACT.Sigmoid)
+            res = work.tile([P, JW], F32, name="res", bufs=4)
+            nc.vector.tensor_tensor(res[:], y[:], gate[:], ALU.mult)
+            nc.sync.dma_start(out[cols, jh * JW : (jh + 1) * JW], res[:])
+
+        first = [[psum.tile([P, JW], F32, name="bank") for t in range(PACK)] for g in range(2)]
+        for g in range(2):
+            for t in range(PACK):
+                sim_pass(first[g][t], 0, g, t, 0)
+        gather_probe_words(1, 0)
+        gather_probe_words(1, 1)
+        for g in range(2):
+            for t in range(PACK):
+                sim_pass(first[g][t], 1, g, t, 0)
+        th00 = separate(first[0], 0)
+        th10 = separate(first[1], 1)
+        nc.vector.tensor_copy(pairs_out(wg_bf[0][:]), pairs_in(wg_raw[0][:]))
+        weigh_and_quantize(th00, 0, 0)
+        th01 = separate(similarity(0, 1), 0)
+        quantize_gate(0)
+        weigh_and_quantize(th10, 1, 0)
+        nc.scalar.copy(pairs_out(wg_bf[1][:]), pairs_in(wg_raw[1][:]))
+        th11 = separate(similarity(1, 1), 1)
+        quantize_gate(1)
+        weigh_and_quantize(th01, 0, 1)
+        project(0, 0)
+        project(1, 0)
+        weigh_and_quantize(th11, 1, 1)
+        project(2, 0)
+        project(3, 0)
+        for nb in range(4):
+            project(nb, 1)

@@ -1,6 +1,7 @@
 from contextlib import ExitStack
 
 import concourse.mybir as mybir
+from concourse.masks import make_identity
 
 K, T, S, T2, S2, N = 1024, 2048, 1024, 4096, 1024, 512
 FLOPS = 2 * K * S * S2 + 2 * 2 * S * N * S2
@@ -21,8 +22,8 @@ PACK = 4
 KP = P * PACK
 JW = 512
 HALF = JW // 2
-V_PLANE = (12, 8)
-V2_PLANE = (0, 4)
+PLANE = (0, 4)
+KIB = 1024
 
 
 def tile_list_hopfield_episode_actions_kernel(
@@ -35,96 +36,106 @@ def tile_list_hopfield_episode_actions_kernel(
         work = ctx.enter_context(tc.tile_pool(name="work", bufs=2))
         psum = ctx.enter_context(tc.psum_pool(name="psum", bufs=8))
 
+        reuse = ctx.enter_context(tc.tile_pool(name="reuse", bufs=1))
+
         idx = keep.tile([P, S // 16], U16, name="idx")
         idx2 = keep.tile([P, S2 // 16], U16, name="idx2")
-        tab_w = [keep.tile([P, T], I32, name=f"tab_w{a}", align_bytes=64) for a in range(2)]
-        tab2_w = [keep.tile([P, T2], I32, name=f"tab2_w{a}", align_bytes=64) for a in range(2)]
+        tab_w = [
+            reuse.tile([P, T], I32, name="tab_w0", offset=0, align_bytes=64),
+            reuse.tile([P, T], I32, name="tab_w1", offset=11 * KIB, align_bytes=64),
+        ]
+        tab2_w = [keep.tile([P, T2], I32, name="tab2_w0", align_bytes=64)]
         tab_s = keep.tile([P, T // 4], I32, name="tab_s", align_bytes=64)
         tab2_s = keep.tile([P, T2 // 4], I32, name="tab2_s", align_bytes=64)
-        wact_w = keep.tile([P, 2, 2 * N // 4], I32, name="wact_w", align_bytes=64)
-        wact_s = keep.tile([P, 2, N // 4], I32, name="wact_s", align_bytes=64)
-        sharp_sb = keep.tile([P, 2, PACK], F32, name="sharp_sb")
-        trust_sb = keep.tile([P, 2, PACK], F32, name="trust_sb")
-        wg_raw = [keep.tile([P, PACK, N], F32, name=f"wg_raw{g}") for g in range(2)]
+        rows = keep.tile([P, KP], F32, name="rows")
+        ident = keep.tile([P, P], F32, name="ident")
+        factors = keep.tile([P, PACK, 4], F32, name="factors")
         warm = keep.tile([P, 8], F32, name="warm")
         warm_out = keep.tile([P, 8], F32, name="warm_out")
 
-        nc.vector.memset(tab_s[:], 0)
-        nc.gpsimd.memset(tab2_s[:], 0)
+        nc.gpsimd.memset(tab_s[:], 0)
+        nc.vector.memset(tab2_s[:], 0)
         nc.vector.memset(warm[:], 0.0)
-        nc.vector.memset(wact_s[:], 0)
+        nc.gpsimd.memset(rows[:], 0.0)
+        nc.gpsimd.dma_start(rows[0:2, :], trust.rearrange("(g i) -> g i", g=2))
+        nc.gpsimd.dma_start(rows[2:4, :], sharp.rearrange("(g i) -> g i", g=2))
+        make_identity(nc, ident[:])
         nc.scalar.activation(warm_out[:], warm[:], ACT.Sigmoid)
 
         def load_words(dst, words, a):
             nc.sync.dma_start(dst[:], words[a].rearrange("p t i -> p (t i)").bitcast(I32))
 
-        def load_scale_rows(dst, scales, planes, a, r):
-            src = scales[a].bitcast(I32).rearrange("(q r) t -> r q t", r=4)[r]
-            nc.sync.dma_start(dst[planes[a] + r : P : 32, :], src)
-
-        rows = [(a, r) for a in range(2) for r in range(4)]
         nc.sync.dma_start(idx[:], offs)
-        load_words(tab_w[0], tab_words, 0)
         nc.sync.dma_start(idx2[:], offs2)
-        nc.sync.dma_start(sharp_sb[:], sharp.rearrange("(g p t) -> p g t", g=2, t=PACK))
-        for a, r in rows[:4]:
-            load_scale_rows(tab_s, tab_scales, V_PLANE, a, r)
+        for dst, scales in ((tab_s, tab_scales), (tab2_s, tab2_scales)):
+            for a in range(2):
+                nc.sync.dma_start(dst[PLANE[a] : P : 8, :], scales[a].bitcast(I32))
+        load_words(tab_w[0], tab_words, 0)
         load_words(tab_w[1], tab_words, 1)
-        for a, r in rows[4:]:
-            load_scale_rows(tab_s, tab_scales, V_PLANE, a, r)
-        for a, r in rows[:2]:
-            load_scale_rows(tab2_s, tab2_scales, V2_PLANE, a, r)
         load_words(tab2_w[0], tab2_words, 0)
-        for a, r in rows[2:]:
-            load_scale_rows(tab2_s, tab2_scales, V2_PLANE, a, r)
-        load_words(tab2_w[1], tab2_words, 1)
-        nc.sync.dma_start(wg_raw[0][:], wgate[0:KP, :].rearrange("(p t) n -> p t n", t=PACK))
-        nc.sync.dma_start(trust_sb[:], trust.rearrange("(g p t) -> p g t", g=2, t=PACK))
-        nc.sync.dma_start(wact_w[:], wact_words.bitcast(I32).rearrange("g p e -> p g e"))
-        for r in range(4):
-            src = wact_scales.bitcast(I32).rearrange("g (q r) e -> r q g e", r=4)[r]
-            nc.sync.dma_start(wact_s[r:P:32, :, :], src)
-        nc.sync.dma_start(wg_raw[1][:], wgate[KP : 2 * KP, :].rearrange("(p t) n -> p t n", t=PACK))
+
+        factors_ps = psum.tile([P, PACK, P], F32, name="bank")
+        for t in range(PACK):
+            nc.tensor.transpose(factors_ps[:, t, :], rows[:, t:KP:PACK], ident[:])
+        nc.scalar.copy(factors[:], factors_ps[:, :, 0:4])
 
         v_w = [keep.tile([P, S], U32, name=f"v_w{a}", align_bytes=64) for a in range(2)]
         v_s_list = keep.tile([P, S], U8, name="v_s_list", align_bytes=64)
-        v_s = keep.tile([P, S], U8, name="v_s", align_bytes=64)
+        v2_s_list = reuse.tile([P, S2], U8, name="v2_s_list", offset=20 * KIB, align_bytes=64)
+        planes = keep.tile([P, S + S2], U8, name="planes", align_bytes=64)
         v2_w = [[keep.tile([P, JW], U32, name=f"v2_w{a}{jh}", align_bytes=64) for jh in range(2)] for a in range(2)]
-        v2_s = [keep.tile([P, JW], U8, name=f"v2_s{jh}", align_bytes=64) for jh in range(2)]
 
+        nc.vector.tensor_copy(v_s_list[:], tab_s[:].bitcast(U8).indirect(idx[:]))
+        nc.vector.tensor_copy(v2_s_list[:], tab2_s[:].bitcast(U8).indirect(idx2[:]))
+        nc.vector.tensor_copy(
+            planes[:, 0:S].rearrange("p (g t m) -> p g t m", g=2, t=PACK),
+            v_s_list[:].rearrange("p (g m t) -> p g t m", g=2, t=PACK),
+        )
+        nc.vector.tensor_copy(planes[:, S:].bitcast(I32), v2_s_list[:].bitcast(I32))
+        for a in range(2):
+            for r in range(1, 4):
+                nc.sync.dma_start(
+                    planes[PLANE[a] + r : P : 32, :].bitcast(I32),
+                    planes[PLANE[a] + 8 * r : P : 32, :].bitcast(I32),
+                )
+        tab2_w.append(reuse.tile([P, T2], I32, name="tab2_w1", offset=20 * KIB, align_bytes=64))
+        load_words(tab2_w[1], tab2_words, 1)
         for a in range(2):
             nc.vector.tensor_copy(
                 v_w[a][:].rearrange("p (g t m) -> p g m t", g=2, t=PACK),
                 tab_w[a][:].bitcast(U32).indirect(idx[:]),
             )
-        nc.vector.tensor_copy(v_s_list[:], tab_s[:].bitcast(U8).indirect(idx[:]))
 
-        def probe_list(jh):
-            return idx2[:, jh * JW // 16 : (jh + 1) * JW // 16]
+        wg_raw = [
+            reuse.tile([P, PACK, N], F32, name="wg_raw0", offset=0, align_bytes=64),
+            reuse.tile([P, PACK, N], F32, name="wg_raw1", offset=8 * KIB, align_bytes=64),
+        ]
+        wact_w = reuse.tile([P, 2, 2 * N // 4], I32, name="wact_w", offset=16 * KIB, align_bytes=64)
+        wact_s = reuse.tile([P, 2, N // 4], I32, name="wact_s", offset=18 * KIB, align_bytes=64)
+        nc.vector.memset(wact_s[:], 0)
+        for g in range(2):
+            nc.sync.dma_start(wg_raw[g][:], wgate[g * KP : (g + 1) * KP, :].rearrange("(p t) n -> p t n", t=PACK))
+        nc.sync.dma_start(wact_w[:], wact_words.bitcast(I32).rearrange("g p e -> p g e"))
+        for r in range(4):
+            src = wact_scales.bitcast(I32).rearrange("g (q r) e -> r q g e", r=4)[r]
+            nc.sync.dma_start(wact_s[r:P:32, :, :], src)
 
         def gather_probe_words(a, jh):
-            nc.vector.tensor_copy(v2_w[a][jh][:], tab2_w[a][:].bitcast(U32).indirect(probe_list(jh)))
+            probe_list = idx2[:, jh * JW // 16 : (jh + 1) * JW // 16]
+            nc.vector.tensor_copy(v2_w[a][jh][:], tab2_w[a][:].bitcast(U32).indirect(probe_list))
 
-        def gather_probe_scales(jh):
-            nc.vector.tensor_copy(v2_s[jh][:], tab2_s[:].bitcast(U8).indirect(probe_list(jh)))
-
-        gather_probe_words(0, 0)
-        nc.vector.tensor_copy(
-            v_s[:].rearrange("p (g t m) -> p g t m", g=2, t=PACK),
-            v_s_list[:].rearrange("p (g m t) -> p g t m", g=2, t=PACK),
-        )
-        gather_probe_scales(0)
-        gather_probe_words(0, 1)
-        gather_probe_scales(1)
+        for jh in range(2):
+            for a in range(2):
+                gather_probe_words(a, jh)
 
         def sim_pass(acc, a, g, t, jh):
             cols = slice(g * KP + t * P, g * KP + (t + 1) * P)
             nc.tensor.matmul_mx(
                 out=acc[:],
                 lhsT=v_w[a][:, cols].bitcast(FP8X4),
-                lhsT_scale=v_s[V_PLANE[a] :, cols],
+                lhsT_scale=planes[PLANE[a] :, cols],
                 rhs=v2_w[a][jh][:].bitcast(FP8X4),
-                rhs_scale=v2_s[jh][V2_PLANE[a] :, :],
+                rhs_scale=planes[PLANE[a] :, S + jh * JW : S + (jh + 1) * JW],
                 start=(a == 0),
                 stop=(a == 1),
             )
@@ -144,12 +155,12 @@ def tile_list_hopfield_episode_actions_kernel(
         def separate(accs, g):
             th = work.tile([P, PACK, JW], F32, name="th", bufs=3)
             for t in range(PACK):
-                nc.scalar.activation(th[:, t, :], accs[t][:], ACT.Tanh, scale=sharp_sb[:, g, t : t + 1])
+                nc.scalar.activation(th[:, t, :], accs[t][:], ACT.Tanh, scale=factors[:, t, 2 + g : 3 + g])
             return th
 
         def weigh_and_quantize(th, g, jh):
             hb = work.tile([P, JW * PACK], BF16, name="hb", align_bytes=64)
-            factor = trust_sb[:, g, :].unsqueeze(1).unsqueeze(3).to_broadcast([P, HALF // 2, PACK, 2])
+            factor = factors[:, :, g : g + 1].unsqueeze(1).to_broadcast([P, HALF // 2, PACK, 2])
             for u in range(2):
                 nc.vector.tensor_tensor(
                     pairs_out(hb[:, u * HALF * PACK : (u + 1) * HALF * PACK]),
@@ -203,8 +214,6 @@ def tile_list_hopfield_episode_actions_kernel(
         for g in range(2):
             for t in range(PACK):
                 sim_pass(first[g][t], 0, g, t, 0)
-        gather_probe_words(1, 0)
-        gather_probe_words(1, 1)
         for g in range(2):
             for t in range(PACK):
                 sim_pass(first[g][t], 1, g, t, 0)

@@ -1,7 +1,6 @@
 from contextlib import ExitStack
 
 import concourse.mybir as mybir
-from concourse.masks import make_identity
 
 K, T, S, T2, S2, N = 1024, 2048, 1024, 4096, 1024, 512
 FLOPS = 2 * K * S * S2 + 2 * 2 * S * N * S2
@@ -34,54 +33,52 @@ def tile_list_hopfield_episode_actions_kernel(
     with ExitStack() as ctx:
         keep = ctx.enter_context(tc.tile_pool(name="keep", bufs=1))
         work = ctx.enter_context(tc.tile_pool(name="work", bufs=2))
-        psum = ctx.enter_context(tc.psum_pool(name="psum", bufs=8))
-
+        psum = ctx.enter_context(tc.psum_pool(name="psum", bufs=1))
         reuse = ctx.enter_context(tc.tile_pool(name="reuse", bufs=1))
 
         idx = keep.tile([P, S // 16], U16, name="idx")
         idx2 = keep.tile([P, S2 // 16], U16, name="idx2")
         tab_w = [
             reuse.tile([P, T], I32, name="tab_w0", offset=0, align_bytes=64),
-            reuse.tile([P, T], I32, name="tab_w1", offset=11 * KIB, align_bytes=64),
+            keep.tile([P, T], I32, name="tab_w1", align_bytes=64),
         ]
-        tab2_w = [keep.tile([P, T2], I32, name="tab2_w0", align_bytes=64)]
+        tab2_w = [reuse.tile([P, T2], I32, name="tab2_w0", offset=8 * KIB, align_bytes=64)]
         tab_s = keep.tile([P, T // 4], I32, name="tab_s", align_bytes=64)
         tab2_s = keep.tile([P, T2 // 4], I32, name="tab2_s", align_bytes=64)
-        rows = keep.tile([P, KP], F32, name="rows")
-        ident = keep.tile([P, P], F32, name="ident")
-        factors = keep.tile([P, PACK, 4], F32, name="factors")
+        wact_s = keep.tile([P, 2, N // 4], I32, name="wact_s", align_bytes=64)
+        sharp_sb = keep.tile([P, 2, 8], F32, name="sharp_sb")
+        trust_sb = keep.tile([P, 2, 8], F32, name="trust_sb")
         warm = keep.tile([P, 8], F32, name="warm")
         warm_out = keep.tile([P, 8], F32, name="warm_out")
 
         nc.gpsimd.memset(tab_s[:], 0)
         nc.vector.memset(tab2_s[:], 0)
         nc.vector.memset(warm[:], 0.0)
-        nc.gpsimd.memset(rows[:], 0.0)
-        nc.gpsimd.dma_start(rows[0:2, :], trust.rearrange("(g i) -> g i", g=2))
-        nc.gpsimd.dma_start(rows[2:4, :], sharp.rearrange("(g i) -> g i", g=2))
-        make_identity(nc, ident[:])
+        nc.gpsimd.memset(wact_s[:], 0)
+        nc.gpsimd.dma_start(sharp_sb[:, :, 0:PACK], sharp.rearrange("(g p t) -> p g t", g=2, t=PACK))
+        nc.gpsimd.dma_start(trust_sb[:, :, 0:PACK], trust.rearrange("(g p t) -> p g t", g=2, t=PACK))
+        for r in range(4):
+            src = wact_scales.bitcast(I32).rearrange("g (q r) e -> r q g e", r=4)[r]
+            nc.gpsimd.dma_start(wact_s[r:P:32, :, :], src)
         nc.scalar.activation(warm_out[:], warm[:], ACT.Sigmoid)
 
         def load_words(dst, words, a):
             nc.sync.dma_start(dst[:], words[a].rearrange("p t i -> p (t i)").bitcast(I32))
 
-        nc.sync.dma_start(idx[:], offs)
-        nc.sync.dma_start(idx2[:], offs2)
-        for dst, scales in ((tab_s, tab_scales), (tab2_s, tab2_scales)):
-            for a in range(2):
-                nc.sync.dma_start(dst[PLANE[a] : P : 8, :], scales[a].bitcast(I32))
-        load_words(tab_w[0], tab_words, 0)
-        load_words(tab_w[1], tab_words, 1)
-        load_words(tab2_w[0], tab2_words, 0)
+        def load_scales(dst, scales):
+            nc.sync.dma_start(dst[0:P:4, :], scales.bitcast(I32).rearrange("a q n -> q a n"))
 
-        factors_ps = psum.tile([P, PACK, P], F32, name="bank")
-        for t in range(PACK):
-            nc.tensor.transpose(factors_ps[:, t, :], rows[:, t:KP:PACK], ident[:])
-        nc.scalar.copy(factors[:], factors_ps[:, :, 0:4])
+        nc.sync.dma_start(idx[:], offs)
+        load_scales(tab_s, tab_scales)
+        nc.sync.dma_start(idx2[:], offs2)
+        load_scales(tab2_s, tab2_scales)
+        load_words(tab_w[0], tab_words, 0)
+        load_words(tab2_w[0], tab2_words, 0)
+        load_words(tab_w[1], tab_words, 1)
 
         v_w = [keep.tile([P, S], U32, name=f"v_w{a}", align_bytes=64) for a in range(2)]
         v_s_list = keep.tile([P, S], U8, name="v_s_list", align_bytes=64)
-        v2_s_list = reuse.tile([P, S2], U8, name="v2_s_list", offset=20 * KIB, align_bytes=64)
+        v2_s_list = reuse.tile([P, S2], U8, name="v2_s_list", offset=24 * KIB, align_bytes=64)
         planes = keep.tile([P, S + S2], U8, name="planes", align_bytes=64)
         v2_w = [[keep.tile([P, JW], U32, name=f"v2_w{a}{jh}", align_bytes=64) for jh in range(2)] for a in range(2)]
 
@@ -98,35 +95,32 @@ def tile_list_hopfield_episode_actions_kernel(
                     planes[PLANE[a] + r : P : 32, :].bitcast(I32),
                     planes[PLANE[a] + 8 * r : P : 32, :].bitcast(I32),
                 )
-        tab2_w.append(reuse.tile([P, T2], I32, name="tab2_w1", offset=20 * KIB, align_bytes=64))
+        tab2_w.append(reuse.tile([P, T2], I32, name="tab2_w1", offset=24 * KIB, align_bytes=64))
         load_words(tab2_w[1], tab2_words, 1)
-        for a in range(2):
-            nc.vector.tensor_copy(
-                v_w[a][:].rearrange("p (g t m) -> p g m t", g=2, t=PACK),
-                tab_w[a][:].bitcast(U32).indirect(idx[:]),
-            )
-
-        wg_raw = [
-            reuse.tile([P, PACK, N], F32, name="wg_raw0", offset=0, align_bytes=64),
-            reuse.tile([P, PACK, N], F32, name="wg_raw1", offset=8 * KIB, align_bytes=64),
-        ]
-        wact_w = reuse.tile([P, 2, 2 * N // 4], I32, name="wact_w", offset=16 * KIB, align_bytes=64)
-        wact_s = reuse.tile([P, 2, N // 4], I32, name="wact_s", offset=18 * KIB, align_bytes=64)
-        nc.vector.memset(wact_s[:], 0)
-        for g in range(2):
-            nc.sync.dma_start(wg_raw[g][:], wgate[g * KP : (g + 1) * KP, :].rearrange("(p t) n -> p t n", t=PACK))
-        nc.sync.dma_start(wact_w[:], wact_words.bitcast(I32).rearrange("g p e -> p g e"))
-        for r in range(4):
-            src = wact_scales.bitcast(I32).rearrange("g (q r) e -> r q g e", r=4)[r]
-            nc.sync.dma_start(wact_s[r:P:32, :, :], src)
 
         def gather_probe_words(a, jh):
             probe_list = idx2[:, jh * JW // 16 : (jh + 1) * JW // 16]
             nc.vector.tensor_copy(v2_w[a][jh][:], tab2_w[a][:].bitcast(U32).indirect(probe_list))
 
-        for jh in range(2):
-            for a in range(2):
+        for a in range(2):
+            nc.vector.tensor_copy(
+                v_w[a][:].rearrange("p (g t m) -> p g m t", g=2, t=PACK),
+                tab_w[a][:].bitcast(U32).indirect(idx[:]),
+            )
+            for jh in range(2):
                 gather_probe_words(a, jh)
+
+        wg_raw = [
+            reuse.tile([P, PACK, N], F32, name="wg_raw0", offset=2 * KIB, align_bytes=64),
+            reuse.tile([P, PACK, N], F32, name="wg_raw1", offset=12 * KIB, align_bytes=64),
+        ]
+        wact_w = reuse.tile([P, 2, 2 * N // 4], I32, name="wact_w", offset=10 * KIB, align_bytes=64)
+        for g in range(2):
+            nc.sync.dma_start(wg_raw[g][:], wgate[g * KP : (g + 1) * KP, :].rearrange("(p t) n -> p t n", t=PACK))
+        nc.sync.dma_start(wact_w[:], wact_words.bitcast(I32).rearrange("g p e -> p g e"))
+
+        def bank(b):
+            return psum.tile([P, JW], F32, name=f"bank{b}")
 
         def sim_pass(acc, a, g, t, jh):
             cols = slice(g * KP + t * P, g * KP + (t + 1) * P)
@@ -152,50 +146,75 @@ def tile_list_hopfield_episode_actions_kernel(
         def pairs_in(ap):
             return ap.rearrange("p t (c i) -> p c t i", i=2)
 
-        def separate(accs, g):
-            th = work.tile([P, PACK, JW], F32, name="th", bufs=3)
+        def separate_whole(accs, g):
+            th = work.tile([P, 2, PACK, HALF], F32, name="th", bufs=3)
             for t in range(PACK):
-                nc.scalar.activation(th[:, t, :], accs[t][:], ACT.Tanh, scale=factors[:, t, 2 + g : 3 + g])
+                nc.scalar.activation(
+                    th[:, :, t, :], accs[t][:].rearrange("p (u c) -> p u c", u=2), ACT.Tanh,
+                    scale=sharp_sb[:, g, t : t + 1],
+                )
             return th
 
+        def separate_halves(accs, g):
+            th = work.tile([P, 2, PACK, HALF], F32, name="th", bufs=3)
+            for u in range(2):
+                for t in range(PACK):
+                    nc.scalar.activation(
+                        th[:, u, t, :], accs[t][:, u * HALF : (u + 1) * HALF], ACT.Tanh,
+                        scale=sharp_sb[:, g, t : t + 1],
+                    )
+            return th
+
+        def weigh(th, hb, g, u):
+            factor = trust_sb[:, g, 0:PACK].unsqueeze(1).unsqueeze(3).to_broadcast([P, HALF // 2, PACK, 2])
+            nc.vector.tensor_tensor(
+                pairs_out(hb[:, u * HALF * PACK : (u + 1) * HALF * PACK]), pairs_in(th[:, u, :, :]), factor, ALU.mult,
+            )
+
+        def quantize(hb, g, jh, first, last):
+            cols = slice(first * HALF, last * HALF)
+            nc.vector.quantize_mx(
+                out=h_w[g][jh][:, cols].bitcast(FP8X4),
+                scales=h_s[g][jh][:, cols],
+                in_=hb[:, first * HALF * PACK : last * HALF * PACK],
+            )
+
+        def rounded():
+            return work.tile([P, JW * PACK], BF16, name="hb", align_bytes=64, bufs=3)
+
         def weigh_and_quantize(th, g, jh):
-            hb = work.tile([P, JW * PACK], BF16, name="hb", align_bytes=64)
-            factor = factors[:, :, g : g + 1].unsqueeze(1).to_broadcast([P, HALF // 2, PACK, 2])
+            hb = rounded()
             for u in range(2):
-                nc.vector.tensor_tensor(
-                    pairs_out(hb[:, u * HALF * PACK : (u + 1) * HALF * PACK]),
-                    pairs_in(th[:, :, u * HALF : (u + 1) * HALF]),
-                    factor,
-                    ALU.mult,
-                )
+                weigh(th, hb, g, u)
             for u in range(2):
-                cols = slice(u * HALF, (u + 1) * HALF)
-                nc.vector.quantize_mx(
-                    out=h_w[g][jh][:, cols].bitcast(FP8X4),
-                    scales=h_s[g][jh][:, cols],
-                    in_=hb[:, u * HALF * PACK : (u + 1) * HALF * PACK],
-                )
+                quantize(hb, g, jh, u, u + 1)
 
         def quantize_gate(g):
             nc.vector.quantize_mx(out=wg_w[g][:].bitcast(FP8X4), scales=wg_s[g][:], in_=wg_bf[g][:])
 
         def similarity(g, jh):
-            accs = [psum.tile([P, JW], F32, name="bank") for t in range(PACK)]
+            accs = [bank(PACK * g + t) for t in range(PACK)]
             for t in range(PACK):
                 sim_pass(accs[t], 0, g, t, jh)
                 sim_pass(accs[t], 1, g, t, jh)
             return accs
 
-        def project(nb, jh):
+        def gate_of(nb, jh):
             cols = slice(nb * P, (nb + 1) * P)
-            c = psum.tile([P, JW], F32, name="bank")
-            y = psum.tile([P, JW], F32, name="bank")
+            c = bank(2 * nb)
             for g in range(2):
                 nc.tensor.matmul_mx(
                     out=c[:], lhsT=wg_w[g][:, cols].bitcast(FP8X4), lhsT_scale=wg_s[g][:, cols],
                     rhs=h_w[g][jh][:].bitcast(FP8X4), rhs_scale=h_s[g][jh][:],
                     start=(g == 0), stop=(g == 1),
                 )
+            gate = work.tile([P, JW], F32, name="gate", bufs=8)
+            nc.scalar.activation(gate[:], c[:], ACT.Sigmoid)
+            return gate
+
+        def act_out(gate, nb, jh):
+            cols = slice(nb * P, (nb + 1) * P)
+            y = bank(2 * nb + 1)
             for g in range(2):
                 nc.tensor.matmul_mx(
                     out=y[:],
@@ -204,34 +223,34 @@ def tile_list_hopfield_episode_actions_kernel(
                     rhs=h_w[g][jh][:].bitcast(FP8X4), rhs_scale=h_s[g][jh][:],
                     start=(g == 0), stop=(g == 1),
                 )
-            gate = work.tile([P, JW], F32, name="gate", bufs=3)
-            nc.scalar.activation(gate[:], c[:], ACT.Sigmoid)
-            res = work.tile([P, JW], F32, name="res", bufs=4)
+            res = work.tile([P, JW], F32, name="res", bufs=8)
             nc.vector.tensor_tensor(res[:], y[:], gate[:], ALU.mult)
             nc.sync.dma_start(out[cols, jh * JW : (jh + 1) * JW], res[:])
 
-        first = [[psum.tile([P, JW], F32, name="bank") for t in range(PACK)] for g in range(2)]
-        for g in range(2):
-            for t in range(PACK):
-                sim_pass(first[g][t], 0, g, t, 0)
-        for g in range(2):
-            for t in range(PACK):
-                sim_pass(first[g][t], 1, g, t, 0)
-        th00 = separate(first[0], 0)
-        th10 = separate(first[1], 1)
+        first = [[bank(PACK * g + t) for t in range(PACK)] for g in range(2)]
+        for a in range(2):
+            for g in range(2):
+                for t in range(PACK):
+                    sim_pass(first[g][t], a, g, t, 0)
+        th00 = separate_halves(first[0], 0)
+        th10 = separate_whole(first[1], 1)
         nc.vector.tensor_copy(pairs_out(wg_bf[0][:]), pairs_in(wg_raw[0][:]))
         weigh_and_quantize(th00, 0, 0)
-        th01 = separate(similarity(0, 1), 0)
+        th01 = separate_whole(similarity(0, 1), 0)
         quantize_gate(0)
         weigh_and_quantize(th10, 1, 0)
         nc.scalar.copy(pairs_out(wg_bf[1][:]), pairs_in(wg_raw[1][:]))
-        th11 = separate(similarity(1, 1), 1)
+        th11 = separate_halves(similarity(1, 1), 1)
+        hb01 = rounded()
+        weigh(th01, hb01, 0, 0)
         quantize_gate(1)
-        weigh_and_quantize(th01, 0, 1)
-        project(0, 0)
-        project(1, 0)
+        weigh(th01, hb01, 0, 1)
+        quantize(hb01, 0, 1, 0, 2)
+        gates = [gate_of(nb, 0) for nb in range(4)]
         weigh_and_quantize(th11, 1, 1)
-        project(2, 0)
-        project(3, 0)
+        later = []
         for nb in range(4):
-            project(nb, 1)
+            act_out(gates[nb], nb, 0)
+            later.append(gate_of(nb, 1))
+        for nb in range(4):
+            act_out(later[nb], nb, 1)

@@ -42,7 +42,10 @@ def tile_list_hopfield_episode_actions_kernel(
             reuse.tile([P, T], I32, name="tab_w0", offset=0, align_bytes=64),
             keep.tile([P, T], I32, name="tab_w1", align_bytes=64),
         ]
-        tab2_w = [reuse.tile([P, T2], I32, name="tab2_w0", offset=8 * KIB, align_bytes=64)]
+        tab2_w = [
+            reuse.tile([P, T2], I32, name="tab2_w0", offset=8 * KIB, align_bytes=64),
+            keep.tile([P, T2], I32, name="tab2_w1", align_bytes=64),
+        ]
         tab_s = keep.tile([P, T // 4], I32, name="tab_s", align_bytes=64)
         tab2_s = keep.tile([P, T2 // 4], I32, name="tab2_s", align_bytes=64)
         wact_s = keep.tile([P, 2, N // 4], I32, name="wact_s", align_bytes=64)
@@ -75,10 +78,11 @@ def tile_list_hopfield_episode_actions_kernel(
         load_words(tab_w[0], tab_words, 0)
         load_words(tab2_w[0], tab2_words, 0)
         load_words(tab_w[1], tab_words, 1)
+        load_words(tab2_w[1], tab2_words, 1)
 
         v_w = [keep.tile([P, S], U32, name=f"v_w{a}", align_bytes=64) for a in range(2)]
         v_s_list = keep.tile([P, S], U8, name="v_s_list", align_bytes=64)
-        v2_s_list = reuse.tile([P, S2], U8, name="v2_s_list", offset=24 * KIB, align_bytes=64)
+        v2_s_list = keep.tile([P, S2], U8, name="v2_s_list", align_bytes=64)
         planes = keep.tile([P, S + S2], U8, name="planes", align_bytes=64)
         v2_w = [[keep.tile([P, JW], U32, name=f"v2_w{a}{jh}", align_bytes=64) for jh in range(2)] for a in range(2)]
 
@@ -91,12 +95,10 @@ def tile_list_hopfield_episode_actions_kernel(
         nc.vector.tensor_copy(planes[:, S:].bitcast(I32), v2_s_list[:].bitcast(I32))
         for a in range(2):
             for r in range(1, 4):
-                nc.sync.dma_start(
+                nc.scalar.dma_start(
                     planes[PLANE[a] + r : P : 32, :].bitcast(I32),
                     planes[PLANE[a] + 8 * r : P : 32, :].bitcast(I32),
                 )
-        tab2_w.append(reuse.tile([P, T2], I32, name="tab2_w1", offset=24 * KIB, align_bytes=64))
-        load_words(tab2_w[1], tab2_words, 1)
 
         def gather_probe_words(a, jh):
             probe_list = idx2[:, jh * JW // 16 : (jh + 1) * JW // 16]
@@ -136,7 +138,7 @@ def tile_list_hopfield_episode_actions_kernel(
 
         h_w = [[keep.tile([P, JW], U32, name=f"h_w{g}{jh}", align_bytes=64) for jh in range(2)] for g in range(2)]
         h_s = [[keep.tile([P, JW], U8, name=f"h_s{g}{jh}", align_bytes=64) for jh in range(2)] for g in range(2)]
-        wg_bf = [keep.tile([P, N * PACK], BF16, name=f"wg_bf{g}", align_bytes=64) for g in range(2)]
+        wg_bf = [keep.tile([P, N * PACK], BF16, name="wg_bf0", align_bytes=64)]
         wg_w = [keep.tile([P, N], U32, name=f"wg_w{g}", align_bytes=64) for g in range(2)]
         wg_s = [keep.tile([P, N], U8, name=f"wg_s{g}", align_bytes=64) for g in range(2)]
 
@@ -147,7 +149,7 @@ def tile_list_hopfield_episode_actions_kernel(
             return ap.rearrange("p t (c i) -> p c t i", i=2)
 
         def separate_whole(accs, g):
-            th = work.tile([P, 2, PACK, HALF], F32, name="th", bufs=3)
+            th = work.tile([P, 2, PACK, HALF], F32, name="th", bufs=3, align_bytes=64)
             for t in range(PACK):
                 nc.scalar.activation(
                     th[:, :, t, :], accs[t][:].rearrange("p (u c) -> p u c", u=2), ACT.Tanh,
@@ -156,7 +158,7 @@ def tile_list_hopfield_episode_actions_kernel(
             return th
 
         def separate_halves(accs, g):
-            th = work.tile([P, 2, PACK, HALF], F32, name="th", bufs=3)
+            th = work.tile([P, 2, PACK, HALF], F32, name="th", bufs=3, align_bytes=64)
             for u in range(2):
                 for t in range(PACK):
                     nc.scalar.activation(
@@ -239,6 +241,7 @@ def tile_list_hopfield_episode_actions_kernel(
         th01 = separate_whole(similarity(0, 1), 0)
         quantize_gate(0)
         weigh_and_quantize(th10, 1, 0)
+        wg_bf.append(work.tile([P, N * PACK], BF16, name="th", bufs=3, align_bytes=64))
         nc.scalar.copy(pairs_out(wg_bf[1][:]), pairs_in(wg_raw[1][:]))
         th11 = separate_halves(similarity(1, 1), 1)
         hb01 = rounded()

@@ -143,10 +143,10 @@ def tile_list_hopfield_episode_actions_kernel(
         wg_s = [keep.tile([P, N], U8, name=f"wg_s{g}", align_bytes=64) for g in range(2)]
 
         def pairs_out(ap):
-            return ap.rearrange("p (c i t) -> p c t i", i=2, t=PACK)
+            return ap.rearrange("p (c i t) -> p c t i", i=4, t=PACK)
 
         def pairs_in(ap):
-            return ap.rearrange("p t (c i) -> p c t i", i=2)
+            return ap.rearrange("p t (c i) -> p c t i", i=4)
 
         def separate_whole(accs, g):
             th = work.tile([P, 2, PACK, HALF], F32, name="th", bufs=3, align_bytes=64)
@@ -168,7 +168,7 @@ def tile_list_hopfield_episode_actions_kernel(
             return th
 
         def weigh(th, hb, g, u):
-            factor = trust_sb[:, g, 0:PACK].unsqueeze(1).unsqueeze(3).to_broadcast([P, HALF // 2, PACK, 2])
+            factor = trust_sb[:, g, 0:PACK].unsqueeze(1).unsqueeze(3).to_broadcast([P, HALF // 4, PACK, 4])
             nc.vector.tensor_tensor(
                 pairs_out(hb[:, u * HALF * PACK : (u + 1) * HALF * PACK]), pairs_in(th[:, u, :, :]), factor, ALU.mult,
             )

@@ -72,10 +72,10 @@ def tile_list_hopfield_episode_actions_kernel(
             nc.sync.dma_start(dst[0:P:4, :], scales.bitcast(I32).rearrange("a q n -> q a n"))
 
         nc.sync.dma_start(idx[:], offs)
-        load_scales(tab_s, tab_scales)
         nc.sync.dma_start(idx2[:], offs2)
-        load_scales(tab2_s, tab2_scales)
+        load_scales(tab_s, tab_scales)
         load_words(tab_w[0], tab_words, 0)
+        load_scales(tab2_s, tab2_scales)
         load_words(tab2_w[0], tab2_words, 0)
         load_words(tab_w[1], tab_words, 1)
         load_words(tab2_w[1], tab2_words, 1)

@@ -39,12 +39,11 @@ def tile_list_hopfield_episode_actions_kernel(
         idx = keep.tile([P, S // 16], U16, name="idx")
         idx2 = keep.tile([P, S2 // 16], U16, name="idx2")
         tab_w = [
-            reuse.tile([P, T], I32, name="tab_w0", offset=0, align_bytes=64),
-            keep.tile([P, T], I32, name="tab_w1", align_bytes=64),
+            keep.tile([P, T], I32, name="tab_w0", align_bytes=64),
+            reuse.tile([P, T], I32, name="tab_w1", offset=7 * KIB, align_bytes=64),
         ]
         tab2_w = [
-            reuse.tile([P, T2], I32, name="tab2_w0", offset=8 * KIB, align_bytes=64),
-            keep.tile([P, T2], I32, name="tab2_w1", align_bytes=64),
+            keep.tile([P, T2], I32, name="tab2_w0", align_bytes=64),
         ]
         tab_s = keep.tile([P, T // 4], I32, name="tab_s", align_bytes=64)
         tab2_s = keep.tile([P, T2 // 4], I32, name="tab2_s", align_bytes=64)
@@ -76,29 +75,34 @@ def tile_list_hopfield_episode_actions_kernel(
         load_scales(tab_s, tab_scales)
         load_words(tab_w[0], tab_words, 0)
         load_scales(tab2_s, tab2_scales)
-        load_words(tab2_w[0], tab2_words, 0)
         load_words(tab_w[1], tab_words, 1)
-        load_words(tab2_w[1], tab2_words, 1)
+        load_words(tab2_w[0], tab2_words, 0)
 
-        v_w = [keep.tile([P, S], U32, name=f"v_w{a}", align_bytes=64) for a in range(2)]
-        v_s_list = keep.tile([P, S], U8, name="v_s_list", align_bytes=64)
-        v2_s_list = keep.tile([P, S2], U8, name="v2_s_list", align_bytes=64)
+        v_s_list = reuse.tile([P, S], U8, name="v_s_list", offset=24 * KIB, align_bytes=64)
+        v2_s_list = reuse.tile([P, S2], U8, name="v2_s_list", offset=40 * KIB, align_bytes=64)
         planes = keep.tile([P, S + S2], U8, name="planes", align_bytes=64)
         v2_w = [[keep.tile([P, JW], U32, name=f"v2_w{a}{jh}", align_bytes=64) for jh in range(2)] for a in range(2)]
 
         nc.vector.tensor_copy(v_s_list[:], tab_s[:].bitcast(U8).indirect(idx[:]))
         nc.vector.tensor_copy(v2_s_list[:], tab2_s[:].bitcast(U8).indirect(idx2[:]))
+        nc.vector.tensor_copy(planes[:, S:].bitcast(I32), v2_s_list[:].bitcast(I32))
         nc.vector.tensor_copy(
             planes[:, 0:S].rearrange("p (g t m) -> p g t m", g=2, t=PACK),
             v_s_list[:].rearrange("p (g m t) -> p g t m", g=2, t=PACK),
         )
-        nc.vector.tensor_copy(planes[:, S:].bitcast(I32), v2_s_list[:].bitcast(I32))
         for a in range(2):
             for r in range(1, 4):
-                nc.scalar.dma_start(
+                nc.sync.dma_start(
                     planes[PLANE[a] + r : P : 32, :].bitcast(I32),
                     planes[PLANE[a] + 8 * r : P : 32, :].bitcast(I32),
                 )
+
+        tab2_w.append(reuse.tile([P, T2], I32, name="tab2_w1", offset=24 * KIB, align_bytes=64))
+        load_words(tab2_w[1], tab2_words, 1)
+        v_w = [
+            reuse.tile([P, S], U32, name="v_w0", offset=40 * KIB, align_bytes=64),
+            keep.tile([P, S], U32, name="v_w1", align_bytes=64),
+        ]
 
         def gather_probe_words(a, jh):
             probe_list = idx2[:, jh * JW // 16 : (jh + 1) * JW // 16]
@@ -109,17 +113,24 @@ def tile_list_hopfield_episode_actions_kernel(
                 v_w[a][:].rearrange("p (g t m) -> p g m t", g=2, t=PACK),
                 tab_w[a][:].bitcast(U32).indirect(idx[:]),
             )
+        for a in range(2):
             for jh in range(2):
                 gather_probe_words(a, jh)
 
         wg_raw = [
-            reuse.tile([P, PACK, N], F32, name="wg_raw0", offset=2 * KIB, align_bytes=64),
-            reuse.tile([P, PACK, N], F32, name="wg_raw1", offset=12 * KIB, align_bytes=64),
+            reuse.tile([P, 2, PACK, N // 2], F32, name="wg_raw0", offset=0, align_bytes=64),
+            reuse.tile([P, 2, PACK, N // 2], F32, name="wg_raw1", offset=10 * KIB, align_bytes=64),
         ]
-        wact_w = reuse.tile([P, 2, 2 * N // 4], I32, name="wact_w", offset=10 * KIB, align_bytes=64)
-        for g in range(2):
-            nc.sync.dma_start(wg_raw[g][:], wgate[g * KP : (g + 1) * KP, :].rearrange("(p t) n -> p t n", t=PACK))
+        wact_w = reuse.tile([P, 2, 2 * N // 4], I32, name="wact_w", offset=8 * KIB, align_bytes=64)
+
+        def load_gate(h):
+            for g in range(2):
+                src = wgate[g * KP : (g + 1) * KP, h * N // 2 : (h + 1) * N // 2]
+                nc.sync.dma_start(wg_raw[h][:, g, :, :], src.rearrange("(p t) n -> p t n", t=PACK))
+
+        load_gate(0)
         nc.sync.dma_start(wact_w[:], wact_words.bitcast(I32).rearrange("g p e -> p g e"))
+        load_gate(1)
 
         def bank(b):
             return psum.tile([P, JW], F32, name=f"bank{b}")
@@ -147,6 +158,12 @@ def tile_list_hopfield_episode_actions_kernel(
 
         def pairs_in(ap):
             return ap.rearrange("p t (c i) -> p c t i", i=4)
+
+        def gate_out(ap):
+            return ap.rearrange("p (g c i t) -> p g c t i", g=2, i=4, t=PACK)
+
+        def gate_in(ap):
+            return ap.rearrange("p g t (c i) -> p g c t i", i=4)
 
         def separate_whole(accs, g):
             th = work.tile([P, 2, PACK, HALF], F32, name="th", bufs=3, align_bytes=64)
@@ -201,12 +218,12 @@ def tile_list_hopfield_episode_actions_kernel(
                 sim_pass(accs[t], 1, g, t, jh)
             return accs
 
-        def gate_of(nb, jh):
-            cols = slice(nb * P, (nb + 1) * P)
-            c = bank(2 * nb)
+        def gate_of(nb, jh, b):
+            c = bank(b)
             for g in range(2):
+                cols = slice((2 * g + nb % 2) * P, (2 * g + nb % 2 + 1) * P)
                 nc.tensor.matmul_mx(
-                    out=c[:], lhsT=wg_w[g][:, cols].bitcast(FP8X4), lhsT_scale=wg_s[g][:, cols],
+                    out=c[:], lhsT=wg_w[nb // 2][:, cols].bitcast(FP8X4), lhsT_scale=wg_s[nb // 2][:, cols],
                     rhs=h_w[g][jh][:].bitcast(FP8X4), rhs_scale=h_s[g][jh][:],
                     start=(g == 0), stop=(g == 1),
                 )
@@ -214,9 +231,9 @@ def tile_list_hopfield_episode_actions_kernel(
             nc.scalar.activation(gate[:], c[:], ACT.Sigmoid)
             return gate
 
-        def act_out(gate, nb, jh):
+        def action_of(nb, jh, b):
             cols = slice(nb * P, (nb + 1) * P)
-            y = bank(2 * nb + 1)
+            y = bank(b)
             for g in range(2):
                 nc.tensor.matmul_mx(
                     out=y[:],
@@ -225,9 +242,16 @@ def tile_list_hopfield_episode_actions_kernel(
                     rhs=h_w[g][jh][:].bitcast(FP8X4), rhs_scale=h_s[g][jh][:],
                     start=(g == 0), stop=(g == 1),
                 )
-            res = work.tile([P, JW], F32, name="res", bufs=8)
-            nc.vector.tensor_tensor(res[:], y[:], gate[:], ALU.mult)
-            nc.sync.dma_start(out[cols, jh * JW : (jh + 1) * JW], res[:])
+            return y
+
+        def finish(y, gate, nb, jh, pieces=1):
+            width = JW // pieces
+            for q in range(pieces):
+                cols = slice(q * width, (q + 1) * width)
+                res = work.tile([P, width], F32, name="res", bufs=8)
+                nc.vector.tensor_tensor(res[:], y[:, cols], gate[:, cols], ALU.mult)
+                start = jh * JW + q * width
+                nc.sync.dma_start(out[nb * P : (nb + 1) * P, start : start + width], res[:])
 
         first = [[bank(PACK * g + t) for t in range(PACK)] for g in range(2)]
         for a in range(2):
@@ -236,24 +260,34 @@ def tile_list_hopfield_episode_actions_kernel(
                     sim_pass(first[g][t], a, g, t, 0)
         th00 = separate_halves(first[0], 0)
         th10 = separate_whole(first[1], 1)
-        nc.vector.tensor_copy(pairs_out(wg_bf[0][:]), pairs_in(wg_raw[0][:]))
+        nc.vector.tensor_copy(gate_out(wg_bf[0][:]), gate_in(wg_raw[0][:]))
         weigh_and_quantize(th00, 0, 0)
         th01 = separate_whole(similarity(0, 1), 0)
         quantize_gate(0)
         weigh_and_quantize(th10, 1, 0)
+        sims11 = similarity(1, 1)
         wg_bf.append(work.tile([P, N * PACK], BF16, name="th", bufs=3, align_bytes=64))
-        nc.scalar.copy(pairs_out(wg_bf[1][:]), pairs_in(wg_raw[1][:]))
-        th11 = separate_halves(similarity(1, 1), 1)
+        nc.scalar.copy(gate_out(wg_bf[1][:]), gate_in(wg_raw[1][:]))
+
+        def project(nb, jh, b):
+            return gate_of(nb, jh, b), action_of(nb, jh, b + 1)
+
+        early = [project(nb, 0, 2 * nb) for nb in range(2)]
+        th11 = separate_halves(sims11, 1)
         hb01 = rounded()
-        weigh(th01, hb01, 0, 0)
+        for u in range(2):
+            weigh(th01, hb01, 0, u)
         quantize_gate(1)
-        weigh(th01, hb01, 0, 1)
         quantize(hb01, 0, 1, 0, 2)
-        gates = [gate_of(nb, 0) for nb in range(4)]
+        for nb in range(2):
+            finish(early[nb][1], early[nb][0], nb, 0)
+        late = [project(2 + nb, 0, 2 * nb) for nb in range(2)]
         weigh_and_quantize(th11, 1, 1)
-        later = []
-        for nb in range(4):
-            act_out(gates[nb], nb, 0)
-            later.append(gate_of(nb, 1))
-        for nb in range(4):
-            act_out(later[nb], nb, 1)
+        for nb in range(2):
+            finish(late[nb][1], late[nb][0], 2 + nb, 0)
+        for nb in range(2):
+            gate, y = project(nb, 1, 4 + 2 * nb)
+            finish(y, gate, nb, 1)
+        gates = [gate_of(2 + nb, 1, 2 * nb) for nb in range(2)]
+        for nb in range(2):
+            finish(action_of(2 + nb, 1, 2 * nb + 1), gates[nb], 2 + nb, 1, pieces=1 + nb)

@@ -47,7 +47,6 @@ def tile_list_hopfield_episode_actions_kernel(
         ]
         tab_s = keep.tile([P, T // 4], I32, name="tab_s", align_bytes=64)
         tab2_s = keep.tile([P, T2 // 4], I32, name="tab2_s", align_bytes=64)
-        wact_s = keep.tile([P, 2, N // 4], I32, name="wact_s", align_bytes=64)
         sharp_sb = keep.tile([P, 2, 8], F32, name="sharp_sb")
         trust_sb = keep.tile([P, 2, 8], F32, name="trust_sb")
         warm = keep.tile([P, 8], F32, name="warm")
@@ -56,12 +55,6 @@ def tile_list_hopfield_episode_actions_kernel(
         nc.gpsimd.memset(tab_s[:], 0)
         nc.vector.memset(tab2_s[:], 0)
         nc.vector.memset(warm[:], 0.0)
-        nc.gpsimd.memset(wact_s[:], 0)
-        nc.gpsimd.dma_start(sharp_sb[:, :, 0:PACK], sharp.rearrange("(g p t) -> p g t", g=2, t=PACK))
-        nc.gpsimd.dma_start(trust_sb[:, :, 0:PACK], trust.rearrange("(g p t) -> p g t", g=2, t=PACK))
-        for r in range(4):
-            src = wact_scales.bitcast(I32).rearrange("g (q r) e -> r q g e", r=4)[r]
-            nc.gpsimd.dma_start(wact_s[r:P:32, :, :], src)
         nc.scalar.activation(warm_out[:], warm[:], ACT.Sigmoid)
 
         def load_words(dst, words, a):
@@ -75,6 +68,8 @@ def tile_list_hopfield_episode_actions_kernel(
         load_scales(tab_s, tab_scales)
         load_words(tab_w[0], tab_words, 0)
         load_scales(tab2_s, tab2_scales)
+        nc.sync.dma_start(sharp_sb[:, :, 0:PACK], sharp.rearrange("(g p t) -> p g t", g=2, t=PACK))
+        nc.sync.dma_start(trust_sb[:, :, 0:PACK], trust.rearrange("(g p t) -> p g t", g=2, t=PACK))
         load_words(tab_w[1], tab_words, 1)
         load_words(tab2_w[0], tab2_words, 0)
 
@@ -119,9 +114,12 @@ def tile_list_hopfield_episode_actions_kernel(
 
         wg_raw = [
             reuse.tile([P, 2, PACK, N // 2], F32, name="wg_raw0", offset=0, align_bytes=64),
-            reuse.tile([P, 2, PACK, N // 2], F32, name="wg_raw1", offset=10 * KIB, align_bytes=64),
+            reuse.tile([P, 2, PACK, N // 2], F32, name="wg_raw1", offset=11 * KIB, align_bytes=64),
         ]
         wact_w = reuse.tile([P, 2, 2 * N // 4], I32, name="wact_w", offset=8 * KIB, align_bytes=64)
+
+        wact_s = reuse.tile([P, 2, N // 4], I32, name="wact_s", offset=10 * KIB, align_bytes=64)
+        nc.gpsimd.memset(wact_s[:], 0)
 
         def load_gate(h):
             for g in range(2):
@@ -130,6 +128,9 @@ def tile_list_hopfield_episode_actions_kernel(
 
         load_gate(0)
         nc.sync.dma_start(wact_w[:], wact_words.bitcast(I32).rearrange("g p e -> p g e"))
+        for r in range(4):
+            src = wact_scales.bitcast(I32).rearrange("g (q r) e -> r q g e", r=4)[r]
+            nc.sync.dma_start(wact_s[r:P:32, :, :], src)
         load_gate(1)
 
         def bank(b):

@@ -38,12 +38,10 @@ def tile_list_hopfield_episode_actions_kernel(
 
         idx = keep.tile([P, S // 16], U16, name="idx")
         idx2 = keep.tile([P, S2 // 16], U16, name="idx2")
-        tab_w = [
-            keep.tile([P, T], I32, name="tab_w0", align_bytes=64),
-            reuse.tile([P, T], I32, name="tab_w1", offset=7 * KIB, align_bytes=64),
-        ]
+        tab_w = [keep.tile([P, T], I32, name="tab_w0", align_bytes=64)]
         tab2_w = [
-            keep.tile([P, T2], I32, name="tab2_w0", align_bytes=64),
+            reuse.tile([P, T2], I32, name="tab2_w0", offset=0, align_bytes=64),
+            keep.tile([P, T2], I32, name="tab2_w1", align_bytes=64),
         ]
         tab_s = keep.tile([P, T // 4], I32, name="tab_s", align_bytes=64)
         tab2_s = keep.tile([P, T2 // 4], I32, name="tab2_s", align_bytes=64)
@@ -70,10 +68,10 @@ def tile_list_hopfield_episode_actions_kernel(
         load_scales(tab2_s, tab2_scales)
         nc.sync.dma_start(sharp_sb[:, :, 0:PACK], sharp.rearrange("(g p t) -> p g t", g=2, t=PACK))
         nc.sync.dma_start(trust_sb[:, :, 0:PACK], trust.rearrange("(g p t) -> p g t", g=2, t=PACK))
-        load_words(tab_w[1], tab_words, 1)
         load_words(tab2_w[0], tab2_words, 0)
+        load_words(tab2_w[1], tab2_words, 1)
 
-        v_s_list = reuse.tile([P, S], U8, name="v_s_list", offset=24 * KIB, align_bytes=64)
+        v_s_list = keep.tile([P, S], U8, name="v_s_list", align_bytes=64)
         v2_s_list = reuse.tile([P, S2], U8, name="v2_s_list", offset=40 * KIB, align_bytes=64)
         planes = keep.tile([P, S + S2], U8, name="planes", align_bytes=64)
         v2_w = [[keep.tile([P, JW], U32, name=f"v2_w{a}{jh}", align_bytes=64) for jh in range(2)] for a in range(2)]
@@ -92,10 +90,10 @@ def tile_list_hopfield_episode_actions_kernel(
                     planes[PLANE[a] + 8 * r : P : 32, :].bitcast(I32),
                 )
 
-        tab2_w.append(reuse.tile([P, T2], I32, name="tab2_w1", offset=24 * KIB, align_bytes=64))
-        load_words(tab2_w[1], tab2_words, 1)
+        tab_w.append(reuse.tile([P, T], I32, name="tab_w1", offset=32 * KIB + S2 // 2, align_bytes=64))
+        load_words(tab_w[1], tab_words, 1)
         v_w = [
-            reuse.tile([P, S], U32, name="v_w0", offset=40 * KIB, align_bytes=64),
+            reuse.tile([P, S], U32, name="v_w0", offset=40 * KIB + S2 // 2, align_bytes=64),
             keep.tile([P, S], U32, name="v_w1", align_bytes=64),
         ]
 
@@ -103,14 +101,18 @@ def tile_list_hopfield_episode_actions_kernel(
             probe_list = idx2[:, jh * JW // 16 : (jh + 1) * JW // 16]
             nc.vector.tensor_copy(v2_w[a][jh][:], tab2_w[a][:].bitcast(U32).indirect(probe_list))
 
-        for a in range(2):
-            nc.vector.tensor_copy(
-                v_w[a][:].rearrange("p (g t m) -> p g m t", g=2, t=PACK),
-                tab_w[a][:].bitcast(U32).indirect(idx[:]),
-            )
+        nc.vector.tensor_copy(
+            v_w[0][:].rearrange("p (g t m) -> p g m t", g=2, t=PACK),
+            tab_w[0][:].bitcast(U32).indirect(idx[:]),
+        )
         for a in range(2):
             for jh in range(2):
                 gather_probe_words(a, jh)
+        for g in range(2):
+            nc.vector.tensor_copy(
+                v_w[1][:, g * KP : (g + 1) * KP].rearrange("p (t m) -> p m t", t=PACK),
+                tab_w[1][:].bitcast(U32).indirect(idx[:, g * KP // 16 : (g + 1) * KP // 16]),
+            )
 
         wg_raw = [
             reuse.tile([P, 2, PACK, N // 2], F32, name="wg_raw0", offset=0, align_bytes=64),
@@ -245,6 +247,50 @@ def tile_list_hopfield_episode_actions_kernel(
                 )
             return y
 
+        def gate_of_pair(h, u, b):
+            c = bank(b)
+            cols = slice(u * HALF, (u + 1) * HALF)
+            for g in range(2):
+                for e in range(2):
+                    w_cols = slice((2 * g + e) * P, (2 * g + e + 1) * P)
+                    nc.tensor.matmul_mx(
+                        out=c[:, e * HALF : (e + 1) * HALF],
+                        lhsT=wg_w[h][:, w_cols].bitcast(FP8X4), lhsT_scale=wg_s[h][:, w_cols],
+                        rhs=h_w[g][1][:, cols].bitcast(FP8X4), rhs_scale=h_s[g][1][:, cols],
+                        start=(g == 0 and e == 0), stop=(g == 1 and e == 1),
+                    )
+            gate = work.tile([P, JW], F32, name="gate", bufs=8)
+            nc.scalar.activation(gate[:], c[:], ACT.Sigmoid)
+            return gate
+
+        def action_of_pair(h, u, b):
+            y = bank(b)
+            for g in range(2):
+                for e in range(2):
+                    nb = 2 * h + e
+                    for q in range(2):
+                        cols = slice(u * HALF + q * P, u * HALF + (q + 1) * P)
+                        nc.tensor.matmul_mx(
+                            out=y[:, e * HALF + q * P : e * HALF + (q + 1) * P],
+                            lhsT=wact_w[:, g, :].bitcast(U8)[:, 2 * nb * P : 2 * (nb + 1) * P].bitcast(FP4X4),
+                            lhsT_scale=wact_s[:, g, :].bitcast(U8)[:, nb * P : (nb + 1) * P],
+                            rhs=h_w[g][1][:, cols].bitcast(FP8X4), rhs_scale=h_s[g][1][:, cols],
+                            start=(g == 0 and e == 0 and q == 0), stop=(g == 1 and e == 1 and q == 1),
+                        )
+            return y
+
+        def finish_pair(y, gate, h, u, pieces=1):
+            blocks = 2 // pieces
+            for q in range(pieces):
+                cols = slice(q * blocks * HALF, (q + 1) * blocks * HALF)
+                res = work.tile([P, blocks * HALF], F32, name="res", bufs=8)
+                nc.vector.tensor_tensor(res[:], y[:, cols], gate[:, cols], ALU.mult)
+                row = (2 * h + q * blocks) * P
+                dst = out[row : row + blocks * P, JW + u * HALF : JW + (u + 1) * HALF]
+                nc.sync.dma_start(
+                    dst.rearrange("(e p) c -> p e c", p=P), res[:].rearrange("p (e c) -> p e c", e=blocks)
+                )
+
         def finish(y, gate, nb, jh, pieces=1):
             width = JW // pieces
             for q in range(pieces):
@@ -280,15 +326,23 @@ def tile_list_hopfield_episode_actions_kernel(
             weigh(th01, hb01, 0, u)
         quantize_gate(1)
         quantize(hb01, 0, 1, 0, 2)
-        for nb in range(2):
-            finish(early[nb][1], early[nb][0], nb, 0)
-        late = [project(2 + nb, 0, 2 * nb) for nb in range(2)]
-        weigh_and_quantize(th11, 1, 1)
-        for nb in range(2):
-            finish(late[nb][1], late[nb][0], 2 + nb, 0)
-        for nb in range(2):
-            gate, y = project(nb, 1, 4 + 2 * nb)
-            finish(y, gate, nb, 1)
-        gates = [gate_of(2 + nb, 1, 2 * nb) for nb in range(2)]
-        for nb in range(2):
-            finish(action_of(2 + nb, 1, 2 * nb + 1), gates[nb], 2 + nb, 1, pieces=1 + nb)
+        hb11 = rounded()
+        late_acts = [action_of(2 + nb, 0, 2 * nb) for nb in range(2)]
+        finish(early[0][1], early[0][0], 0, 0)
+        late_gates = [gate_of(2, 0, 1)]
+        weigh(th11, hb11, 1, 0)
+        finish(early[1][1], early[1][0], 1, 0)
+        late_gates.append(gate_of(3, 0, 3))
+        quantize(hb11, 1, 1, 0, 1)
+        gates0 = [gate_of_pair(h, 0, 4 + h) for h in range(2)]
+        acts0 = [action_of_pair(h, 0, 6 + h) for h in range(2)]
+        weigh(th11, hb11, 1, 1)
+        finish(late_acts[0], late_gates[0], 2, 0)
+        quantize(hb11, 1, 1, 1, 2)
+        gates1 = [gate_of_pair(h, 1, 2 * h + 1) for h in range(2)]
+        finish(late_acts[1], late_gates[1], 3, 0)
+        acts1 = [action_of_pair(h, 1, 2 * h) for h in range(2)]
+        for h in range(2):
+            finish_pair(acts0[h], gates0[h], h, 0)
+        for h in range(2):
+            finish_pair(acts1[h], gates1[h], h, 1, pieces=1 + h)

@@ -45,8 +45,6 @@ def tile_list_hopfield_episode_actions_kernel(
         ]
         tab_s = keep.tile([P, T // 4], I32, name="tab_s", align_bytes=64)
         tab2_s = keep.tile([P, T2 // 4], I32, name="tab2_s", align_bytes=64)
-        sharp_sb = keep.tile([P, 2, 8], F32, name="sharp_sb")
-        trust_sb = keep.tile([P, 2, 8], F32, name="trust_sb")
         warm = keep.tile([P, 8], F32, name="warm")
         warm_out = keep.tile([P, 8], F32, name="warm_out")
 
@@ -66,8 +64,6 @@ def tile_list_hopfield_episode_actions_kernel(
         load_scales(tab_s, tab_scales)
         load_words(tab_w[0], tab_words, 0)
         load_scales(tab2_s, tab2_scales)
-        nc.sync.dma_start(sharp_sb[:, :, 0:PACK], sharp.rearrange("(g p t) -> p g t", g=2, t=PACK))
-        nc.sync.dma_start(trust_sb[:, :, 0:PACK], trust.rearrange("(g p t) -> p g t", g=2, t=PACK))
         load_words(tab2_w[0], tab2_words, 0)
         load_words(tab2_w[1], tab2_words, 1)
 
@@ -92,8 +88,10 @@ def tile_list_hopfield_episode_actions_kernel(
 
         tab_w.append(reuse.tile([P, T], I32, name="tab_w1", offset=32 * KIB + S2 // 2, align_bytes=64))
         load_words(tab_w[1], tab_words, 1)
+        sharp_sb = reuse.tile([P, 2, 8], F32, name="sharp_sb", offset=40 * KIB + S2 // 2, align_bytes=64)
+        nc.sync.dma_start(sharp_sb[:, :, 0:PACK], sharp.rearrange("(g p t) -> p g t", g=2, t=PACK))
         v_w = [
-            reuse.tile([P, S], U32, name="v_w0", offset=40 * KIB + S2 // 2, align_bytes=64),
+            reuse.tile([P, S], U32, name="v_w0", offset=40 * KIB + 3 * S2 // 4, align_bytes=64),
             keep.tile([P, S], U32, name="v_w1", align_bytes=64),
         ]
 
@@ -116,7 +114,7 @@ def tile_list_hopfield_episode_actions_kernel(
 
         wg_raw = [
             reuse.tile([P, 2, PACK, N // 2], F32, name="wg_raw0", offset=0, align_bytes=64),
-            reuse.tile([P, 2, PACK, N // 2], F32, name="wg_raw1", offset=11 * KIB, align_bytes=64),
+            reuse.tile([P, 2, PACK, N // 2], F32, name="wg_raw1", offset=12 * KIB, align_bytes=64),
         ]
         wact_w = reuse.tile([P, 2, 2 * N // 4], I32, name="wact_w", offset=8 * KIB, align_bytes=64)
 
@@ -129,6 +127,8 @@ def tile_list_hopfield_episode_actions_kernel(
                 nc.sync.dma_start(wg_raw[h][:, g, :, :], src.rearrange("(p t) n -> p t n", t=PACK))
 
         load_gate(0)
+        trust_sb = reuse.tile([P, 2, 8], F32, name="trust_sb", offset=11 * KIB, align_bytes=64)
+        nc.sync.dma_start(trust_sb[:, :, 0:PACK], trust.rearrange("(g p t) -> p g t", g=2, t=PACK))
         nc.sync.dma_start(wact_w[:], wact_words.bitcast(I32).rearrange("g p e -> p g e"))
         for r in range(4):
             src = wact_scales.bitcast(I32).rearrange("g (q r) e -> r q g e", r=4)[r]

@@ -53,16 +53,17 @@ def tile_list_hopfield_episode_actions_kernel(
         nc.vector.memset(warm[:], 0.0)
         nc.scalar.activation(warm_out[:], warm[:], ACT.Sigmoid)
 
-        def load_words(dst, words, a):
-            nc.sync.dma_start(dst[:], words[a].rearrange("p t i -> p (t i)").bitcast(I32))
+        def load_words(dst, words, a, cols=slice(None)):
+            nc.sync.dma_start(dst[:, cols], words[a].rearrange("p t i -> p (t i)").bitcast(I32)[:, cols])
 
         def load_scales(dst, scales):
             nc.sync.dma_start(dst[0:P:4, :], scales.bitcast(I32).rearrange("a q n -> q a n"))
 
         nc.sync.dma_start(idx[:], offs)
         nc.sync.dma_start(idx2[:], offs2)
+        load_words(tab_w[0], tab_words, 0, slice(0, T // 4))
         load_scales(tab_s, tab_scales)
-        load_words(tab_w[0], tab_words, 0)
+        load_words(tab_w[0], tab_words, 0, slice(T // 4, T))
         load_scales(tab2_s, tab2_scales)
         load_words(tab2_w[0], tab2_words, 0)
         load_words(tab2_w[1], tab2_words, 1)
@@ -79,8 +80,8 @@ def tile_list_hopfield_episode_actions_kernel(
             planes[:, 0:S].rearrange("p (g t m) -> p g t m", g=2, t=PACK),
             v_s_list[:].rearrange("p (g m t) -> p g t m", g=2, t=PACK),
         )
-        for a in range(2):
-            for r in range(1, 4):
+        for r in range(1, 4):
+            for a in range(2):
                 nc.sync.dma_start(
                     planes[PLANE[a] + r : P : 32, :].bitcast(I32),
                     planes[PLANE[a] + 8 * r : P : 32, :].bitcast(I32),
@@ -307,7 +308,10 @@ def tile_list_hopfield_episode_actions_kernel(
                     sim_pass(first[g][t], a, g, t, 0)
         th00 = separate_halves(first[0], 0)
         th10 = separate_whole(first[1], 1)
-        nc.vector.tensor_copy(gate_out(wg_bf[0][:]), gate_in(wg_raw[0][:]))
+        for g in range(2):
+            nc.vector.tensor_copy(
+                pairs_out(wg_bf[0][:, g * HALF * PACK : (g + 1) * HALF * PACK]), pairs_in(wg_raw[0][:, g, :, :])
+            )
         weigh_and_quantize(th00, 0, 0)
         th01 = separate_whole(similarity(0, 1), 0)
         quantize_gate(0)

@@ -1,6 +1,7 @@
 from contextlib import ExitStack
 
 import concourse.mybir as mybir
+from concourse.masks import make_identity
 
 K, T, S, T2, S2, N = 1024, 2048, 1024, 4096, 1024, 512
 FLOPS = 2 * K * S * S2 + 2 * 2 * S * N * S2
@@ -48,7 +49,12 @@ def tile_list_hopfield_episode_actions_kernel(
         warm = keep.tile([P, 8], F32, name="warm")
         warm_out = keep.tile([P, 8], F32, name="warm_out")
 
+        rows = keep.tile([P, KP], F32, name="rows", align_bytes=64)
+        ident = keep.tile([P, P], F32, name="ident", align_bytes=64)
+
         nc.gpsimd.memset(tab_s[:], 0)
+        nc.gpsimd.memset(rows[:], 0.0)
+        make_identity(nc, ident[:])
         nc.vector.memset(tab2_s[:], 0)
         nc.vector.memset(warm[:], 0.0)
         nc.scalar.activation(warm_out[:], warm[:], ACT.Sigmoid)
@@ -65,8 +71,16 @@ def tile_list_hopfield_episode_actions_kernel(
         load_scales(tab_s, tab_scales)
         load_words(tab_w[0], tab_words, 0, slice(T // 4, T))
         load_scales(tab2_s, tab2_scales)
+        nc.sync.dma_start(rows[0:2, :], trust.rearrange("(g m) -> g m", g=2))
+        nc.sync.dma_start(rows[2:4, :], sharp.rearrange("(g m) -> g m", g=2))
         load_words(tab2_w[0], tab2_words, 0)
         load_words(tab2_w[1], tab2_words, 1)
+
+        turned = psum.tile([P, KP], F32, name="turned")
+        for t in range(PACK):
+            nc.tensor.transpose(turned[:, t * P : (t + 1) * P], rows[:, t:KP:PACK], ident[:])
+        sharp_sb = keep.tile([P, 2, 8], F32, name="sharp_sb", align_bytes=64)
+        nc.scalar.copy(sharp_sb[:, :, 0:PACK], turned[:].rearrange("p (t k) -> p k t", t=PACK)[:, 2:4, :])
 
         v_s_list = keep.tile([P, S], U8, name="v_s_list", align_bytes=64)
         v2_s_list = reuse.tile([P, S2], U8, name="v2_s_list", offset=40 * KIB, align_bytes=64)
@@ -89,8 +103,6 @@ def tile_list_hopfield_episode_actions_kernel(
 
         tab_w.append(reuse.tile([P, T], I32, name="tab_w1", offset=32 * KIB + S2 // 2, align_bytes=64))
         load_words(tab_w[1], tab_words, 1)
-        sharp_sb = reuse.tile([P, 2, 8], F32, name="sharp_sb", offset=40 * KIB + S2 // 2, align_bytes=64)
-        nc.sync.dma_start(sharp_sb[:, :, 0:PACK], sharp.rearrange("(g p t) -> p g t", g=2, t=PACK))
         v_w = [
             reuse.tile([P, S], U32, name="v_w0", offset=40 * KIB + 3 * S2 // 4, align_bytes=64),
             keep.tile([P, S], U32, name="v_w1", align_bytes=64),
@@ -113,28 +125,25 @@ def tile_list_hopfield_episode_actions_kernel(
                 tab_w[1][:].bitcast(U32).indirect(idx[:, g * KP // 16 : (g + 1) * KP // 16]),
             )
 
-        wg_raw = [
-            reuse.tile([P, 2, PACK, N // 2], F32, name="wg_raw0", offset=0, align_bytes=64),
-            reuse.tile([P, 2, PACK, N // 2], F32, name="wg_raw1", offset=12 * KIB, align_bytes=64),
-        ]
+        raw0 = [reuse.tile([P, PACK, HALF], F32, name=f"raw0{g}", offset=4 * g * KIB, align_bytes=64) for g in range(2)]
+        raw1 = reuse.tile([P, 2, PACK, HALF], F32, name="raw1", offset=12 * KIB, align_bytes=64)
         wact_w = reuse.tile([P, 2, 2 * N // 4], I32, name="wact_w", offset=8 * KIB, align_bytes=64)
-
         wact_s = reuse.tile([P, 2, N // 4], I32, name="wact_s", offset=10 * KIB, align_bytes=64)
         nc.gpsimd.memset(wact_s[:], 0)
+        raw = [[raw0[0][:], raw0[1][:]], [raw1[:, 0, :, :], raw1[:, 1, :, :]]]
 
-        def load_gate(h):
-            for g in range(2):
-                src = wgate[g * KP : (g + 1) * KP, h * N // 2 : (h + 1) * N // 2]
-                nc.sync.dma_start(wg_raw[h][:, g, :, :], src.rearrange("(p t) n -> p t n", t=PACK))
+        def load_gate(h, g):
+            src = wgate[g * KP : (g + 1) * KP, h * HALF : (h + 1) * HALF]
+            nc.sync.dma_start(raw[h][g], src.rearrange("(p t) n -> p t n", t=PACK))
 
-        load_gate(0)
-        trust_sb = reuse.tile([P, 2, 8], F32, name="trust_sb", offset=11 * KIB, align_bytes=64)
-        nc.sync.dma_start(trust_sb[:, :, 0:PACK], trust.rearrange("(g p t) -> p g t", g=2, t=PACK))
+        load_gate(0, 0)
+        load_gate(0, 1)
+        load_gate(1, 0)
         nc.sync.dma_start(wact_w[:], wact_words.bitcast(I32).rearrange("g p e -> p g e"))
         for r in range(4):
             src = wact_scales.bitcast(I32).rearrange("g (q r) e -> r q g e", r=4)[r]
             nc.sync.dma_start(wact_s[r:P:32, :, :], src)
-        load_gate(1)
+        load_gate(1, 1)
 
         def bank(b):
             return psum.tile([P, JW], F32, name=f"bank{b}")
@@ -151,35 +160,21 @@ def tile_list_hopfield_episode_actions_kernel(
                 stop=(a == 1),
             )
 
+        def placed(name, shape, dtype, kib):
+            return reuse.tile(shape, dtype, name=name, offset=kib * KIB, align_bytes=64)
+
         h_w = [[keep.tile([P, JW], U32, name=f"h_w{g}{jh}", align_bytes=64) for jh in range(2)] for g in range(2)]
         h_s = [[keep.tile([P, JW], U8, name=f"h_s{g}{jh}", align_bytes=64) for jh in range(2)] for g in range(2)]
-        wg_bf = [keep.tile([P, N * PACK], BF16, name="wg_bf0", align_bytes=64)]
-        wg_w = [keep.tile([P, N], U32, name=f"wg_w{g}", align_bytes=64) for g in range(2)]
-        wg_s = [keep.tile([P, N], U8, name=f"wg_s{g}", align_bytes=64) for g in range(2)]
+        wg_s = [keep.tile([P, N], U8, name=f"wg_s{h}", align_bytes=64) for h in range(2)]
 
-        def pairs_out(ap):
+        def walk_out(ap):
             return ap.rearrange("p (c i t) -> p c t i", i=4, t=PACK)
 
-        def pairs_in(ap):
+        def walk_in(ap):
             return ap.rearrange("p t (c i) -> p c t i", i=4)
 
-        def gate_out(ap):
-            return ap.rearrange("p (g c i t) -> p g c t i", g=2, i=4, t=PACK)
-
-        def gate_in(ap):
-            return ap.rearrange("p g t (c i) -> p g c t i", i=4)
-
-        def separate_whole(accs, g):
-            th = work.tile([P, 2, PACK, HALF], F32, name="th", bufs=3, align_bytes=64)
-            for t in range(PACK):
-                nc.scalar.activation(
-                    th[:, :, t, :], accs[t][:].rearrange("p (u c) -> p u c", u=2), ACT.Tanh,
-                    scale=sharp_sb[:, g, t : t + 1],
-                )
-            return th
-
-        def separate_halves(accs, g):
-            th = work.tile([P, 2, PACK, HALF], F32, name="th", bufs=3, align_bytes=64)
+        def separate_halves(name, accs, g):
+            th = keep.tile([P, 2, PACK, HALF], F32, name=name, align_bytes=64)
             for u in range(2):
                 for t in range(PACK):
                     nc.scalar.activation(
@@ -188,54 +183,49 @@ def tile_list_hopfield_episode_actions_kernel(
                     )
             return th
 
-        def weigh(th, hb, g, u):
-            factor = trust_sb[:, g, 0:PACK].unsqueeze(1).unsqueeze(3).to_broadcast([P, HALF // 4, PACK, 4])
-            nc.vector.tensor_tensor(
-                pairs_out(hb[:, u * HALF * PACK : (u + 1) * HALF * PACK]), pairs_in(th[:, u, :, :]), factor, ALU.mult,
-            )
+        def weigh(dst, th, g):
+            width = th.shape[2]
+            factor = turned[:, g:KP:P].unsqueeze(1).unsqueeze(3).to_broadcast([P, width // 4, PACK, 4])
+            nc.vector.tensor_tensor(walk_out(dst), walk_in(th), factor, ALU.mult)
 
-        def quantize(hb, g, jh, first, last):
+        def quantize(src, g, jh, first, last):
             cols = slice(first * HALF, last * HALF)
-            nc.vector.quantize_mx(
-                out=h_w[g][jh][:, cols].bitcast(FP8X4),
-                scales=h_s[g][jh][:, cols],
-                in_=hb[:, first * HALF * PACK : last * HALF * PACK],
+            nc.vector.quantize_mx(out=h_w[g][jh][:, cols].bitcast(FP8X4), scales=h_s[g][jh][:, cols], in_=src)
+
+        def round_gate_on_gpsimd(dst, h, g):
+            nc.gpsimd.tensor_scalar(
+                dst[:].rearrange("p (c t) -> p c t", t=PACK), raw[h][g].rearrange("p t c -> p c t"),
+                1.0, 0.0, ALU.mult, ALU.add,
             )
 
-        def rounded():
-            return work.tile([P, JW * PACK], BF16, name="hb", align_bytes=64, bufs=3)
+        def quantize_gate(codes, src, h, g):
+            cols = slice(g * HALF, (g + 1) * HALF)
+            nc.vector.quantize_mx(out=codes[:, cols].bitcast(FP8X4), scales=wg_s[h][:, cols], in_=src[:])
 
-        def weigh_and_quantize(th, g, jh):
-            hb = rounded()
-            for u in range(2):
-                weigh(th, hb, g, u)
-            for u in range(2):
-                quantize(hb, g, jh, u, u + 1)
-
-        def quantize_gate(g):
-            nc.vector.quantize_mx(out=wg_w[g][:].bitcast(FP8X4), scales=wg_s[g][:], in_=wg_bf[g][:])
-
-        def similarity(g, jh):
-            accs = [bank(PACK * g + t) for t in range(PACK)]
+        def similarity(g, jh, banks):
+            accs = [bank(b) for b in banks]
             for t in range(PACK):
                 sim_pass(accs[t], 0, g, t, jh)
                 sim_pass(accs[t], 1, g, t, jh)
             return accs
 
-        def gate_of(nb, jh, b):
+        def gate_sum(nb, b):
             c = bank(b)
             for g in range(2):
                 cols = slice((2 * g + nb % 2) * P, (2 * g + nb % 2 + 1) * P)
                 nc.tensor.matmul_mx(
                     out=c[:], lhsT=wg_w[nb // 2][:, cols].bitcast(FP8X4), lhsT_scale=wg_s[nb // 2][:, cols],
-                    rhs=h_w[g][jh][:].bitcast(FP8X4), rhs_scale=h_s[g][jh][:],
+                    rhs=h_w[g][0][:].bitcast(FP8X4), rhs_scale=h_s[g][0][:],
                     start=(g == 0), stop=(g == 1),
                 )
+            return c
+
+        def opened(c):
             gate = work.tile([P, JW], F32, name="gate", bufs=8)
             nc.scalar.activation(gate[:], c[:], ACT.Sigmoid)
             return gate
 
-        def action_of(nb, jh, b):
+        def action_of(nb, b):
             cols = slice(nb * P, (nb + 1) * P)
             y = bank(b)
             for g in range(2):
@@ -243,7 +233,7 @@ def tile_list_hopfield_episode_actions_kernel(
                     out=y[:],
                     lhsT=wact_w[:, g, :].bitcast(U8)[:, 2 * nb * P : 2 * (nb + 1) * P].bitcast(FP4X4),
                     lhsT_scale=wact_s[:, g, :].bitcast(U8)[:, cols],
-                    rhs=h_w[g][jh][:].bitcast(FP8X4), rhs_scale=h_s[g][jh][:],
+                    rhs=h_w[g][0][:].bitcast(FP8X4), rhs_scale=h_s[g][0][:],
                     start=(g == 0), stop=(g == 1),
                 )
             return y
@@ -260,9 +250,7 @@ def tile_list_hopfield_episode_actions_kernel(
                         rhs=h_w[g][1][:, cols].bitcast(FP8X4), rhs_scale=h_s[g][1][:, cols],
                         start=(g == 0 and e == 0), stop=(g == 1 and e == 1),
                     )
-            gate = work.tile([P, JW], F32, name="gate", bufs=8)
-            nc.scalar.activation(gate[:], c[:], ACT.Sigmoid)
-            return gate
+            return opened(c)
 
         def action_of_pair(h, u, b):
             y = bank(b)
@@ -292,60 +280,96 @@ def tile_list_hopfield_episode_actions_kernel(
                     dst.rearrange("(e p) c -> p e c", p=P), res[:].rearrange("p (e c) -> p e c", e=blocks)
                 )
 
-        def finish(y, gate, nb, jh, pieces=1):
-            width = JW // pieces
-            for q in range(pieces):
-                cols = slice(q * width, (q + 1) * width)
-                res = work.tile([P, width], F32, name="res", bufs=8)
-                nc.vector.tensor_tensor(res[:], y[:, cols], gate[:, cols], ALU.mult)
-                start = jh * JW + q * width
-                nc.sync.dma_start(out[nb * P : (nb + 1) * P, start : start + width], res[:])
+        def finish(y, gate, nb):
+            res = work.tile([P, JW], F32, name="res", bufs=8)
+            nc.vector.tensor_tensor(res[:], y[:], gate[:], ALU.mult)
+            nc.sync.dma_start(out[nb * P : (nb + 1) * P, 0:JW], res[:])
 
-        first = [[bank(PACK * g + t) for t in range(PACK)] for g in range(2)]
+        def staged(y):
+            y_sb = work.tile([P, JW], F32, name="y_sb", bufs=2)
+            nc.scalar.copy(y_sb[:], y[:])
+            return y_sb
+
+        def finish_on_gpsimd(res, y_sb, gate, nb):
+            nc.gpsimd.tensor_tensor(res[:], y_sb[:], gate[:], ALU.mult)
+            nc.sync.dma_start(out[nb * P : (nb + 1) * P, 0:JW], res[:])
+
+        QUARTER = HALF * PACK
+        early = [(0, t) for t in range(PACK)] + [(1, t) for t in range(PACK - 1)]
+        first = [bank(b) for b in range(len(early))]
         for a in range(2):
-            for g in range(2):
-                for t in range(PACK):
-                    sim_pass(first[g][t], a, g, t, 0)
-        th00 = separate_halves(first[0], 0)
-        th10 = separate_whole(first[1], 1)
-        for g in range(2):
-            nc.vector.tensor_copy(
-                pairs_out(wg_bf[0][:, g * HALF * PACK : (g + 1) * HALF * PACK]), pairs_in(wg_raw[0][:, g, :, :])
-            )
-        weigh_and_quantize(th00, 0, 0)
-        th01 = separate_whole(similarity(0, 1), 0)
-        quantize_gate(0)
-        weigh_and_quantize(th10, 1, 0)
-        sims11 = similarity(1, 1)
-        wg_bf.append(work.tile([P, N * PACK], BF16, name="th", bufs=3, align_bytes=64))
-        nc.scalar.copy(gate_out(wg_bf[1][:]), gate_in(wg_raw[1][:]))
+            for b, (g, t) in enumerate(early):
+                sim_pass(first[b], a, g, t, 0)
+        th00 = separate_halves("th00", first[0:PACK], 0)
+        last = bank(0)
+        for a in range(2):
+            sim_pass(last, a, 1, PACK - 1, 0)
+        th10 = separate_halves("th10", first[PACK:] + [last], 1)
 
-        def project(nb, jh, b):
-            return gate_of(nb, jh, b), action_of(nb, jh, b + 1)
+        bf00 = keep.tile([P, QUARTER], BF16, name="bf00", align_bytes=64)
+        nc.vector.tensor_copy(walk_out(bf00[:]), walk_in(raw[0][0]))
+        bf01 = placed("bf01", [P, QUARTER], BF16, 0)
+        round_gate_on_gpsimd(bf01, 0, 1)
 
-        early = [project(nb, 0, 2 * nb) for nb in range(2)]
-        th11 = separate_halves(sims11, 1)
-        hb01 = rounded()
+        hb00 = placed("hb00", [P, 2 * QUARTER], BF16, 48)
         for u in range(2):
-            weigh(th01, hb01, 0, u)
-        quantize_gate(1)
-        quantize(hb01, 0, 1, 0, 2)
-        hb11 = rounded()
-        late_acts = [action_of(2 + nb, 0, 2 * nb) for nb in range(2)]
-        finish(early[0][1], early[0][0], 0, 0)
-        late_gates = [gate_of(2, 0, 1)]
-        weigh(th11, hb11, 1, 0)
-        finish(early[1][1], early[1][0], 1, 0)
-        late_gates.append(gate_of(3, 0, 3))
-        quantize(hb11, 1, 1, 0, 1)
-        gates0 = [gate_of_pair(h, 0, 4 + h) for h in range(2)]
-        acts0 = [action_of_pair(h, 0, 6 + h) for h in range(2)]
-        weigh(th11, hb11, 1, 1)
-        finish(late_acts[0], late_gates[0], 2, 0)
-        quantize(hb11, 1, 1, 1, 2)
-        gates1 = [gate_of_pair(h, 1, 2 * h + 1) for h in range(2)]
-        finish(late_acts[1], late_gates[1], 3, 0)
-        acts1 = [action_of_pair(h, 1, 2 * h) for h in range(2)]
+            weigh(hb00[:, u * QUARTER : (u + 1) * QUARTER], th00[:, u, :, :], 0)
+        for u in range(2):
+            quantize(hb00[:, u * QUARTER : (u + 1) * QUARTER], 0, 0, u, u + 1)
+        bf10 = placed("bf10", [P, QUARTER], BF16, 48)
+        round_gate_on_gpsimd(bf10, 1, 0)
+        wg_w = [placed("wg_w0", [P, N], U32, 50), keep.tile([P, N], U32, name="wg_w1", align_bytes=64)]
+
+        sims = similarity(0, 1, (1, 2, 3, 4))
+        th01 = keep.tile([P, PACK, JW], F32, name="th01", align_bytes=64)
+        for t in range(PACK):
+            nc.scalar.activation(th01[:, t, :], sims[t][:], ACT.Tanh, scale=sharp_sb[:, 0, t : t + 1])
+
+        hb10 = placed("hb10", [P, 2 * QUARTER], BF16, 52)
+        for u in range(2):
+            weigh(hb10[:, u * QUARTER : (u + 1) * QUARTER], th10[:, u, :, :], 1)
+        quantize_gate(wg_w[0], bf00, 0, 0)
+        quantize_gate(wg_w[0], bf01, 0, 1)
+        quantize(hb10[:], 1, 0, 0, 2)
+        bf11 = placed("bf11", [P, QUARTER], BF16, 52)
+        round_gate_on_gpsimd(bf11, 1, 1)
+
+        sims = similarity(1, 1, (5, 6, 0, 1))
+        th11 = keep.tile([P, 2, PACK, HALF], F32, name="th11", align_bytes=64)
+        for t in range(PACK):
+            nc.scalar.activation(
+                th11[:, :, t, :], sims[t][:].rearrange("p (u c) -> p u c", u=2), ACT.Tanh,
+                scale=sharp_sb[:, 1, t : t + 1],
+            )
+
+        c0, y0 = gate_sum(0, 2), action_of(0, 3)
+        c1, y1 = gate_sum(1, 4), action_of(1, 5)
+        hb01 = placed("hb01", [P, 2 * QUARTER], BF16, 56)
+        weigh(hb01[:], th01[:], 0)
+        quantize_gate(wg_w[1], bf10, 1, 0)
+        quantize_gate(wg_w[1], bf11, 1, 1)
+        quantize(hb01[:], 0, 1, 0, 2)
+        gate0 = opened(c0)
+        finish_on_gpsimd(placed("res0", [P, JW], F32, 56), staged(y0), gate0, 0)
+        c2, y2, y3 = gate_sum(2, 6), action_of(2, 0), action_of(3, 1)
+        c3 = gate_sum(3, 2)
+        gate2 = opened(c2)
+        gate1 = opened(c1)
+        y1_sb = staged(y1)
+        gate3 = opened(c3)
+
+        hb11 = [placed(f"hb11{u}", [P, QUARTER], BF16, 60 + 2 * u) for u in range(2)]
+        weigh(hb11[0][:], th11[:, 0, :, :], 1)
+        finish(y2, gate2, 2)
+        quantize(hb11[0][:], 1, 1, 0, 1)
+        finish_on_gpsimd(placed("res1", [P, JW], F32, 60), y1_sb, gate1, 1)
+        gates0 = [gate_of_pair(0, 0, 3), gate_of_pair(1, 0, 6)]
+        acts0 = [action_of_pair(0, 0, 4), action_of_pair(1, 0, 5)]
+        weigh(hb11[1][:], th11[:, 1, :, :], 1)
+        finish(y3, gate3, 3)
+        quantize(hb11[1][:], 1, 1, 1, 2)
+        gates1 = [gate_of_pair(0, 1, 0), gate_of_pair(1, 1, 2)]
+        acts1 = [action_of_pair(0, 1, 3), action_of_pair(1, 1, 1)]
         for h in range(2):
             finish_pair(acts0[h], gates0[h], h, 0)
         for h in range(2):

@@ -22,7 +22,6 @@ PACK = 4
 KP = P * PACK
 JW = 512
 HALF = JW // 2
-PLANE = (0, 4)
 KIB = 1024
 
 
@@ -55,6 +54,8 @@ def tile_list_hopfield_episode_actions_kernel(
         nc.gpsimd.memset(tab_s[:], 0)
         nc.gpsimd.memset(rows[:], 0.0)
         make_identity(nc, ident[:])
+        late_plane = keep.tile([P, (S + S2) // 4], I32, name="late_plane", align_bytes=64)
+        nc.gpsimd.memset(late_plane[:], 0)
         nc.vector.memset(tab2_s[:], 0)
         nc.vector.memset(warm[:], 0.0)
         nc.scalar.activation(warm_out[:], warm[:], ACT.Sigmoid)
@@ -95,14 +96,13 @@ def tile_list_hopfield_episode_actions_kernel(
             v_s_list[:].rearrange("p (g m t) -> p g t m", g=2, t=PACK),
         )
         for r in range(1, 4):
-            for a in range(2):
-                nc.sync.dma_start(
-                    planes[PLANE[a] + r : P : 32, :].bitcast(I32),
-                    planes[PLANE[a] + 8 * r : P : 32, :].bitcast(I32),
-                )
+            nc.sync.dma_start(planes[r:P:32, :].bitcast(I32), planes[8 * r : P : 32, :].bitcast(I32))
 
         tab_w.append(reuse.tile([P, T], I32, name="tab_w1", offset=32 * KIB + S2 // 2, align_bytes=64))
         load_words(tab_w[1], tab_words, 1)
+        for r in range(4):
+            nc.sync.dma_start(late_plane[r:P:32, :], planes[8 * r + 4 : P : 32, :].bitcast(I32))
+        plane = [planes[:], late_plane[:].bitcast(U8)]
         v_w = [
             reuse.tile([P, S], U32, name="v_w0", offset=40 * KIB + 3 * S2 // 4, align_bytes=64),
             keep.tile([P, S], U32, name="v_w1", align_bytes=64),
@@ -139,11 +139,11 @@ def tile_list_hopfield_episode_actions_kernel(
         load_gate(0, 0)
         load_gate(0, 1)
         load_gate(1, 0)
+        load_gate(1, 1)
         nc.sync.dma_start(wact_w[:], wact_words.bitcast(I32).rearrange("g p e -> p g e"))
         for r in range(4):
             src = wact_scales.bitcast(I32).rearrange("g (q r) e -> r q g e", r=4)[r]
             nc.sync.dma_start(wact_s[r:P:32, :, :], src)
-        load_gate(1, 1)
 
         def bank(b):
             return psum.tile([P, JW], F32, name=f"bank{b}")
@@ -153,9 +153,9 @@ def tile_list_hopfield_episode_actions_kernel(
             nc.tensor.matmul_mx(
                 out=acc[:],
                 lhsT=v_w[a][:, cols].bitcast(FP8X4),
-                lhsT_scale=planes[PLANE[a] :, cols],
+                lhsT_scale=plane[a][:, cols],
                 rhs=v2_w[a][jh][:].bitcast(FP8X4),
-                rhs_scale=planes[PLANE[a] :, S + jh * JW : S + (jh + 1) * JW],
+                rhs_scale=plane[a][:, S + jh * JW : S + (jh + 1) * JW],
                 start=(a == 0),
                 stop=(a == 1),
             )
@@ -198,6 +198,17 @@ def tile_list_hopfield_episode_actions_kernel(
                 1.0, 0.0, ALU.mult, ALU.add,
             )
 
+        def round_block_on_gpsimd(dst, e):
+            nc.gpsimd.tensor_scalar(
+                dst[:].rearrange("p (g c t) -> p g c t", g=2, t=PACK),
+                raw1[:, :, :, e * P : (e + 1) * P].rearrange("p g t c -> p g c t"),
+                1.0, 0.0, ALU.mult, ALU.add,
+            )
+
+        def gate_cols(nb, g):
+            piece = 2 * g + nb if nb < 2 else 2 * (nb - 2) + g
+            return slice(piece * P, (piece + 1) * P)
+
         def quantize_gate(codes, src, h, g):
             cols = slice(g * HALF, (g + 1) * HALF)
             nc.vector.quantize_mx(out=codes[:, cols].bitcast(FP8X4), scales=wg_s[h][:, cols], in_=src[:])
@@ -212,7 +223,7 @@ def tile_list_hopfield_episode_actions_kernel(
         def gate_sum(nb, b):
             c = bank(b)
             for g in range(2):
-                cols = slice((2 * g + nb % 2) * P, (2 * g + nb % 2 + 1) * P)
+                cols = gate_cols(nb, g)
                 nc.tensor.matmul_mx(
                     out=c[:], lhsT=wg_w[nb // 2][:, cols].bitcast(FP8X4), lhsT_scale=wg_s[nb // 2][:, cols],
                     rhs=h_w[g][0][:].bitcast(FP8X4), rhs_scale=h_s[g][0][:],
@@ -221,7 +232,7 @@ def tile_list_hopfield_episode_actions_kernel(
             return c
 
         def opened(c):
-            gate = work.tile([P, JW], F32, name="gate", bufs=8)
+            gate = work.tile([P, JW], F32, name="gate", bufs=10)
             nc.scalar.activation(gate[:], c[:], ACT.Sigmoid)
             return gate
 
@@ -243,14 +254,14 @@ def tile_list_hopfield_episode_actions_kernel(
             cols = slice(u * HALF, (u + 1) * HALF)
             for g in range(2):
                 for e in range(2):
-                    w_cols = slice((2 * g + e) * P, (2 * g + e + 1) * P)
+                    w_cols = gate_cols(2 * h + e, g)
                     nc.tensor.matmul_mx(
                         out=c[:, e * HALF : (e + 1) * HALF],
                         lhsT=wg_w[h][:, w_cols].bitcast(FP8X4), lhsT_scale=wg_s[h][:, w_cols],
                         rhs=h_w[g][1][:, cols].bitcast(FP8X4), rhs_scale=h_s[g][1][:, cols],
                         start=(g == 0 and e == 0), stop=(g == 1 and e == 1),
                     )
-            return opened(c)
+            return c
 
         def action_of_pair(h, u, b):
             y = bank(b)
@@ -268,20 +279,36 @@ def tile_list_hopfield_episode_actions_kernel(
                         )
             return y
 
-        def finish_pair(y, gate, h, u, pieces=1):
-            blocks = 2 // pieces
-            for q in range(pieces):
-                cols = slice(q * blocks * HALF, (q + 1) * blocks * HALF)
-                res = work.tile([P, blocks * HALF], F32, name="res", bufs=8)
-                nc.vector.tensor_tensor(res[:], y[:, cols], gate[:, cols], ALU.mult)
-                row = (2 * h + q * blocks) * P
-                dst = out[row : row + blocks * P, JW + u * HALF : JW + (u + 1) * HALF]
-                nc.sync.dma_start(
-                    dst.rearrange("(e p) c -> p e c", p=P), res[:].rearrange("p (e c) -> p e c", e=blocks)
+        def finish_pair(y, gate, h, u):
+            res = work.tile([P, JW], F32, name="res", bufs=10)
+            nc.vector.tensor_tensor(res[:], y[:], gate[:], ALU.mult)
+            dst = out[2 * h * P : 2 * (h + 1) * P, JW + u * HALF : JW + (u + 1) * HALF]
+            nc.sync.dma_start(dst.rearrange("(e p) c -> p e c", p=P), res[:].rearrange("p (e c) -> p e c", e=2))
+
+        def gate_of_block(nb, u, b):
+            c = bank(b)
+            cols = slice(u * HALF, (u + 1) * HALF)
+            for g in range(2):
+                nc.tensor.matmul_mx(
+                    out=c[:, 0:HALF],
+                    lhsT=wg_w[nb // 2][:, gate_cols(nb, g)].bitcast(FP8X4), lhsT_scale=wg_s[nb // 2][:, gate_cols(nb, g)],
+                    rhs=h_w[g][1][:, cols].bitcast(FP8X4), rhs_scale=h_s[g][1][:, cols],
+                    start=(g == 0), stop=(g == 1),
                 )
+            return c
+
+        def opened_half(c, e):
+            gate = work.tile([P, HALF], F32, name="gate", bufs=10)
+            nc.scalar.activation(gate[:], c[:, e * HALF : (e + 1) * HALF], ACT.Sigmoid)
+            return gate
+
+        def finish_block(y, gate, nb, u):
+            res = work.tile([P, HALF], F32, name="res", bufs=10)
+            nc.vector.tensor_tensor(res[:], y, gate, ALU.mult)
+            nc.sync.dma_start(out[nb * P : (nb + 1) * P, JW + u * HALF : JW + (u + 1) * HALF], res[:])
 
         def finish(y, gate, nb):
-            res = work.tile([P, JW], F32, name="res", bufs=8)
+            res = work.tile([P, JW], F32, name="res", bufs=10)
             nc.vector.tensor_tensor(res[:], y[:], gate[:], ALU.mult)
             nc.sync.dma_start(out[nb * P : (nb + 1) * P, 0:JW], res[:])
 
@@ -290,9 +317,9 @@ def tile_list_hopfield_episode_actions_kernel(
             nc.scalar.copy(y_sb[:], y[:])
             return y_sb
 
-        def finish_on_gpsimd(res, y_sb, gate, nb):
-            nc.gpsimd.tensor_tensor(res[:], y_sb[:], gate[:], ALU.mult)
-            nc.sync.dma_start(out[nb * P : (nb + 1) * P, 0:JW], res[:])
+        def finish_on_gpsimd(res, y_sb, gate, nb, cols=slice(0, JW)):
+            nc.gpsimd.tensor_tensor(res[:], y_sb[:, cols], gate[:, cols], ALU.mult)
+            nc.sync.dma_start(out[nb * P : (nb + 1) * P, cols], res[:])
 
         QUARTER = HALF * PACK
         early = [(0, t) for t in range(PACK)] + [(1, t) for t in range(PACK - 1)]
@@ -304,35 +331,50 @@ def tile_list_hopfield_episode_actions_kernel(
         last = bank(0)
         for a in range(2):
             sim_pass(last, a, 1, PACK - 1, 0)
-        th10 = separate_halves("th10", first[PACK:] + [last], 1)
+        accs = first[PACK:] + [last]
+        th10 = keep.tile([P, 2, PACK, HALF], F32, name="th10", align_bytes=64)
+        nc.scalar.activation(
+            th10[:, :, 0, :], accs[0][:].rearrange("p (u c) -> p u c", u=2), ACT.Tanh, scale=sharp_sb[:, 1, 0:1]
+        )
+        for u in range(2):
+            for t in range(1, PACK):
+                nc.scalar.activation(
+                    th10[:, u, t, :], accs[t][:, u * HALF : (u + 1) * HALF], ACT.Tanh,
+                    scale=sharp_sb[:, 1, t : t + 1],
+                )
 
-        bf00 = keep.tile([P, QUARTER], BF16, name="bf00", align_bytes=64)
+        bf00 = placed("bf00", [P, QUARTER], BF16, 64)
         nc.vector.tensor_copy(walk_out(bf00[:]), walk_in(raw[0][0]))
         bf01 = placed("bf01", [P, QUARTER], BF16, 0)
         round_gate_on_gpsimd(bf01, 0, 1)
 
-        hb00 = placed("hb00", [P, 2 * QUARTER], BF16, 48)
+        hb00 = [placed(f"hb00{u}", [P, QUARTER], BF16, 48 + 2 * u) for u in range(2)]
         for u in range(2):
-            weigh(hb00[:, u * QUARTER : (u + 1) * QUARTER], th00[:, u, :, :], 0)
+            weigh(hb00[u][:], th00[:, u, :, :], 0)
         for u in range(2):
-            quantize(hb00[:, u * QUARTER : (u + 1) * QUARTER], 0, 0, u, u + 1)
-        bf10 = placed("bf10", [P, QUARTER], BF16, 48)
-        round_gate_on_gpsimd(bf10, 1, 0)
-        wg_w = [placed("wg_w0", [P, N], U32, 50), keep.tile([P, N], U32, name="wg_w1", align_bytes=64)]
-
-        sims = similarity(0, 1, (1, 2, 3, 4))
-        th01 = keep.tile([P, PACK, JW], F32, name="th01", align_bytes=64)
-        for t in range(PACK):
-            nc.scalar.activation(th01[:, t, :], sims[t][:], ACT.Tanh, scale=sharp_sb[:, 0, t : t + 1])
-
-        hb10 = placed("hb10", [P, 2 * QUARTER], BF16, 52)
-        for u in range(2):
-            weigh(hb10[:, u * QUARTER : (u + 1) * QUARTER], th10[:, u, :, :], 1)
+            quantize(hb00[u][:], 0, 0, u, u + 1)
+        wg_w = [placed("wg_w0", [P, N], U32, 48), keep.tile([P, N], U32, name="wg_w1", align_bytes=64)]
         quantize_gate(wg_w[0], bf00, 0, 0)
         quantize_gate(wg_w[0], bf01, 0, 1)
-        quantize(hb10[:], 1, 0, 0, 2)
-        bf11 = placed("bf11", [P, QUARTER], BF16, 52)
-        round_gate_on_gpsimd(bf11, 1, 1)
+        bf10 = placed("bf10", [P, QUARTER], BF16, 64)
+        round_block_on_gpsimd(bf10, 0)
+
+        sims = similarity(0, 1, (1, 2, 3, 4))
+        th01 = keep.tile([P, 2, PACK, HALF], F32, name="th01", align_bytes=64)
+        for t in range(PACK):
+            nc.scalar.activation(
+                th01[:, :, t, :], sims[t][:].rearrange("p (u c) -> p u c", u=2), ACT.Tanh,
+                scale=sharp_sb[:, 0, t : t + 1],
+            )
+
+        hb10 = [placed(f"hb10{u}", [P, QUARTER], BF16, 52 + 2 * u) for u in range(2)]
+        for u in range(2):
+            weigh(hb10[u][:], th10[:, u, :, :], 1)
+        for u in range(2):
+            quantize(hb10[u][:], 1, 0, u, u + 1)
+        quantize_gate(wg_w[1], bf10, 1, 0)
+        bf11 = placed("bf11", [P, QUARTER], BF16, 54)
+        round_block_on_gpsimd(bf11, 1)
 
         sims = similarity(1, 1, (5, 6, 0, 1))
         th11 = keep.tile([P, 2, PACK, HALF], F32, name="th11", align_bytes=64)
@@ -344,33 +386,41 @@ def tile_list_hopfield_episode_actions_kernel(
 
         c0, y0 = gate_sum(0, 2), action_of(0, 3)
         c1, y1 = gate_sum(1, 4), action_of(1, 5)
-        hb01 = placed("hb01", [P, 2 * QUARTER], BF16, 56)
-        weigh(hb01[:], th01[:], 0)
-        quantize_gate(wg_w[1], bf10, 1, 0)
+        c2, y2 = gate_sum(2, 6), action_of(2, 0)
+        hb0a = placed("hb0a", [P, QUARTER], BF16, 56)
+        hb1a = placed("hb1a", [P, QUARTER], BF16, 58)
+        weigh(hb0a[:], th01[:, 0, :, :], 0)
+        weigh(hb1a[:], th11[:, 0, :, :], 1)
         quantize_gate(wg_w[1], bf11, 1, 1)
-        quantize(hb01[:], 0, 1, 0, 2)
+        quantize(hb0a[:], 0, 1, 0, 1)
+        quantize(hb1a[:], 1, 1, 0, 1)
         gate0 = opened(c0)
-        finish_on_gpsimd(placed("res0", [P, JW], F32, 56), staged(y0), gate0, 0)
-        c2, y2, y3 = gate_sum(2, 6), action_of(2, 0), action_of(3, 1)
-        c3 = gate_sum(3, 2)
-        gate2 = opened(c2)
+        finish_on_gpsimd(placed("res0", [P, JW], F32, 58), staged(y0), gate0, 0)
+        y3, c3 = action_of(3, 1), gate_sum(3, 2)
         gate1 = opened(c1)
-        y1_sb = staged(y1)
+        gate2 = opened(c2)
+        y2_sb = staged(y2)
         gate3 = opened(c3)
+        gates0 = [opened(gate_of_pair(0, 0, 3)), opened(gate_of_pair(1, 0, 4))]
+        acts0 = [action_of_pair(0, 0, 6), action_of_pair(1, 0, 0)]
 
-        hb11 = [placed(f"hb11{u}", [P, QUARTER], BF16, 60 + 2 * u) for u in range(2)]
-        weigh(hb11[0][:], th11[:, 0, :, :], 1)
-        finish(y2, gate2, 2)
-        quantize(hb11[0][:], 1, 1, 0, 1)
-        finish_on_gpsimd(placed("res1", [P, JW], F32, 60), y1_sb, gate1, 1)
-        gates0 = [gate_of_pair(0, 0, 3), gate_of_pair(1, 0, 6)]
-        acts0 = [action_of_pair(0, 0, 4), action_of_pair(1, 0, 5)]
-        weigh(hb11[1][:], th11[:, 1, :, :], 1)
+
+        hb0b = placed("hb0b", [P, QUARTER], BF16, 60)
+        hb1b = placed("hb1b", [P, QUARTER], BF16, 62)
+        weigh(hb0b[:], th01[:, 1, :, :], 0)
+        finish(y1, gate1, 1)
+        quantize(hb0b[:], 0, 1, 1, 2)
+        finish_on_gpsimd(placed("res2", [P, JW], F32, 60), y2_sb, gate2, 2)
+        weigh(hb1b[:], th11[:, 1, :, :], 1)
         finish(y3, gate3, 3)
-        quantize(hb11[1][:], 1, 1, 1, 2)
-        gates1 = [gate_of_pair(0, 1, 0), gate_of_pair(1, 1, 2)]
-        acts1 = [action_of_pair(0, 1, 3), action_of_pair(1, 1, 1)]
+        quantize(hb1b[:], 1, 1, 1, 2)
+        last_gates = [opened_half(gate_of_block(0, 1, 2), 0), opened_half(gate_of_block(1, 1, 5), 0)]
+        low_act = action_of_pair(0, 1, 3)
+        high_sum = gate_of_pair(1, 1, 4)
+        last_gates = last_gates + [opened_half(high_sum, e) for e in range(2)]
+        last_acts = [low_act, action_of_pair(1, 1, 1)]
         for h in range(2):
             finish_pair(acts0[h], gates0[h], h, 0)
-        for h in range(2):
-            finish_pair(acts1[h], gates1[h], h, 1, pieces=1 + h)
+        for nb in range(4):
+            e = nb % 2
+            finish_block(last_acts[nb // 2][:, e * HALF : (e + 1) * HALF], last_gates[nb][:], nb, 1)

@@ -173,10 +173,15 @@ def tile_list_hopfield_episode_actions_kernel(
         def walk_in(ap):
             return ap.rearrange("p t (c i) -> p c t i", i=4)
 
-        def separate_halves(name, accs, g):
+        def separate(name, accs, g, whole):
             th = keep.tile([P, 2, PACK, HALF], F32, name=name, align_bytes=64)
+            for t in range(whole):
+                nc.scalar.activation(
+                    th[:, :, t, :], accs[t][:].rearrange("p (u c) -> p u c", u=2), ACT.Tanh,
+                    scale=sharp_sb[:, g, t : t + 1],
+                )
             for u in range(2):
-                for t in range(PACK):
+                for t in range(whole, PACK):
                     nc.scalar.activation(
                         th[:, u, t, :], accs[t][:, u * HALF : (u + 1) * HALF], ACT.Tanh,
                         scale=sharp_sb[:, g, t : t + 1],
@@ -307,10 +312,10 @@ def tile_list_hopfield_episode_actions_kernel(
             nc.vector.tensor_tensor(res[:], y, gate, ALU.mult)
             nc.sync.dma_start(out[nb * P : (nb + 1) * P, JW + u * HALF : JW + (u + 1) * HALF], res[:])
 
-        def finish(y, gate, nb):
-            res = work.tile([P, JW], F32, name="res", bufs=10)
-            nc.vector.tensor_tensor(res[:], y[:], gate[:], ALU.mult)
-            nc.sync.dma_start(out[nb * P : (nb + 1) * P, 0:JW], res[:])
+        def finish(y, gate, nb, cols=slice(0, JW)):
+            res = work.tile([P, cols.stop - cols.start], F32, name="res", bufs=10)
+            nc.vector.tensor_tensor(res[:], y[:, cols], gate[:, cols], ALU.mult)
+            nc.sync.dma_start(out[nb * P : (nb + 1) * P, cols], res[:])
 
         def staged(y):
             y_sb = work.tile([P, JW], F32, name="y_sb", bufs=2)
@@ -327,21 +332,11 @@ def tile_list_hopfield_episode_actions_kernel(
         for a in range(2):
             for b, (g, t) in enumerate(early):
                 sim_pass(first[b], a, g, t, 0)
-        th00 = separate_halves("th00", first[0:PACK], 0)
+        th00 = separate("th00", first[0:PACK], 0, 0)
         last = bank(0)
         for a in range(2):
             sim_pass(last, a, 1, PACK - 1, 0)
-        accs = first[PACK:] + [last]
-        th10 = keep.tile([P, 2, PACK, HALF], F32, name="th10", align_bytes=64)
-        nc.scalar.activation(
-            th10[:, :, 0, :], accs[0][:].rearrange("p (u c) -> p u c", u=2), ACT.Tanh, scale=sharp_sb[:, 1, 0:1]
-        )
-        for u in range(2):
-            for t in range(1, PACK):
-                nc.scalar.activation(
-                    th10[:, u, t, :], accs[t][:, u * HALF : (u + 1) * HALF], ACT.Tanh,
-                    scale=sharp_sb[:, 1, t : t + 1],
-                )
+        th10 = separate("th10", first[PACK:] + [last], 1, PACK)
 
         bf00 = placed("bf00", [P, QUARTER], BF16, 64)
         nc.vector.tensor_copy(walk_out(bf00[:]), walk_in(raw[0][0]))
@@ -359,13 +354,7 @@ def tile_list_hopfield_episode_actions_kernel(
         bf10 = placed("bf10", [P, QUARTER], BF16, 64)
         round_block_on_gpsimd(bf10, 0)
 
-        sims = similarity(0, 1, (1, 2, 3, 4))
-        th01 = keep.tile([P, 2, PACK, HALF], F32, name="th01", align_bytes=64)
-        for t in range(PACK):
-            nc.scalar.activation(
-                th01[:, :, t, :], sims[t][:].rearrange("p (u c) -> p u c", u=2), ACT.Tanh,
-                scale=sharp_sb[:, 0, t : t + 1],
-            )
+        th01 = separate("th01", similarity(0, 1, (1, 2, 3, 4)), 0, PACK)
 
         hb10 = [placed(f"hb10{u}", [P, QUARTER], BF16, 52 + 2 * u) for u in range(2)]
         for u in range(2):
@@ -376,13 +365,7 @@ def tile_list_hopfield_episode_actions_kernel(
         bf11 = placed("bf11", [P, QUARTER], BF16, 54)
         round_block_on_gpsimd(bf11, 1)
 
-        sims = similarity(1, 1, (5, 6, 0, 1))
-        th11 = keep.tile([P, 2, PACK, HALF], F32, name="th11", align_bytes=64)
-        for t in range(PACK):
-            nc.scalar.activation(
-                th11[:, :, t, :], sims[t][:].rearrange("p (u c) -> p u c", u=2), ACT.Tanh,
-                scale=sharp_sb[:, 1, t : t + 1],
-            )
+        th11 = separate("th11", similarity(1, 1, (5, 6, 0, 1)), 1, 2)
 
         c0, y0 = gate_sum(0, 2), action_of(0, 3)
         c1, y1 = gate_sum(1, 4), action_of(1, 5)
@@ -411,8 +394,9 @@ def tile_list_hopfield_episode_actions_kernel(
         finish(y1, gate1, 1)
         quantize(hb0b[:], 0, 1, 1, 2)
         finish_on_gpsimd(placed("res2", [P, JW], F32, 60), y2_sb, gate2, 2)
+        finish(y3, gate3, 3, slice(0, HALF))
         weigh(hb1b[:], th11[:, 1, :, :], 1)
-        finish(y3, gate3, 3)
+        finish(y3, gate3, 3, slice(HALF, JW))
         quantize(hb1b[:], 1, 1, 1, 2)
         last_gates = [opened_half(gate_of_block(0, 1, 2), 0), opened_half(gate_of_block(1, 1, 5), 0)]
         low_act = action_of_pair(0, 1, 3)

@@ -22,6 +22,7 @@ PACK = 4
 KP = P * PACK
 JW = 512
 HALF = JW // 2
+PLANE = (0, 4)
 KIB = 1024
 
 
@@ -54,8 +55,6 @@ def tile_list_hopfield_episode_actions_kernel(
         nc.gpsimd.memset(tab_s[:], 0)
         nc.gpsimd.memset(rows[:], 0.0)
         make_identity(nc, ident[:])
-        late_plane = keep.tile([P, (S + S2) // 4], I32, name="late_plane", align_bytes=64)
-        nc.gpsimd.memset(late_plane[:], 0)
         nc.vector.memset(tab2_s[:], 0)
         nc.vector.memset(warm[:], 0.0)
         nc.scalar.activation(warm_out[:], warm[:], ACT.Sigmoid)
@@ -96,13 +95,14 @@ def tile_list_hopfield_episode_actions_kernel(
             v_s_list[:].rearrange("p (g m t) -> p g t m", g=2, t=PACK),
         )
         for r in range(1, 4):
-            nc.sync.dma_start(planes[r:P:32, :].bitcast(I32), planes[8 * r : P : 32, :].bitcast(I32))
+            for a in range(2):
+                nc.sync.dma_start(
+                    planes[PLANE[a] + r : P : 32, :].bitcast(I32),
+                    planes[PLANE[a] + 8 * r : P : 32, :].bitcast(I32),
+                )
 
         tab_w.append(reuse.tile([P, T], I32, name="tab_w1", offset=32 * KIB + S2 // 2, align_bytes=64))
         load_words(tab_w[1], tab_words, 1)
-        for r in range(4):
-            nc.sync.dma_start(late_plane[r:P:32, :], planes[8 * r + 4 : P : 32, :].bitcast(I32))
-        plane = [planes[:], late_plane[:].bitcast(U8)]
         v_w = [
             reuse.tile([P, S], U32, name="v_w0", offset=40 * KIB + 3 * S2 // 4, align_bytes=64),
             keep.tile([P, S], U32, name="v_w1", align_bytes=64),
@@ -139,11 +139,11 @@ def tile_list_hopfield_episode_actions_kernel(
         load_gate(0, 0)
         load_gate(0, 1)
         load_gate(1, 0)
-        load_gate(1, 1)
         nc.sync.dma_start(wact_w[:], wact_words.bitcast(I32).rearrange("g p e -> p g e"))
         for r in range(4):
             src = wact_scales.bitcast(I32).rearrange("g (q r) e -> r q g e", r=4)[r]
             nc.sync.dma_start(wact_s[r:P:32, :, :], src)
+        load_gate(1, 1)
 
         def bank(b):
             return psum.tile([P, JW], F32, name=f"bank{b}")
@@ -153,9 +153,9 @@ def tile_list_hopfield_episode_actions_kernel(
             nc.tensor.matmul_mx(
                 out=acc[:],
                 lhsT=v_w[a][:, cols].bitcast(FP8X4),
-                lhsT_scale=plane[a][:, cols],
+                lhsT_scale=planes[PLANE[a] :, cols],
                 rhs=v2_w[a][jh][:].bitcast(FP8X4),
-                rhs_scale=plane[a][:, S + jh * JW : S + (jh + 1) * JW],
+                rhs_scale=planes[PLANE[a] :, S + jh * JW : S + (jh + 1) * JW],
                 start=(a == 0),
                 stop=(a == 1),
             )
@@ -203,15 +203,8 @@ def tile_list_hopfield_episode_actions_kernel(
                 1.0, 0.0, ALU.mult, ALU.add,
             )
 
-        def round_block_on_gpsimd(dst, e):
-            nc.gpsimd.tensor_scalar(
-                dst[:].rearrange("p (g c t) -> p g c t", g=2, t=PACK),
-                raw1[:, :, :, e * P : (e + 1) * P].rearrange("p g t c -> p g c t"),
-                1.0, 0.0, ALU.mult, ALU.add,
-            )
-
         def gate_cols(nb, g):
-            piece = 2 * g + nb if nb < 2 else 2 * (nb - 2) + g
+            piece = 2 * g + nb % 2
             return slice(piece * P, (piece + 1) * P)
 
         def quantize_gate(codes, src, h, g):
@@ -352,7 +345,7 @@ def tile_list_hopfield_episode_actions_kernel(
         quantize_gate(wg_w[0], bf00, 0, 0)
         quantize_gate(wg_w[0], bf01, 0, 1)
         bf10 = placed("bf10", [P, QUARTER], BF16, 64)
-        round_block_on_gpsimd(bf10, 0)
+        round_gate_on_gpsimd(bf10, 1, 0)
 
         th01 = separate("th01", similarity(0, 1, (1, 2, 3, 4)), 0, PACK)
 
@@ -363,13 +356,13 @@ def tile_list_hopfield_episode_actions_kernel(
             quantize(hb10[u][:], 1, 0, u, u + 1)
         quantize_gate(wg_w[1], bf10, 1, 0)
         bf11 = placed("bf11", [P, QUARTER], BF16, 54)
-        round_block_on_gpsimd(bf11, 1)
+        round_gate_on_gpsimd(bf11, 1, 1)
 
         th11 = separate("th11", similarity(1, 1, (5, 6, 0, 1)), 1, 2)
 
         c0, y0 = gate_sum(0, 2), action_of(0, 3)
         c1, y1 = gate_sum(1, 4), action_of(1, 5)
-        c2, y2 = gate_sum(2, 6), action_of(2, 0)
+        y2, y3 = action_of(2, 6), action_of(3, 0)
         hb0a = placed("hb0a", [P, QUARTER], BF16, 56)
         hb1a = placed("hb1a", [P, QUARTER], BF16, 58)
         weigh(hb0a[:], th01[:, 0, :, :], 0)
@@ -379,13 +372,13 @@ def tile_list_hopfield_episode_actions_kernel(
         quantize(hb1a[:], 1, 1, 0, 1)
         gate0 = opened(c0)
         finish_on_gpsimd(placed("res0", [P, JW], F32, 58), staged(y0), gate0, 0)
-        y3, c3 = action_of(3, 1), gate_sum(3, 2)
+        c2, c3 = gate_sum(2, 1), gate_sum(3, 2)
         gate1 = opened(c1)
-        gate2 = opened(c2)
         y2_sb = staged(y2)
+        gate2 = opened(c2)
         gate3 = opened(c3)
         gates0 = [opened(gate_of_pair(0, 0, 3)), opened(gate_of_pair(1, 0, 4))]
-        acts0 = [action_of_pair(0, 0, 6), action_of_pair(1, 0, 0)]
+        acts0 = [action_of_pair(0, 0, 6), action_of_pair(1, 0, 1)]
 
 
         hb0b = placed("hb0b", [P, QUARTER], BF16, 60)
@@ -402,7 +395,7 @@ def tile_list_hopfield_episode_actions_kernel(
         low_act = action_of_pair(0, 1, 3)
         high_sum = gate_of_pair(1, 1, 4)
         last_gates = last_gates + [opened_half(high_sum, e) for e in range(2)]
-        last_acts = [low_act, action_of_pair(1, 1, 1)]
+        last_acts = [low_act, action_of_pair(1, 1, 0)]
         for h in range(2):
             finish_pair(acts0[h], gates0[h], h, 0)
         for nb in range(4):

@@ -22,8 +22,24 @@ PACK = 4
 KP = P * PACK
 JW = 512
 HALF = JW // 2
+PIECE = HALF * PACK
+LIST_ROWS = 16
 PLANE = (0, 4)
+WALK = 4
 KIB = 1024
+FIRST, SECOND = slice(0, HALF), slice(HALF, JW)
+WHOLE = slice(0, JW)
+
+AT_PROBE_TABLE = 0
+AT_GATE_LOW = (0, 4 * KIB)
+AT_ACT_WORDS = 8 * KIB
+AT_ACT_SCALES = 10 * KIB
+AT_GATE_HIGH = 12 * KIB
+AT_PROBE_SCALES = 40 * KIB
+AT_LAST_TABLE = AT_PROBE_SCALES - 4 * T + S2 // 2
+AT_STATE_WORDS = AT_PROBE_SCALES + 3 * S2 // 4
+AT_PIECES = 48 * KIB
+AT_GATE_ROUNDED = 64 * KIB
 
 
 def tile_list_hopfield_episode_actions_kernel(
@@ -33,31 +49,31 @@ def tile_list_hopfield_episode_actions_kernel(
     nc = tc.nc
     with ExitStack() as ctx:
         keep = ctx.enter_context(tc.tile_pool(name="keep", bufs=1))
-        work = ctx.enter_context(tc.tile_pool(name="work", bufs=2))
+        work = ctx.enter_context(tc.tile_pool(name="work", bufs=1))
         psum = ctx.enter_context(tc.psum_pool(name="psum", bufs=1))
         reuse = ctx.enter_context(tc.tile_pool(name="reuse", bufs=1))
 
-        idx = keep.tile([P, S // 16], U16, name="idx")
-        idx2 = keep.tile([P, S2 // 16], U16, name="idx2")
-        tab_w = [keep.tile([P, T], I32, name="tab_w0", align_bytes=64)]
-        tab2_w = [
-            reuse.tile([P, T2], I32, name="tab2_w0", offset=0, align_bytes=64),
-            keep.tile([P, T2], I32, name="tab2_w1", align_bytes=64),
-        ]
-        tab_s = keep.tile([P, T // 4], I32, name="tab_s", align_bytes=64)
-        tab2_s = keep.tile([P, T2 // 4], I32, name="tab2_s", align_bytes=64)
-        warm = keep.tile([P, 8], F32, name="warm")
-        warm_out = keep.tile([P, 8], F32, name="warm_out")
+        def placed(name, shape, dtype, offset):
+            return reuse.tile(shape, dtype, name=name, offset=offset, align_bytes=64)
 
-        rows = keep.tile([P, KP], F32, name="rows", align_bytes=64)
-        ident = keep.tile([P, P], F32, name="ident", align_bytes=64)
+        def kept(name, shape, dtype):
+            return keep.tile(shape, dtype, name=name, align_bytes=64)
+
+        idx = keep.tile([P, S // LIST_ROWS], U16, name="idx")
+        idx2 = keep.tile([P, S2 // LIST_ROWS], U16, name="idx2")
+        tab_w = [kept("tab_w0", [P, T], I32)]
+        tab2_w = [placed("tab2_w0", [P, T2], I32, AT_PROBE_TABLE), kept("tab2_w1", [P, T2], I32)]
+        tab_s = kept("tab_s", [P, T // 4], I32)
+        tab2_s = kept("tab2_s", [P, T2 // 4], I32)
+        rows = kept("rows", [P, KP], F32)
+        ident = kept("ident", [P, P], F32)
 
         nc.gpsimd.memset(tab_s[:], 0)
         nc.gpsimd.memset(rows[:], 0.0)
         make_identity(nc, ident[:])
         nc.vector.memset(tab2_s[:], 0)
-        nc.vector.memset(warm[:], 0.0)
-        nc.scalar.activation(warm_out[:], warm[:], ACT.Sigmoid)
+        warm = keep.tile([P, 8], F32, name="warm")
+        nc.scalar.activation(warm[:], ident[:, 0:8], ACT.Sigmoid)
 
         def load_words(dst, words, a, cols=slice(None)):
             nc.sync.dma_start(dst[:, cols], words[a].rearrange("p t i -> p (t i)").bitcast(I32)[:, cols])
@@ -79,14 +95,12 @@ def tile_list_hopfield_episode_actions_kernel(
         turned = psum.tile([P, KP], F32, name="turned")
         for t in range(PACK):
             nc.tensor.transpose(turned[:, t * P : (t + 1) * P], rows[:, t:KP:PACK], ident[:])
-        sharp_sb = keep.tile([P, 2, 8], F32, name="sharp_sb", align_bytes=64)
-        nc.scalar.copy(sharp_sb[:, :, 0:PACK], turned[:].rearrange("p (t k) -> p k t", t=PACK)[:, 2:4, :])
+        sharp_sb = kept("sharp_sb", [P, 2, PACK], F32)
+        nc.scalar.copy(sharp_sb[:], turned[:].rearrange("p (t r) -> p r t", t=PACK)[:, 2:4, :])
 
-        v_s_list = keep.tile([P, S], U8, name="v_s_list", align_bytes=64)
-        v2_s_list = reuse.tile([P, S2], U8, name="v2_s_list", offset=40 * KIB, align_bytes=64)
-        planes = keep.tile([P, S + S2], U8, name="planes", align_bytes=64)
-        v2_w = [[keep.tile([P, JW], U32, name=f"v2_w{a}{jh}", align_bytes=64) for jh in range(2)] for a in range(2)]
-
+        v_s_list = kept("v_s_list", [P, S], U8)
+        v2_s_list = placed("v2_s_list", [P, S2], U8, AT_PROBE_SCALES)
+        planes = kept("planes", [P, S + S2], U8)
         nc.vector.tensor_copy(v_s_list[:], tab_s[:].bitcast(U8).indirect(idx[:]))
         nc.vector.tensor_copy(v2_s_list[:], tab2_s[:].bitcast(U8).indirect(idx2[:]))
         nc.vector.tensor_copy(planes[:, S:].bitcast(I32), v2_s_list[:].bitcast(I32))
@@ -101,16 +115,10 @@ def tile_list_hopfield_episode_actions_kernel(
                     planes[PLANE[a] + 8 * r : P : 32, :].bitcast(I32),
                 )
 
-        tab_w.append(reuse.tile([P, T], I32, name="tab_w1", offset=32 * KIB + S2 // 2, align_bytes=64))
+        tab_w.append(placed("tab_w1", [P, T], I32, AT_LAST_TABLE))
         load_words(tab_w[1], tab_words, 1)
-        v_w = [
-            reuse.tile([P, S], U32, name="v_w0", offset=40 * KIB + 3 * S2 // 4, align_bytes=64),
-            keep.tile([P, S], U32, name="v_w1", align_bytes=64),
-        ]
-
-        def gather_probe_words(a, jh):
-            probe_list = idx2[:, jh * JW // 16 : (jh + 1) * JW // 16]
-            nc.vector.tensor_copy(v2_w[a][jh][:], tab2_w[a][:].bitcast(U32).indirect(probe_list))
+        v_w = [placed("v_w0", [P, S], U32, AT_STATE_WORDS), kept("v_w1", [P, S], U32)]
+        v2_w = [[kept(f"v2_w{a}{jh}", [P, JW], U32) for jh in range(2)] for a in range(2)]
 
         nc.vector.tensor_copy(
             v_w[0][:].rearrange("p (g t m) -> p g m t", g=2, t=PACK),
@@ -118,23 +126,24 @@ def tile_list_hopfield_episode_actions_kernel(
         )
         for a in range(2):
             for jh in range(2):
-                gather_probe_words(a, jh)
+                probes = idx2[:, jh * JW // LIST_ROWS : (jh + 1) * JW // LIST_ROWS]
+                nc.vector.tensor_copy(v2_w[a][jh][:], tab2_w[a][:].bitcast(U32).indirect(probes))
         for g in range(2):
             nc.vector.tensor_copy(
                 v_w[1][:, g * KP : (g + 1) * KP].rearrange("p (t m) -> p m t", t=PACK),
-                tab_w[1][:].bitcast(U32).indirect(idx[:, g * KP // 16 : (g + 1) * KP // 16]),
+                tab_w[1][:].bitcast(U32).indirect(idx[:, g * KP // LIST_ROWS : (g + 1) * KP // LIST_ROWS]),
             )
 
-        raw0 = [reuse.tile([P, PACK, HALF], F32, name=f"raw0{g}", offset=4 * g * KIB, align_bytes=64) for g in range(2)]
-        raw1 = reuse.tile([P, 2, PACK, HALF], F32, name="raw1", offset=12 * KIB, align_bytes=64)
-        wact_w = reuse.tile([P, 2, 2 * N // 4], I32, name="wact_w", offset=8 * KIB, align_bytes=64)
-        wact_s = reuse.tile([P, 2, N // 4], I32, name="wact_s", offset=10 * KIB, align_bytes=64)
+        gate_low = [placed(f"gate_low{g}", [P, PACK, HALF], F32, AT_GATE_LOW[g]) for g in range(2)]
+        gate_high = placed("gate_high", [P, 2, PACK, HALF], F32, AT_GATE_HIGH)
+        gate_raw = [[gate_low[g][:] for g in range(2)], [gate_high[:, g, :, :] for g in range(2)]]
+        wact_w = placed("wact_w", [P, 2, 2 * N // 4], I32, AT_ACT_WORDS)
+        wact_s = placed("wact_s", [P, 2, N // 4], I32, AT_ACT_SCALES)
         nc.gpsimd.memset(wact_s[:], 0)
-        raw = [[raw0[0][:], raw0[1][:]], [raw1[:, 0, :, :], raw1[:, 1, :, :]]]
 
-        def load_gate(h, g):
-            src = wgate[g * KP : (g + 1) * KP, h * HALF : (h + 1) * HALF]
-            nc.sync.dma_start(raw[h][g], src.rearrange("(p t) n -> p t n", t=PACK))
+        def load_gate(nh, g):
+            src = wgate[g * KP : (g + 1) * KP, nh * HALF : (nh + 1) * HALF]
+            nc.sync.dma_start(gate_raw[nh][g], src.rearrange("(p t) n -> p t n", t=PACK))
 
         load_gate(0, 0)
         load_gate(0, 1)
@@ -145,10 +154,15 @@ def tile_list_hopfield_episode_actions_kernel(
             nc.sync.dma_start(wact_s[r:P:32, :, :], src)
         load_gate(1, 1)
 
+        h_w = [[kept(f"h_w{g}{jh}", [P, JW], U32) for jh in range(2)] for g in range(2)]
+        h_s = [[kept(f"h_s{g}{jh}", [P, JW], U8) for jh in range(2)] for g in range(2)]
+        wg_w = [kept(f"wg_w{nh}", [P, N], U32) for nh in range(2)]
+        wg_s = [kept(f"wg_s{nh}", [P, N], U8) for nh in range(2)]
+
         def bank(b):
             return psum.tile([P, JW], F32, name=f"bank{b}")
 
-        def sim_pass(acc, a, g, t, jh):
+        def similarity_pass(acc, a, g, t, jh):
             cols = slice(g * KP + t * P, g * KP + (t + 1) * P)
             nc.tensor.matmul_mx(
                 out=acc[:],
@@ -160,244 +174,175 @@ def tile_list_hopfield_episode_actions_kernel(
                 stop=(a == 1),
             )
 
-        def placed(name, shape, dtype, kib):
-            return reuse.tile(shape, dtype, name=name, offset=kib * KIB, align_bytes=64)
+        def similarity(g, jh, banks):
+            accs = [bank(b) for b in banks]
+            for t in range(PACK):
+                for a in range(2):
+                    similarity_pass(accs[t], a, g, t, jh)
+            return accs
 
-        h_w = [[keep.tile([P, JW], U32, name=f"h_w{g}{jh}", align_bytes=64) for jh in range(2)] for g in range(2)]
-        h_s = [[keep.tile([P, JW], U8, name=f"h_s{g}{jh}", align_bytes=64) for jh in range(2)] for g in range(2)]
-        wg_s = [keep.tile([P, N], U8, name=f"wg_s{h}", align_bytes=64) for h in range(2)]
-
-        def walk_out(ap):
-            return ap.rearrange("p (c i t) -> p c t i", i=4, t=PACK)
-
-        def walk_in(ap):
-            return ap.rearrange("p t (c i) -> p c t i", i=4)
-
-        def separate(name, accs, g, whole):
-            th = keep.tile([P, 2, PACK, HALF], F32, name=name, align_bytes=64)
+        def separate(accs, g, jh, whole):
+            th = kept(f"th{g}{jh}", [P, 2, PACK, HALF], F32)
             for t in range(whole):
                 nc.scalar.activation(
                     th[:, :, t, :], accs[t][:].rearrange("p (u c) -> p u c", u=2), ACT.Tanh,
                     scale=sharp_sb[:, g, t : t + 1],
                 )
-            for u in range(2):
+            for u, cols in enumerate((FIRST, SECOND)):
                 for t in range(whole, PACK):
-                    nc.scalar.activation(
-                        th[:, u, t, :], accs[t][:, u * HALF : (u + 1) * HALF], ACT.Tanh,
-                        scale=sharp_sb[:, g, t : t + 1],
-                    )
+                    nc.scalar.activation(th[:, u, t, :], accs[t][:, cols], ACT.Tanh, scale=sharp_sb[:, g, t : t + 1])
             return th
 
-        def weigh(dst, th, g):
-            width = th.shape[2]
-            factor = turned[:, g:KP:P].unsqueeze(1).unsqueeze(3).to_broadcast([P, width // 4, PACK, 4])
-            nc.vector.tensor_tensor(walk_out(dst), walk_in(th), factor, ALU.mult)
+        def walk_out(ap):
+            return ap.rearrange("p (c i t) -> p c t i", i=WALK, t=PACK)
 
-        def quantize(src, g, jh, first, last):
-            cols = slice(first * HALF, last * HALF)
-            nc.vector.quantize_mx(out=h_w[g][jh][:, cols].bitcast(FP8X4), scales=h_s[g][jh][:, cols], in_=src)
+        def walk_in(ap):
+            return ap.rearrange("p t (c i) -> p c t i", i=WALK)
 
-        def round_gate_on_gpsimd(dst, h, g):
+        def piece_at(number):
+            return AT_PIECES + number * 2 * PIECE
+
+        def weigh(number, th, g, u):
+            hb = placed(f"hb{number}", [P, PIECE], BF16, piece_at(number))
+            factor = turned[:, g:KP:P].unsqueeze(1).unsqueeze(3).to_broadcast([P, HALF // WALK, PACK, WALK])
+            nc.vector.tensor_tensor(walk_out(hb[:]), walk_in(th[:, u, :, :]), factor, ALU.mult)
+            return hb
+
+        def quantize(hb, g, jh, cols):
+            nc.vector.quantize_mx(out=h_w[g][jh][:, cols].bitcast(FP8X4), scales=h_s[g][jh][:, cols], in_=hb[:])
+
+        def round_gate_on_gpsimd(nh, g, offset):
+            rounded = placed(f"gate_bf{nh}{g}", [P, PIECE], BF16, offset)
             nc.gpsimd.tensor_scalar(
-                dst[:].rearrange("p (c t) -> p c t", t=PACK), raw[h][g].rearrange("p t c -> p c t"),
+                rounded[:].rearrange("p (c t) -> p c t", t=PACK), gate_raw[nh][g].rearrange("p t c -> p c t"),
                 1.0, 0.0, ALU.mult, ALU.add,
             )
+            return rounded
 
-        def gate_cols(nb, g):
-            piece = 2 * g + nb % 2
-            return slice(piece * P, (piece + 1) * P)
-
-        def quantize_gate(codes, src, h, g):
+        def quantize_gate(rounded, nh, g):
             cols = slice(g * HALF, (g + 1) * HALF)
-            nc.vector.quantize_mx(out=codes[:, cols].bitcast(FP8X4), scales=wg_s[h][:, cols], in_=src[:])
+            nc.vector.quantize_mx(out=wg_w[nh][:, cols].bitcast(FP8X4), scales=wg_s[nh][:, cols], in_=rounded[:])
 
-        def similarity(g, jh, banks):
-            accs = [bank(b) for b in banks]
-            for t in range(PACK):
-                sim_pass(accs[t], 0, g, t, jh)
-                sim_pass(accs[t], 1, g, t, jh)
-            return accs
+        def gate_weights(nb, g):
+            cols = slice(g * HALF + nb % 2 * P, g * HALF + (nb % 2 + 1) * P)
+            return wg_w[nb // 2][:, cols].bitcast(FP8X4), wg_s[nb // 2][:, cols]
 
-        def gate_sum(nb, b):
-            c = bank(b)
-            for g in range(2):
-                cols = gate_cols(nb, g)
+        def action_weights(nb, g):
+            words = wact_w[:, g, :].bitcast(U8)[:, 2 * nb * P : 2 * (nb + 1) * P]
+            return words.bitcast(FP4X4), wact_s[:, g, :].bitcast(U8)[:, nb * P : (nb + 1) * P]
+
+        def project(b, weights, blocks, jh, cols, step):
+            acc = bank(b)
+            width = cols.stop - cols.start
+            passes = [(g, e, at) for g in range(2) for e in range(len(blocks)) for at in range(0, width, step)]
+            for g, e, at in passes:
+                words, scales = weights(blocks[e], g)
+                moving = slice(cols.start + at, cols.start + at + step)
                 nc.tensor.matmul_mx(
-                    out=c[:], lhsT=wg_w[nb // 2][:, cols].bitcast(FP8X4), lhsT_scale=wg_s[nb // 2][:, cols],
-                    rhs=h_w[g][0][:].bitcast(FP8X4), rhs_scale=h_s[g][0][:],
-                    start=(g == 0), stop=(g == 1),
+                    out=acc[:, e * width + at : e * width + at + step], lhsT=words, lhsT_scale=scales,
+                    rhs=h_w[g][jh][:, moving].bitcast(FP8X4), rhs_scale=h_s[g][jh][:, moving],
+                    start=((g, e, at) == passes[0]), stop=((g, e, at) == passes[-1]),
                 )
-            return c
+            return acc
 
-        def opened(c):
-            gate = work.tile([P, JW], F32, name="gate", bufs=10)
-            nc.scalar.activation(gate[:], c[:], ACT.Sigmoid)
+        def gate_sum(b, blocks, jh, cols):
+            return project(b, gate_weights, blocks, jh, cols, cols.stop - cols.start)
+
+        def action_sum(b, blocks, jh, cols):
+            return project(b, action_weights, blocks, jh, cols, JW if cols == WHOLE else P)
+
+        def opened(c, cols=WHOLE):
+            gate = work.tile([P, cols.stop - cols.start], F32, name="gate", bufs=10)
+            nc.scalar.activation(gate[:], c[:, cols], ACT.Sigmoid)
             return gate
-
-        def action_of(nb, b):
-            cols = slice(nb * P, (nb + 1) * P)
-            y = bank(b)
-            for g in range(2):
-                nc.tensor.matmul_mx(
-                    out=y[:],
-                    lhsT=wact_w[:, g, :].bitcast(U8)[:, 2 * nb * P : 2 * (nb + 1) * P].bitcast(FP4X4),
-                    lhsT_scale=wact_s[:, g, :].bitcast(U8)[:, cols],
-                    rhs=h_w[g][0][:].bitcast(FP8X4), rhs_scale=h_s[g][0][:],
-                    start=(g == 0), stop=(g == 1),
-                )
-            return y
-
-        def gate_of_pair(h, u, b):
-            c = bank(b)
-            cols = slice(u * HALF, (u + 1) * HALF)
-            for g in range(2):
-                for e in range(2):
-                    w_cols = gate_cols(2 * h + e, g)
-                    nc.tensor.matmul_mx(
-                        out=c[:, e * HALF : (e + 1) * HALF],
-                        lhsT=wg_w[h][:, w_cols].bitcast(FP8X4), lhsT_scale=wg_s[h][:, w_cols],
-                        rhs=h_w[g][1][:, cols].bitcast(FP8X4), rhs_scale=h_s[g][1][:, cols],
-                        start=(g == 0 and e == 0), stop=(g == 1 and e == 1),
-                    )
-            return c
-
-        def action_of_pair(h, u, b):
-            y = bank(b)
-            for g in range(2):
-                for e in range(2):
-                    nb = 2 * h + e
-                    for q in range(2):
-                        cols = slice(u * HALF + q * P, u * HALF + (q + 1) * P)
-                        nc.tensor.matmul_mx(
-                            out=y[:, e * HALF + q * P : e * HALF + (q + 1) * P],
-                            lhsT=wact_w[:, g, :].bitcast(U8)[:, 2 * nb * P : 2 * (nb + 1) * P].bitcast(FP4X4),
-                            lhsT_scale=wact_s[:, g, :].bitcast(U8)[:, nb * P : (nb + 1) * P],
-                            rhs=h_w[g][1][:, cols].bitcast(FP8X4), rhs_scale=h_s[g][1][:, cols],
-                            start=(g == 0 and e == 0 and q == 0), stop=(g == 1 and e == 1 and q == 1),
-                        )
-            return y
-
-        def finish_pair(y, gate, h, u):
-            res = work.tile([P, JW], F32, name="res", bufs=10)
-            nc.vector.tensor_tensor(res[:], y[:], gate[:], ALU.mult)
-            dst = out[2 * h * P : 2 * (h + 1) * P, JW + u * HALF : JW + (u + 1) * HALF]
-            nc.sync.dma_start(dst.rearrange("(e p) c -> p e c", p=P), res[:].rearrange("p (e c) -> p e c", e=2))
-
-        def gate_of_block(nb, u, b):
-            c = bank(b)
-            cols = slice(u * HALF, (u + 1) * HALF)
-            for g in range(2):
-                nc.tensor.matmul_mx(
-                    out=c[:, 0:HALF],
-                    lhsT=wg_w[nb // 2][:, gate_cols(nb, g)].bitcast(FP8X4), lhsT_scale=wg_s[nb // 2][:, gate_cols(nb, g)],
-                    rhs=h_w[g][1][:, cols].bitcast(FP8X4), rhs_scale=h_s[g][1][:, cols],
-                    start=(g == 0), stop=(g == 1),
-                )
-            return c
-
-        def opened_half(c, e):
-            gate = work.tile([P, HALF], F32, name="gate", bufs=10)
-            nc.scalar.activation(gate[:], c[:, e * HALF : (e + 1) * HALF], ACT.Sigmoid)
-            return gate
-
-        def finish_block(y, gate, nb, u):
-            res = work.tile([P, HALF], F32, name="res", bufs=10)
-            nc.vector.tensor_tensor(res[:], y, gate, ALU.mult)
-            nc.sync.dma_start(out[nb * P : (nb + 1) * P, JW + u * HALF : JW + (u + 1) * HALF], res[:])
-
-        def finish(y, gate, nb, cols=slice(0, JW)):
-            res = work.tile([P, cols.stop - cols.start], F32, name="res", bufs=10)
-            nc.vector.tensor_tensor(res[:], y[:, cols], gate[:, cols], ALU.mult)
-            nc.sync.dma_start(out[nb * P : (nb + 1) * P, cols], res[:])
 
         def staged(y):
             y_sb = work.tile([P, JW], F32, name="y_sb", bufs=2)
             nc.scalar.copy(y_sb[:], y[:])
             return y_sb
 
-        def finish_on_gpsimd(res, y_sb, gate, nb, cols=slice(0, JW)):
-            nc.gpsimd.tensor_tensor(res[:], y_sb[:, cols], gate[:, cols], ALU.mult)
-            nc.sync.dma_start(out[nb * P : (nb + 1) * P, cols], res[:])
+        def store(res, blocks, jh, cols):
+            dst = out[blocks[0] * P : (blocks[-1] + 1) * P, jh * JW + cols.start : jh * JW + cols.stop]
+            nc.sync.dma_start(
+                dst.rearrange("(e p) c -> p e c", p=P), res[:].rearrange("p (e c) -> p e c", e=len(blocks))
+            )
 
-        QUARTER = HALF * PACK
-        early = [(0, t) for t in range(PACK)] + [(1, t) for t in range(PACK - 1)]
+        def finish(y, gate, blocks, jh, cols):
+            res = work.tile([P, len(blocks) * (cols.stop - cols.start)], F32, name="res", bufs=9)
+            nc.vector.tensor_tensor(res[:], y, gate, ALU.mult)
+            store(res, blocks, jh, cols)
+
+        def finish_on_gpsimd(y_sb, gate, nb, offset):
+            res = placed(f"res{nb}", [P, JW], F32, offset)
+            nc.gpsimd.tensor_tensor(res[:], y_sb[:], gate[:], ALU.mult)
+            store(res, [nb], 0, WHOLE)
+
+        early = [(g, t) for g in range(2) for t in range(PACK)][:-1]
         first = [bank(b) for b in range(len(early))]
         for a in range(2):
-            for b, (g, t) in enumerate(early):
-                sim_pass(first[b], a, g, t, 0)
-        th00 = separate("th00", first[0:PACK], 0, 0)
-        last = bank(0)
+            for acc, (g, t) in zip(first, early):
+                similarity_pass(acc, a, g, t, 0)
+        th00 = separate(first[:PACK], 0, 0, whole=0)
+        eighth = bank(0)
         for a in range(2):
-            sim_pass(last, a, 1, PACK - 1, 0)
-        th10 = separate("th10", first[PACK:] + [last], 1, PACK)
+            similarity_pass(eighth, a, 1, PACK - 1, 0)
+        th10 = separate(first[PACK:] + [eighth], 1, 0, whole=PACK)
 
-        bf00 = placed("bf00", [P, QUARTER], BF16, 64)
-        nc.vector.tensor_copy(walk_out(bf00[:]), walk_in(raw[0][0]))
-        bf01 = placed("bf01", [P, QUARTER], BF16, 0)
-        round_gate_on_gpsimd(bf01, 0, 1)
+        rounded = placed("gate_bf00", [P, PIECE], BF16, AT_GATE_ROUNDED)
+        nc.vector.tensor_copy(walk_out(rounded[:]), walk_in(gate_raw[0][0]))
+        quantize_gate(rounded, 0, 0)
+        rounded = round_gate_on_gpsimd(0, 1, AT_GATE_ROUNDED)
 
-        hb00 = [placed(f"hb00{u}", [P, QUARTER], BF16, 48 + 2 * u) for u in range(2)]
-        for u in range(2):
-            weigh(hb00[u][:], th00[:, u, :, :], 0)
-        for u in range(2):
-            quantize(hb00[u][:], 0, 0, u, u + 1)
-        wg_w = [placed("wg_w0", [P, N], U32, 48), keep.tile([P, N], U32, name="wg_w1", align_bytes=64)]
-        quantize_gate(wg_w[0], bf00, 0, 0)
-        quantize_gate(wg_w[0], bf01, 0, 1)
-        bf10 = placed("bf10", [P, QUARTER], BF16, 64)
-        round_gate_on_gpsimd(bf10, 1, 0)
+        weighed = [weigh(u, th00, 0, u) for u in range(2)]
+        quantize(weighed[0], 0, 0, FIRST)
+        quantize(weighed[1], 0, 0, SECOND)
+        quantize_gate(rounded, 0, 1)
+        rounded = round_gate_on_gpsimd(1, 0, AT_GATE_ROUNDED)
 
-        th01 = separate("th01", similarity(0, 1, (1, 2, 3, 4)), 0, PACK)
+        th01 = separate(similarity(0, 1, (1, 2, 3, 4)), 0, 1, whole=PACK)
 
-        hb10 = [placed(f"hb10{u}", [P, QUARTER], BF16, 52 + 2 * u) for u in range(2)]
-        for u in range(2):
-            weigh(hb10[u][:], th10[:, u, :, :], 1)
-        for u in range(2):
-            quantize(hb10[u][:], 1, 0, u, u + 1)
-        quantize_gate(wg_w[1], bf10, 1, 0)
-        bf11 = placed("bf11", [P, QUARTER], BF16, 54)
-        round_gate_on_gpsimd(bf11, 1, 1)
+        weighed = [weigh(2 + u, th10, 1, u) for u in range(2)]
+        quantize(weighed[0], 1, 0, FIRST)
+        quantize(weighed[1], 1, 0, SECOND)
+        quantize_gate(rounded, 1, 0)
+        rounded = round_gate_on_gpsimd(1, 1, piece_at(3))
 
-        th11 = separate("th11", similarity(1, 1, (5, 6, 0, 1)), 1, 2)
+        th11 = separate(similarity(1, 1, (5, 6, 0, 1)), 1, 1, whole=2)
 
-        c0, y0 = gate_sum(0, 2), action_of(0, 3)
-        c1, y1 = gate_sum(1, 4), action_of(1, 5)
-        y2, y3 = action_of(2, 6), action_of(3, 0)
-        hb0a = placed("hb0a", [P, QUARTER], BF16, 56)
-        hb1a = placed("hb1a", [P, QUARTER], BF16, 58)
-        weigh(hb0a[:], th01[:, 0, :, :], 0)
-        weigh(hb1a[:], th11[:, 0, :, :], 1)
-        quantize_gate(wg_w[1], bf11, 1, 1)
-        quantize(hb0a[:], 0, 1, 0, 1)
-        quantize(hb1a[:], 1, 1, 0, 1)
+        c0, y0 = gate_sum(2, [0], 0, WHOLE), action_sum(3, [0], 0, WHOLE)
+        c1, y1 = gate_sum(4, [1], 0, WHOLE), action_sum(5, [1], 0, WHOLE)
+        y2, y3 = action_sum(6, [2], 0, WHOLE), action_sum(0, [3], 0, WHOLE)
+        weighed = [weigh(4, th01, 0, 0), weigh(5, th11, 1, 0)]
+        quantize_gate(rounded, 1, 1)
+        quantize(weighed[0], 0, 1, FIRST)
+        quantize(weighed[1], 1, 1, FIRST)
         gate0 = opened(c0)
-        finish_on_gpsimd(placed("res0", [P, JW], F32, 58), staged(y0), gate0, 0)
-        c2, c3 = gate_sum(2, 1), gate_sum(3, 2)
+        finish_on_gpsimd(staged(y0), gate0, 0, piece_at(5))
+        c2, c3 = gate_sum(1, [2], 0, WHOLE), gate_sum(2, [3], 0, WHOLE)
         gate1 = opened(c1)
         y2_sb = staged(y2)
         gate2 = opened(c2)
         gate3 = opened(c3)
-        gates0 = [opened(gate_of_pair(0, 0, 3)), opened(gate_of_pair(1, 0, 4))]
-        acts0 = [action_of_pair(0, 0, 6), action_of_pair(1, 0, 1)]
 
+        pairs = ([0, 1], [2, 3])
+        pair_gates = [opened(gate_sum(b, pair, 1, FIRST)) for b, pair in zip((3, 4), pairs)]
+        pair_actions = [action_sum(b, pair, 1, FIRST) for b, pair in zip((6, 1), pairs)]
 
-        hb0b = placed("hb0b", [P, QUARTER], BF16, 60)
-        hb1b = placed("hb1b", [P, QUARTER], BF16, 62)
-        weigh(hb0b[:], th01[:, 1, :, :], 0)
-        finish(y1, gate1, 1)
-        quantize(hb0b[:], 0, 1, 1, 2)
-        finish_on_gpsimd(placed("res2", [P, JW], F32, 60), y2_sb, gate2, 2)
-        finish(y3, gate3, 3, slice(0, HALF))
-        weigh(hb1b[:], th11[:, 1, :, :], 1)
-        finish(y3, gate3, 3, slice(HALF, JW))
-        quantize(hb1b[:], 1, 1, 1, 2)
-        last_gates = [opened_half(gate_of_block(0, 1, 2), 0), opened_half(gate_of_block(1, 1, 5), 0)]
-        low_act = action_of_pair(0, 1, 3)
-        high_sum = gate_of_pair(1, 1, 4)
-        last_gates = last_gates + [opened_half(high_sum, e) for e in range(2)]
-        last_acts = [low_act, action_of_pair(1, 1, 0)]
-        for h in range(2):
-            finish_pair(acts0[h], gates0[h], h, 0)
+        hb = weigh(6, th01, 0, 1)
+        finish(y1[:], gate1[:], [1], 0, WHOLE)
+        quantize(hb, 0, 1, SECOND)
+        finish_on_gpsimd(y2_sb, gate2, 2, piece_at(6))
+        finish(y3[:, FIRST], gate3[:, FIRST], [3], 0, FIRST)
+        hb = weigh(7, th11, 1, 1)
+        finish(y3[:, SECOND], gate3[:, SECOND], [3], 0, SECOND)
+        quantize(hb, 1, 1, SECOND)
+
+        last_gates = [opened(gate_sum(b, [nb], 1, SECOND), FIRST) for b, nb in ((2, 0), (5, 1))]
+        low_actions = action_sum(3, pairs[0], 1, SECOND)
+        high_gates = gate_sum(4, pairs[1], 1, SECOND)
+        last_gates = last_gates + [opened(high_gates, cols) for cols in (FIRST, SECOND)]
+        last_actions = [low_actions, action_sum(0, pairs[1], 1, SECOND)]
+        for y, gate, pair in zip(pair_actions, pair_gates, pairs):
+            finish(y[:], gate[:], pair, 1, FIRST)
         for nb in range(4):
-            e = nb % 2
-            finish_block(last_acts[nb // 2][:, e * HALF : (e + 1) * HALF], last_gates[nb][:], nb, 1)
+            finish(last_actions[nb // 2][:, (FIRST, SECOND)[nb % 2]], last_gates[nb][:], [nb], 1, SECOND)

@@ -268,7 +268,7 @@ def tile_list_hopfield_episode_actions_kernel(
             )
 
         def finish(y, gate, blocks, jh, cols):
-            res = work.tile([P, len(blocks) * (cols.stop - cols.start)], F32, name="res", bufs=9)
+            res = work.tile([P, len(blocks) * (cols.stop - cols.start)], F32, name="res", bufs=11)
             nc.vector.tensor_tensor(res[:], y, gate, ALU.mult)
             store(res, blocks, jh, cols)
 
@@ -342,7 +342,11 @@ def tile_list_hopfield_episode_actions_kernel(
         high_gates = gate_sum(4, pairs[1], 1, SECOND)
         last_gates = last_gates + [opened(high_gates, cols) for cols in (FIRST, SECOND)]
         last_actions = [low_actions, action_sum(0, pairs[1], 1, SECOND)]
-        for y, gate, pair in zip(pair_actions, pair_gates, pairs):
-            finish(y[:], gate[:], pair, 1, FIRST)
-        for nb in range(4):
+        for nb, cols in enumerate((FIRST, SECOND)):
+            finish(pair_actions[0][:, cols], pair_gates[0][:, cols], [nb], 1, FIRST)
+        finish(pair_actions[1][:], pair_gates[1][:], pairs[1], 1, FIRST)
+        for nb in range(3):
             finish(last_actions[nb // 2][:, (FIRST, SECOND)[nb % 2]], last_gates[nb][:], [nb], 1, SECOND)
+        for at in (0, P):
+            cols = slice(HALF + at, HALF + at + P)
+            finish(last_actions[1][:, cols], last_gates[3][:, at : at + P], [3], 1, cols)

@@ -98,25 +98,25 @@ def tile_list_hopfield_episode_actions_kernel(
         sharp_sb = kept("sharp_sb", [P, 2, PACK], F32)
         nc.scalar.copy(sharp_sb[:], turned[:].rearrange("p (t r) -> p r t", t=PACK)[:, 2:4, :])
 
-        v_s_list = kept("v_s_list", [P, S], U8)
-        v2_s_list = placed("v2_s_list", [P, S2], U8, AT_PROBE_SCALES)
-        planes = kept("planes", [P, S + S2], U8)
-        nc.vector.tensor_copy(v_s_list[:], tab_s[:].bitcast(U8).indirect(idx[:]))
-        nc.vector.tensor_copy(v2_s_list[:], tab2_s[:].bitcast(U8).indirect(idx2[:]))
-        nc.vector.tensor_copy(planes[:, S:].bitcast(I32), v2_s_list[:].bitcast(I32))
+        listed = placed("listed", [P, S + S2], U8, AT_PROBE_SCALES - S)
+        planes = [kept(f"planes{a}", [P, S + S2], U8) for a in range(2)]
         nc.vector.tensor_copy(
-            planes[:, 0:S].rearrange("p (g t m) -> p g t m", g=2, t=PACK),
-            v_s_list[:].rearrange("p (g m t) -> p g t m", g=2, t=PACK),
+            listed[:, 0:S].rearrange("p (g t m) -> p g m t", g=2, t=PACK), tab_s[:].bitcast(U8).indirect(idx[:])
         )
-        for r in range(1, 4):
-            for a in range(2):
+        nc.vector.tensor_copy(listed[:, S:], tab2_s[:].bitcast(U8).indirect(idx2[:]))
+        for a in range(2):
+            nc.vector.tensor_copy(planes[a][:].bitcast(I32), listed[:].bitcast(I32))
+        def move_rows(a):
+            for r in range(1, 4):
                 nc.sync.dma_start(
-                    planes[PLANE[a] + r : P : 32, :].bitcast(I32),
-                    planes[PLANE[a] + 8 * r : P : 32, :].bitcast(I32),
+                    planes[a][PLANE[a] + r : P : 32, :].bitcast(I32),
+                    planes[a][PLANE[a] + 8 * r : P : 32, :].bitcast(I32),
                 )
 
+        move_rows(0)
         tab_w.append(placed("tab_w1", [P, T], I32, AT_LAST_TABLE))
         load_words(tab_w[1], tab_words, 1)
+        move_rows(1)
         v_w = [placed("v_w0", [P, S], U32, AT_STATE_WORDS), kept("v_w1", [P, S], U32)]
         v2_w = [[kept(f"v2_w{a}{jh}", [P, JW], U32) for jh in range(2)] for a in range(2)]
 
@@ -167,9 +167,9 @@ def tile_list_hopfield_episode_actions_kernel(
             nc.tensor.matmul_mx(
                 out=acc[:],
                 lhsT=v_w[a][:, cols].bitcast(FP8X4),
-                lhsT_scale=planes[PLANE[a] :, cols],
+                lhsT_scale=planes[a][PLANE[a] :, cols],
                 rhs=v2_w[a][jh][:].bitcast(FP8X4),
-                rhs_scale=planes[PLANE[a] :, S + jh * JW : S + (jh + 1) * JW],
+                rhs_scale=planes[a][PLANE[a] :, S + jh * JW : S + (jh + 1) * JW],
                 start=(a == 0),
                 stop=(a == 1),
             )

@@ -81,15 +81,15 @@ def tile_list_hopfield_episode_actions_kernel(
         def load_scales(dst, scales):
             nc.sync.dma_start(dst[0:P:4, :], scales.bitcast(I32).rearrange("a q n -> q a n"))
 
+        load_words(tab_w[0], tab_words, 0, slice(0, T // 4))
         nc.sync.dma_start(idx[:], offs)
         nc.sync.dma_start(idx2[:], offs2)
-        load_words(tab_w[0], tab_words, 0, slice(0, T // 4))
         load_scales(tab_s, tab_scales)
         load_words(tab_w[0], tab_words, 0, slice(T // 4, T))
         load_scales(tab2_s, tab2_scales)
+        load_words(tab2_w[0], tab2_words, 0)
         nc.sync.dma_start(rows[0:2, :], trust.rearrange("(g m) -> g m", g=2))
         nc.sync.dma_start(rows[2:4, :], sharp.rearrange("(g m) -> g m", g=2))
-        load_words(tab2_w[0], tab2_words, 0)
         load_words(tab2_w[1], tab2_words, 1)
 
         turned = psum.tile([P, KP], F32, name="turned")
@@ -249,7 +249,7 @@ def tile_list_hopfield_episode_actions_kernel(
             return project(b, gate_weights, blocks, jh, cols, cols.stop - cols.start)
 
         def action_sum(b, blocks, jh, cols):
-            return project(b, action_weights, blocks, jh, cols, JW if cols == WHOLE else P)
+            return project(b, action_weights, blocks, jh, cols, cols.stop - cols.start)
 
         def opened(c, cols=WHOLE):
             gate = work.tile([P, cols.stop - cols.start], F32, name="gate", bufs=10)

@@ -289,8 +289,14 @@ def tile_list_hopfield_episode_actions_kernel(
         th10 = separate(first[PACK:] + [eighth], 1, 0, whole=PACK)
 
         rounded = placed("gate_bf00", [P, PIECE], BF16, AT_GATE_ROUNDED)
-        nc.vector.tensor_copy(walk_out(rounded[:]), walk_in(gate_raw[0][0]))
-        quantize_gate(rounded, 0, 0)
+        for nb in range(2):
+            values = rounded[:, nb * KP : (nb + 1) * KP]
+            nc.vector.tensor_copy(walk_out(values), walk_in(gate_raw[0][0][:, :, nb * P : (nb + 1) * P]))
+        for nb in range(2):
+            cols = slice(nb * P, (nb + 1) * P)
+            nc.vector.quantize_mx(
+                out=wg_w[0][:, cols].bitcast(FP8X4), scales=wg_s[0][:, cols], in_=rounded[:, nb * KP : (nb + 1) * KP]
+            )
         rounded = round_gate_on_gpsimd(0, 1, AT_GATE_ROUNDED)
 
         weighed = [weigh(u, th00, 0, u) for u in range(2)]

@@ -35,9 +35,9 @@ AT_GATE_LOW = (0, 4 * KIB)
 AT_ACT_WORDS = 8 * KIB
 AT_ACT_SCALES = 10 * KIB
 AT_GATE_HIGH = 12 * KIB
-AT_PROBE_SCALES = 40 * KIB
-AT_LAST_TABLE = AT_PROBE_SCALES - 4 * T + S2 // 2
-AT_STATE_WORDS = AT_PROBE_SCALES + 3 * S2 // 4
+AT_LISTED = 39 * KIB
+AT_LAST_TABLE = AT_LISTED + 3 * KIB // 2 - 4 * T
+AT_STATE_WORDS = AT_LISTED + 7 * KIB // 4
 AT_PIECES = 48 * KIB
 AT_GATE_ROUNDED = 64 * KIB
 
@@ -98,7 +98,7 @@ def tile_list_hopfield_episode_actions_kernel(
         sharp_sb = kept("sharp_sb", [P, 2, PACK], F32)
         nc.scalar.copy(sharp_sb[:], turned[:].rearrange("p (t r) -> p r t", t=PACK)[:, 2:4, :])
 
-        listed = placed("listed", [P, S + S2], U8, AT_PROBE_SCALES - S)
+        listed = placed("listed", [P, S + S2], U8, AT_LISTED)
         planes = [kept(f"planes{a}", [P, S + S2], U8) for a in range(2)]
         nc.vector.tensor_copy(
             listed[:, 0:S].rearrange("p (g t m) -> p g m t", g=2, t=PACK), tab_s[:].bitcast(U8).indirect(idx[:])
@@ -106,6 +106,7 @@ def tile_list_hopfield_episode_actions_kernel(
         nc.vector.tensor_copy(listed[:, S:], tab2_s[:].bitcast(U8).indirect(idx2[:]))
         for a in range(2):
             nc.vector.tensor_copy(planes[a][:].bitcast(I32), listed[:].bitcast(I32))
+
         def move_rows(a):
             for r in range(1, 4):
                 nc.sync.dma_start(
@@ -214,7 +215,8 @@ def tile_list_hopfield_episode_actions_kernel(
         def round_gate_on_gpsimd(nh, g, offset):
             rounded = placed(f"gate_bf{nh}{g}", [P, PIECE], BF16, offset)
             nc.gpsimd.tensor_scalar(
-                rounded[:].rearrange("p (c t) -> p c t", t=PACK), gate_raw[nh][g].rearrange("p t c -> p c t"),
+                rounded[:].rearrange("p (c i t) -> p c t i", i=2, t=PACK),
+                gate_raw[nh][g].rearrange("p t (c i) -> p c t i", i=2),
                 1.0, 0.0, ALU.mult, ALU.add,
             )
             return rounded
@@ -231,25 +233,24 @@ def tile_list_hopfield_episode_actions_kernel(
             words = wact_w[:, g, :].bitcast(U8)[:, 2 * nb * P : 2 * (nb + 1) * P]
             return words.bitcast(FP4X4), wact_s[:, g, :].bitcast(U8)[:, nb * P : (nb + 1) * P]
 
-        def project(b, weights, blocks, jh, cols, step):
+        def project(b, weights, blocks, jh, cols):
             acc = bank(b)
             width = cols.stop - cols.start
-            passes = [(g, e, at) for g in range(2) for e in range(len(blocks)) for at in range(0, width, step)]
-            for g, e, at in passes:
+            passes = [(g, e) for g in range(2) for e in range(len(blocks))]
+            for g, e in passes:
                 words, scales = weights(blocks[e], g)
-                moving = slice(cols.start + at, cols.start + at + step)
                 nc.tensor.matmul_mx(
-                    out=acc[:, e * width + at : e * width + at + step], lhsT=words, lhsT_scale=scales,
-                    rhs=h_w[g][jh][:, moving].bitcast(FP8X4), rhs_scale=h_s[g][jh][:, moving],
-                    start=((g, e, at) == passes[0]), stop=((g, e, at) == passes[-1]),
+                    out=acc[:, e * width : (e + 1) * width], lhsT=words, lhsT_scale=scales,
+                    rhs=h_w[g][jh][:, cols].bitcast(FP8X4), rhs_scale=h_s[g][jh][:, cols],
+                    start=((g, e) == passes[0]), stop=((g, e) == passes[-1]),
                 )
             return acc
 
         def gate_sum(b, blocks, jh, cols):
-            return project(b, gate_weights, blocks, jh, cols, cols.stop - cols.start)
+            return project(b, gate_weights, blocks, jh, cols)
 
         def action_sum(b, blocks, jh, cols):
-            return project(b, action_weights, blocks, jh, cols, cols.stop - cols.start)
+            return project(b, action_weights, blocks, jh, cols)
 
         def opened(c, cols=WHOLE):
             gate = work.tile([P, cols.stop - cols.start], F32, name="gate", bufs=10)
@@ -290,13 +291,12 @@ def tile_list_hopfield_episode_actions_kernel(
 
         rounded = placed("gate_bf00", [P, PIECE], BF16, AT_GATE_ROUNDED)
         for nb in range(2):
-            values = rounded[:, nb * KP : (nb + 1) * KP]
+            values = rounded[:, nb * PACK * P : (nb + 1) * PACK * P]
             nc.vector.tensor_copy(walk_out(values), walk_in(gate_raw[0][0][:, :, nb * P : (nb + 1) * P]))
         for nb in range(2):
             cols = slice(nb * P, (nb + 1) * P)
-            nc.vector.quantize_mx(
-                out=wg_w[0][:, cols].bitcast(FP8X4), scales=wg_s[0][:, cols], in_=rounded[:, nb * KP : (nb + 1) * KP]
-            )
+            values = rounded[:, nb * PACK * P : (nb + 1) * PACK * P]
+            nc.vector.quantize_mx(out=wg_w[0][:, cols].bitcast(FP8X4), scales=wg_s[0][:, cols], in_=values)
         rounded = round_gate_on_gpsimd(0, 1, AT_GATE_ROUNDED)
 
         weighed = [weigh(u, th00, 0, u) for u in range(2)]

@@ -27,6 +27,7 @@ LIST_ROWS = 16
 PLANE = (0, 4)
 WALK = 4
 KIB = 1024
+ALIGN = 256
 FIRST, SECOND = slice(0, HALF), slice(HALF, JW)
 WHOLE = slice(0, JW)
 
@@ -54,10 +55,10 @@ def tile_list_hopfield_episode_actions_kernel(
         reuse = ctx.enter_context(tc.tile_pool(name="reuse", bufs=1))
 
         def placed(name, shape, dtype, offset):
-            return reuse.tile(shape, dtype, name=name, offset=offset, align_bytes=64)
+            return reuse.tile(shape, dtype, name=name, offset=offset, align_bytes=ALIGN)
 
         def kept(name, shape, dtype):
-            return keep.tile(shape, dtype, name=name, align_bytes=64)
+            return keep.tile(shape, dtype, name=name, align_bytes=ALIGN)
 
         idx = keep.tile([P, S // LIST_ROWS], U16, name="idx")
         idx2 = keep.tile([P, S2 // LIST_ROWS], U16, name="idx2")
@@ -253,12 +254,12 @@ def tile_list_hopfield_episode_actions_kernel(
             return project(b, action_weights, blocks, jh, cols)
 
         def opened(c, cols=WHOLE):
-            gate = work.tile([P, cols.stop - cols.start], F32, name="gate", bufs=10)
+            gate = work.tile([P, cols.stop - cols.start], F32, name="gate", bufs=10, align_bytes=ALIGN)
             nc.scalar.activation(gate[:], c[:, cols], ACT.Sigmoid)
             return gate
 
         def staged(y):
-            y_sb = work.tile([P, JW], F32, name="y_sb", bufs=2)
+            y_sb = work.tile([P, JW], F32, name="y_sb", bufs=2, align_bytes=ALIGN)
             nc.scalar.copy(y_sb[:], y[:])
             return y_sb
 
@@ -269,7 +270,7 @@ def tile_list_hopfield_episode_actions_kernel(
             )
 
         def finish(y, gate, blocks, jh, cols):
-            res = work.tile([P, len(blocks) * (cols.stop - cols.start)], F32, name="res", bufs=11)
+            res = work.tile([P, len(blocks) * (cols.stop - cols.start)], F32, name="res", bufs=11, align_bytes=ALIGN)
             nc.vector.tensor_tensor(res[:], y, gate, ALU.mult)
             store(res, blocks, jh, cols)
 

@@ -38,9 +38,9 @@ AT_ACT_SCALES = 10 * KIB
 AT_GATE_HIGH = 12 * KIB
 AT_LISTED = 39 * KIB
 AT_LAST_TABLE = AT_LISTED + 3 * KIB // 2 - 4 * T
-AT_STATE_WORDS = AT_LISTED + 7 * KIB // 4
 AT_PIECES = 48 * KIB
 AT_GATE_ROUNDED = 64 * KIB
+AT_SECOND_GATE = 66 * KIB
 
 
 def tile_list_hopfield_episode_actions_kernel(
@@ -104,6 +104,11 @@ def tile_list_hopfield_episode_actions_kernel(
         nc.vector.tensor_copy(
             listed[:, 0:S].rearrange("p (g t m) -> p g m t", g=2, t=PACK), tab_s[:].bitcast(U8).indirect(idx[:])
         )
+        v_w = [kept(f"v_w{a}", [P, S], U32) for a in range(2)]
+        nc.vector.tensor_copy(
+            v_w[0][:].rearrange("p (g t m) -> p g m t", g=2, t=PACK),
+            tab_w[0][:].bitcast(U32).indirect(idx[:]),
+        )
         nc.vector.tensor_copy(listed[:, S:], tab2_s[:].bitcast(U8).indirect(idx2[:]))
         for a in range(2):
             nc.vector.tensor_copy(planes[a][:].bitcast(I32), listed[:].bitcast(I32))
@@ -119,13 +124,8 @@ def tile_list_hopfield_episode_actions_kernel(
         tab_w.append(placed("tab_w1", [P, T], I32, AT_LAST_TABLE))
         load_words(tab_w[1], tab_words, 1)
         move_rows(1)
-        v_w = [placed("v_w0", [P, S], U32, AT_STATE_WORDS), kept("v_w1", [P, S], U32)]
         v2_w = [[kept(f"v2_w{a}{jh}", [P, JW], U32) for jh in range(2)] for a in range(2)]
 
-        nc.vector.tensor_copy(
-            v_w[0][:].rearrange("p (g t m) -> p g m t", g=2, t=PACK),
-            tab_w[0][:].bitcast(U32).indirect(idx[:]),
-        )
         for a in range(2):
             for jh in range(2):
                 probes = idx2[:, jh * JW // LIST_ROWS : (jh + 1) * JW // LIST_ROWS]
@@ -253,8 +253,11 @@ def tile_list_hopfield_episode_actions_kernel(
         def action_sum(b, blocks, jh, cols):
             return project(b, action_weights, blocks, jh, cols)
 
-        def opened(c, cols=WHOLE):
-            gate = work.tile([P, cols.stop - cols.start], F32, name="gate", bufs=10, align_bytes=ALIGN)
+        def opened(c, cols=WHOLE, offset=None):
+            if offset is None:
+                gate = work.tile([P, cols.stop - cols.start], F32, name="gate", bufs=9, align_bytes=ALIGN)
+            else:
+                gate = placed("gate_placed", [P, cols.stop - cols.start], F32, offset)
             nc.scalar.activation(gate[:], c[:, cols], ACT.Sigmoid)
             return gate
 
@@ -304,7 +307,7 @@ def tile_list_hopfield_episode_actions_kernel(
         quantize(weighed[0], 0, 0, FIRST)
         quantize(weighed[1], 0, 0, SECOND)
         quantize_gate(rounded, 0, 1)
-        rounded = round_gate_on_gpsimd(1, 0, AT_GATE_ROUNDED)
+        rounded = round_gate_on_gpsimd(1, 0, piece_at(1))
 
         th01 = separate(similarity(0, 1, (1, 2, 3, 4)), 0, 1, whole=PACK)
 
@@ -324,9 +327,9 @@ def tile_list_hopfield_episode_actions_kernel(
         quantize(weighed[0], 0, 1, FIRST)
         quantize(weighed[1], 1, 1, FIRST)
         gate0 = opened(c0)
-        finish_on_gpsimd(staged(y0), gate0, 0, piece_at(5))
+        finish_on_gpsimd(staged(y0), gate0, 0, piece_at(4))
         c2, c3 = gate_sum(1, [2], 0, WHOLE), gate_sum(2, [3], 0, WHOLE)
-        gate1 = opened(c1)
+        gate1 = opened(c1, offset=AT_SECOND_GATE)
         y2_sb = staged(y2)
         gate2 = opened(c2)
         gate3 = opened(c3)
@@ -338,7 +341,7 @@ def tile_list_hopfield_episode_actions_kernel(
         hb = weigh(6, th01, 0, 1)
         finish(y1[:], gate1[:], [1], 0, WHOLE)
         quantize(hb, 0, 1, SECOND)
-        finish_on_gpsimd(y2_sb, gate2, 2, piece_at(6))
+        finish_on_gpsimd(y2_sb, gate2, 2, AT_SECOND_GATE)
         finish(y3[:, FIRST], gate3[:, FIRST], [3], 0, FIRST)
         hb = weigh(7, th11, 1, 1)
         finish(y3[:, SECOND], gate3[:, SECOND], [3], 0, SECOND)

@@ -237,13 +237,14 @@ def tile_list_hopfield_episode_actions_kernel(
         def project(b, weights, blocks, jh, cols):
             acc = bank(b)
             width = cols.stop - cols.start
-            passes = [(g, e) for g in range(2) for e in range(len(blocks))]
-            for g, e in passes:
+            passes = [(g, e, at) for g in range(2) for e in range(len(blocks)) for at in range(0, width, HALF)]
+            for g, e, at in passes:
                 words, scales = weights(blocks[e], g)
+                part = slice(cols.start + at, cols.start + at + HALF)
                 nc.tensor.matmul_mx(
-                    out=acc[:, e * width : (e + 1) * width], lhsT=words, lhsT_scale=scales,
-                    rhs=h_w[g][jh][:, cols].bitcast(FP8X4), rhs_scale=h_s[g][jh][:, cols],
-                    start=((g, e) == passes[0]), stop=((g, e) == passes[-1]),
+                    out=acc[:, e * width + at : e * width + at + HALF], lhsT=words, lhsT_scale=scales,
+                    rhs=h_w[g][jh][:, part].bitcast(FP8X4), rhs_scale=h_s[g][jh][:, part],
+                    start=((g, e, at) == passes[0]), stop=((g, e, at) == passes[-1]),
                 )
             return acc
 

from contextlib import ExitStack

import concourse.mybir as mybir
from concourse.masks import make_identity

K, T, S, T2, S2, N = 1024, 2048, 1024, 4096, 1024, 512
FLOPS = 2 * K * S * S2 + 2 * 2 * S * N * S2

F32 = mybir.dt.float32
BF16 = mybir.dt.bfloat16
I32 = mybir.dt.int32
U32 = mybir.dt.uint32
U16 = mybir.dt.uint16
U8 = mybir.dt.uint8
FP8X4 = mybir.dt.float8_e4m3fn_x4
FP4X4 = mybir.dt.float4_e2m1fn_x4
ACT = mybir.ActivationFunctionType
ALU = mybir.AluOpType

P = 128
PACK = 4
KP = P * PACK
JW = 512
HALF = JW // 2
PIECE = HALF * PACK
LIST_ROWS = 16
PLANE = (0, 4)
WALK = 4
KIB = 1024
ALIGN = 256
FIRST, SECOND = slice(0, HALF), slice(HALF, JW)
WHOLE = slice(0, JW)

AT_PROBE_TABLE = 0
AT_GATE_LOW = (0, 4 * KIB)
AT_ACT_WORDS = 8 * KIB
AT_ACT_SCALES = 10 * KIB
AT_GATE_HIGH = 12 * KIB
AT_LISTED = 39 * KIB
AT_LAST_TABLE = AT_LISTED + 3 * KIB // 2 - 4 * T
AT_PIECES = 48 * KIB
AT_GATE_ROUNDED = 64 * KIB
AT_SECOND_GATE = 66 * KIB


def tile_list_hopfield_episode_actions_kernel(
    tc, tab_words, tab_scales, offs, tab2_words, tab2_scales, offs2,
    sharp, trust, wact_words, wact_scales, wgate, out,
):
    nc = tc.nc
    with ExitStack() as ctx:
        keep = ctx.enter_context(tc.tile_pool(name="keep", bufs=1))
        work = ctx.enter_context(tc.tile_pool(name="work", bufs=1))
        psum = ctx.enter_context(tc.psum_pool(name="psum", bufs=1))
        reuse = ctx.enter_context(tc.tile_pool(name="reuse", bufs=1))

        def placed(name, shape, dtype, offset):
            return reuse.tile(shape, dtype, name=name, offset=offset, align_bytes=ALIGN)

        def kept(name, shape, dtype):
            return keep.tile(shape, dtype, name=name, align_bytes=ALIGN)

        idx = keep.tile([P, S // LIST_ROWS], U16, name="idx")
        idx2 = keep.tile([P, S2 // LIST_ROWS], U16, name="idx2")
        tab_w = [kept("tab_w0", [P, T], I32)]
        tab2_w = [placed("tab2_w0", [P, T2], I32, AT_PROBE_TABLE), kept("tab2_w1", [P, T2], I32)]
        tab_s = kept("tab_s", [P, T // 4], I32)
        tab2_s = kept("tab2_s", [P, T2 // 4], I32)
        rows = kept("rows", [P, KP], F32)
        ident = kept("ident", [P, P], F32)

        nc.gpsimd.memset(tab_s[:], 0)
        nc.gpsimd.memset(rows[:], 0.0)
        make_identity(nc, ident[:])
        nc.vector.memset(tab2_s[:], 0)
        warm = keep.tile([P, 8], F32, name="warm")
        nc.scalar.activation(warm[:], ident[:, 0:8], ACT.Sigmoid)

        def load_words(dst, words, a, cols=slice(None)):
            nc.sync.dma_start(dst[:, cols], words[a].rearrange("p t i -> p (t i)").bitcast(I32)[:, cols])

        def load_scales(dst, scales):
            nc.sync.dma_start(dst[0:P:4, :], scales.bitcast(I32).rearrange("a q n -> q a n"))

        load_words(tab_w[0], tab_words, 0, slice(0, T // 4))
        nc.sync.dma_start(idx[:], offs)
        nc.sync.dma_start(idx2[:], offs2)
        load_scales(tab_s, tab_scales)
        load_words(tab_w[0], tab_words, 0, slice(T // 4, T))
        load_scales(tab2_s, tab2_scales)
        load_words(tab2_w[0], tab2_words, 0)
        nc.sync.dma_start(rows[0:2, :], trust.rearrange("(g m) -> g m", g=2))
        nc.sync.dma_start(rows[2:4, :], sharp.rearrange("(g m) -> g m", g=2))
        load_words(tab2_w[1], tab2_words, 1)

        turned = psum.tile([P, KP], F32, name="turned")
        for t in range(PACK):
            nc.tensor.transpose(turned[:, t * P : (t + 1) * P], rows[:, t:KP:PACK], ident[:])
        sharp_sb = kept("sharp_sb", [P, 2, PACK], F32)
        nc.scalar.copy(sharp_sb[:], turned[:].rearrange("p (t r) -> p r t", t=PACK)[:, 2:4, :])

        listed = placed("listed", [P, S + S2], U8, AT_LISTED)
        planes = [kept(f"planes{a}", [P, S + S2], U8) for a in range(2)]
        nc.vector.tensor_copy(
            listed[:, 0:S].rearrange("p (g t m) -> p g m t", g=2, t=PACK), tab_s[:].bitcast(U8).indirect(idx[:])
        )
        v_w = [kept(f"v_w{a}", [P, S], U32) for a in range(2)]
        nc.vector.tensor_copy(
            v_w[0][:].rearrange("p (g t m) -> p g m t", g=2, t=PACK),
            tab_w[0][:].bitcast(U32).indirect(idx[:]),
        )
        nc.vector.tensor_copy(listed[:, S:], tab2_s[:].bitcast(U8).indirect(idx2[:]))
        for a in range(2):
            nc.vector.tensor_copy(planes[a][:].bitcast(I32), listed[:].bitcast(I32))

        def move_rows(a):
            for r in range(1, 4):
                nc.sync.dma_start(
                    planes[a][PLANE[a] + r : P : 32, :].bitcast(I32),
                    planes[a][PLANE[a] + 8 * r : P : 32, :].bitcast(I32),
                )

        move_rows(0)
        tab_w.append(placed("tab_w1", [P, T], I32, AT_LAST_TABLE))
        load_words(tab_w[1], tab_words, 1)
        move_rows(1)
        v2_w = [[kept(f"v2_w{a}{jh}", [P, JW], U32) for jh in range(2)] for a in range(2)]

        for a in range(2):
            for jh in range(2):
                probes = idx2[:, jh * JW // LIST_ROWS : (jh + 1) * JW // LIST_ROWS]
                nc.vector.tensor_copy(v2_w[a][jh][:], tab2_w[a][:].bitcast(U32).indirect(probes))
        for g in range(2):
            nc.vector.tensor_copy(
                v_w[1][:, g * KP : (g + 1) * KP].rearrange("p (t m) -> p m t", t=PACK),
                tab_w[1][:].bitcast(U32).indirect(idx[:, g * KP // LIST_ROWS : (g + 1) * KP // LIST_ROWS]),
            )

        gate_low = [placed(f"gate_low{g}", [P, PACK, HALF], F32, AT_GATE_LOW[g]) for g in range(2)]
        gate_high = placed("gate_high", [P, 2, PACK, HALF], F32, AT_GATE_HIGH)
        gate_raw = [[gate_low[g][:] for g in range(2)], [gate_high[:, g, :, :] for g in range(2)]]
        wact_w = placed("wact_w", [P, 2, 2 * N // 4], I32, AT_ACT_WORDS)
        wact_s = placed("wact_s", [P, 2, N // 4], I32, AT_ACT_SCALES)
        nc.gpsimd.memset(wact_s[:], 0)

        def load_gate(nh, g):
            src = wgate[g * KP : (g + 1) * KP, nh * HALF : (nh + 1) * HALF]
            nc.sync.dma_start(gate_raw[nh][g], src.rearrange("(p t) n -> p t n", t=PACK))

        load_gate(0, 0)
        load_gate(0, 1)
        load_gate(1, 0)
        nc.sync.dma_start(wact_w[:], wact_words.bitcast(I32).rearrange("g p e -> p g e"))
        for r in range(4):
            src = wact_scales.bitcast(I32).rearrange("g (q r) e -> r q g e", r=4)[r]
            nc.sync.dma_start(wact_s[r:P:32, :, :], src)
        load_gate(1, 1)

        h_w = [[kept(f"h_w{g}{jh}", [P, JW], U32) for jh in range(2)] for g in range(2)]
        h_s = [[kept(f"h_s{g}{jh}", [P, JW], U8) for jh in range(2)] for g in range(2)]
        wg_w = [kept(f"wg_w{nh}", [P, N], U32) for nh in range(2)]
        wg_s = [kept(f"wg_s{nh}", [P, N], U8) for nh in range(2)]

        def bank(b):
            return psum.tile([P, JW], F32, name=f"bank{b}")

        def similarity_pass(acc, a, g, t, jh):
            cols = slice(g * KP + t * P, g * KP + (t + 1) * P)
            nc.tensor.matmul_mx(
                out=acc[:],
                lhsT=v_w[a][:, cols].bitcast(FP8X4),
                lhsT_scale=planes[a][PLANE[a] :, cols],
                rhs=v2_w[a][jh][:].bitcast(FP8X4),
                rhs_scale=planes[a][PLANE[a] :, S + jh * JW : S + (jh + 1) * JW],
                start=(a == 0),
                stop=(a == 1),
            )

        def similarity(g, jh, banks):
            accs = [bank(b) for b in banks]
            for t in range(PACK):
                for a in range(2):
                    similarity_pass(accs[t], a, g, t, jh)
            return accs

        def separate(accs, g, jh, whole):
            th = kept(f"th{g}{jh}", [P, 2, PACK, HALF], F32)
            for t in range(whole):
                nc.scalar.activation(
                    th[:, :, t, :], accs[t][:].rearrange("p (u c) -> p u c", u=2), ACT.Tanh,
                    scale=sharp_sb[:, g, t : t + 1],
                )
            for u, cols in enumerate((FIRST, SECOND)):
                for t in range(whole, PACK):
                    nc.scalar.activation(th[:, u, t, :], accs[t][:, cols], ACT.Tanh, scale=sharp_sb[:, g, t : t + 1])
            return th

        def walk_out(ap):
            return ap.rearrange("p (c i t) -> p c t i", i=WALK, t=PACK)

        def walk_in(ap):
            return ap.rearrange("p t (c i) -> p c t i", i=WALK)

        def piece_at(number):
            return AT_PIECES + number * 2 * PIECE

        def weigh(number, th, g, u):
            hb = placed(f"hb{number}", [P, PIECE], BF16, piece_at(number))
            factor = turned[:, g:KP:P].unsqueeze(1).unsqueeze(3).to_broadcast([P, HALF // WALK, PACK, WALK])
            nc.vector.tensor_tensor(walk_out(hb[:]), walk_in(th[:, u, :, :]), factor, ALU.mult)
            return hb

        def quantize(hb, g, jh, cols):
            nc.vector.quantize_mx(out=h_w[g][jh][:, cols].bitcast(FP8X4), scales=h_s[g][jh][:, cols], in_=hb[:])

        def round_gate_on_gpsimd(nh, g, offset):
            rounded = placed(f"gate_bf{nh}{g}", [P, PIECE], BF16, offset)
            nc.gpsimd.tensor_scalar(
                rounded[:].rearrange("p (c i t) -> p c t i", i=2, t=PACK),
                gate_raw[nh][g].rearrange("p t (c i) -> p c t i", i=2),
                1.0, 0.0, ALU.mult, ALU.add,
            )
            return rounded

        def quantize_gate(rounded, nh, g):
            cols = slice(g * HALF, (g + 1) * HALF)
            nc.vector.quantize_mx(out=wg_w[nh][:, cols].bitcast(FP8X4), scales=wg_s[nh][:, cols], in_=rounded[:])

        def gate_weights(nb, g):
            cols = slice(g * HALF + nb % 2 * P, g * HALF + (nb % 2 + 1) * P)
            return wg_w[nb // 2][:, cols].bitcast(FP8X4), wg_s[nb // 2][:, cols]

        def action_weights(nb, g):
            words = wact_w[:, g, :].bitcast(U8)[:, 2 * nb * P : 2 * (nb + 1) * P]
            return words.bitcast(FP4X4), wact_s[:, g, :].bitcast(U8)[:, nb * P : (nb + 1) * P]

        def project(b, weights, blocks, jh, cols):
            acc = bank(b)
            width = cols.stop - cols.start
            passes = [(g, e, at) for g in range(2) for e in range(len(blocks)) for at in range(0, width, HALF)]
            for g, e, at in passes:
                words, scales = weights(blocks[e], g)
                part = slice(cols.start + at, cols.start + at + HALF)
                nc.tensor.matmul_mx(
                    out=acc[:, e * width + at : e * width + at + HALF], lhsT=words, lhsT_scale=scales,
                    rhs=h_w[g][jh][:, part].bitcast(FP8X4), rhs_scale=h_s[g][jh][:, part],
                    start=((g, e, at) == passes[0]), stop=((g, e, at) == passes[-1]),
                )
            return acc

        def gate_sum(b, blocks, jh, cols):
            return project(b, gate_weights, blocks, jh, cols)

        def action_sum(b, blocks, jh, cols):
            return project(b, action_weights, blocks, jh, cols)

        def opened(c, cols=WHOLE, offset=None):
            if offset is None:
                gate = work.tile([P, cols.stop - cols.start], F32, name="gate", bufs=9, align_bytes=ALIGN)
            else:
                gate = placed("gate_placed", [P, cols.stop - cols.start], F32, offset)
            nc.scalar.activation(gate[:], c[:, cols], ACT.Sigmoid)
            return gate

        def staged(y):
            y_sb = work.tile([P, JW], F32, name="y_sb", bufs=2, align_bytes=ALIGN)
            nc.scalar.copy(y_sb[:], y[:])
            return y_sb

        def store(res, blocks, jh, cols):
            dst = out[blocks[0] * P : (blocks[-1] + 1) * P, jh * JW + cols.start : jh * JW + cols.stop]
            nc.sync.dma_start(
                dst.rearrange("(e p) c -> p e c", p=P), res[:].rearrange("p (e c) -> p e c", e=len(blocks))
            )

        def finish(y, gate, blocks, jh, cols):
            res = work.tile([P, len(blocks) * (cols.stop - cols.start)], F32, name="res", bufs=11, align_bytes=ALIGN)
            nc.vector.tensor_tensor(res[:], y, gate, ALU.mult)
            store(res, blocks, jh, cols)

        def finish_on_gpsimd(y_sb, gate, nb, offset):
            res = placed(f"res{nb}", [P, JW], F32, offset)
            nc.gpsimd.tensor_tensor(res[:], y_sb[:], gate[:], ALU.mult)
            store(res, [nb], 0, WHOLE)

        early = [(g, t) for g in range(2) for t in range(PACK)][:-1]
        first = [bank(b) for b in range(len(early))]
        for a in range(2):
            for acc, (g, t) in zip(first, early):
                similarity_pass(acc, a, g, t, 0)
        th00 = separate(first[:PACK], 0, 0, whole=0)
        eighth = bank(0)
        for a in range(2):
            similarity_pass(eighth, a, 1, PACK - 1, 0)
        th10 = separate(first[PACK:] + [eighth], 1, 0, whole=PACK)

        rounded = placed("gate_bf00", [P, PIECE], BF16, AT_GATE_ROUNDED)
        for nb in range(2):
            values = rounded[:, nb * PACK * P : (nb + 1) * PACK * P]
            nc.vector.tensor_copy(walk_out(values), walk_in(gate_raw[0][0][:, :, nb * P : (nb + 1) * P]))
        for nb in range(2):
            cols = slice(nb * P, (nb + 1) * P)
            values = rounded[:, nb * PACK * P : (nb + 1) * PACK * P]
            nc.vector.quantize_mx(out=wg_w[0][:, cols].bitcast(FP8X4), scales=wg_s[0][:, cols], in_=values)
        rounded = round_gate_on_gpsimd(0, 1, AT_GATE_ROUNDED)

        weighed = [weigh(u, th00, 0, u) for u in range(2)]
        quantize(weighed[0], 0, 0, FIRST)
        quantize(weighed[1], 0, 0, SECOND)
        quantize_gate(rounded, 0, 1)
        rounded = round_gate_on_gpsimd(1, 0, piece_at(1))

        th01 = separate(similarity(0, 1, (1, 2, 3, 4)), 0, 1, whole=PACK)

        weighed = [weigh(2 + u, th10, 1, u) for u in range(2)]
        quantize(weighed[0], 1, 0, FIRST)
        quantize(weighed[1], 1, 0, SECOND)
        quantize_gate(rounded, 1, 0)
        rounded = round_gate_on_gpsimd(1, 1, piece_at(3))

        th11 = separate(similarity(1, 1, (5, 6, 0, 1)), 1, 1, whole=2)

        c0, y0 = gate_sum(2, [0], 0, WHOLE), action_sum(3, [0], 0, WHOLE)
        c1, y1 = gate_sum(4, [1], 0, WHOLE), action_sum(5, [1], 0, WHOLE)
        y2, y3 = action_sum(6, [2], 0, WHOLE), action_sum(0, [3], 0, WHOLE)
        weighed = [weigh(4, th01, 0, 0), weigh(5, th11, 1, 0)]
        quantize_gate(rounded, 1, 1)
        quantize(weighed[0], 0, 1, FIRST)
        quantize(weighed[1], 1, 1, FIRST)
        gate0 = opened(c0)
        finish_on_gpsimd(staged(y0), gate0, 0, piece_at(4))
        c2, c3 = gate_sum(1, [2], 0, WHOLE), gate_sum(2, [3], 0, WHOLE)
        gate1 = opened(c1, offset=AT_SECOND_GATE)
        y2_sb = staged(y2)
        gate2 = opened(c2)
        gate3 = opened(c3)

        pairs = ([0, 1], [2, 3])
        pair_gates = [opened(gate_sum(b, pair, 1, FIRST)) for b, pair in zip((3, 4), pairs)]
        pair_actions = [action_sum(b, pair, 1, FIRST) for b, pair in zip((6, 1), pairs)]

        hb = weigh(6, th01, 0, 1)
        finish(y1[:], gate1[:], [1], 0, WHOLE)
        quantize(hb, 0, 1, SECOND)
        finish_on_gpsimd(y2_sb, gate2, 2, AT_SECOND_GATE)
        finish(y3[:, FIRST], gate3[:, FIRST], [3], 0, FIRST)
        hb = weigh(7, th11, 1, 1)
        finish(y3[:, SECOND], gate3[:, SECOND], [3], 0, SECOND)
        quantize(hb, 1, 1, SECOND)

        last_gates = [opened(gate_sum(b, [nb], 1, SECOND), FIRST) for b, nb in ((2, 0), (5, 1))]
        low_actions = action_sum(3, pairs[0], 1, SECOND)
        high_gates = gate_sum(4, pairs[1], 1, SECOND)
        last_gates = last_gates + [opened(high_gates, cols) for cols in (FIRST, SECOND)]
        last_actions = [low_actions, action_sum(0, pairs[1], 1, SECOND)]
        for nb, cols in enumerate((FIRST, SECOND)):
            finish(pair_actions[0][:, cols], pair_gates[0][:, cols], [nb], 1, FIRST)
        finish(pair_actions[1][:], pair_gates[1][:], pairs[1], 1, FIRST)
        for nb in range(3):
            finish(last_actions[nb // 2][:, (FIRST, SECOND)[nb % 2]], last_gates[nb][:], [nb], 1, SECOND)
        for at in (0, P):
            cols = slice(HALF + at, HALF + at + P)
            finish(last_actions[1][:, cols], last_gates[3][:, at : at + P], [3], 1, cols)
